import numpy as np, ml_dtypes
CORES = [36,164,52,180,100,228,116,244]
N = 8
import mx_ref
BF = ml_dtypes.bfloat16
def gentries(a):
    return np.ascontiguousarray(a.reshape(8, 16, -1).transpose(0, 2, 1)).reshape(8, -1)
def gtable(e):
    e = np.asarray(e); return np.ascontiguousarray(e.reshape(8, -1, 16).transpose(0, 2, 1)).reshape(128, -1).astype(np.int32)
def gcols(t, e):
    v = np.concatenate([t.reshape(8, 16, -1, 4), np.zeros((8, 16, 1, 4), BF)], axis=2)
    return np.ascontiguousarray(np.stack([v[g][:, e[g]] for g in range(8)])).reshape(128, -1)
def tile(rs):
    return np.stack(rs, axis=2).reshape(128, -1).astype(BF)
def pick(q, e):
    c = np.concatenate([q[0].reshape(128, -1, 4), np.zeros((128, 1, 4), np.uint8)], axis=1); s = np.concatenate([q[1], np.ones((16, 1), np.uint8)], axis=1)
    return (np.ascontiguousarray(c[:, e].reshape(128, -1)), np.ascontiguousarray(s[:, e]))
def join(*qs):
    return (np.concatenate([q[0] for q in qs], axis=1), np.concatenate([q[1] for q in qs], axis=1))
def put(q, e, v):
    c, s = q[0].reshape(128, -1, 4).copy(), q[1].copy(); c[:, e] = v[0].reshape(128, -1, 4); s[:, e] = v[1]
    return (c.reshape(128, -1), s)
def pk(c, s):
    return (np.ascontiguousarray(c), mx_ref.live(s))
def emit(q):
    return q[0], q[1]
def packed(v, rng):
    q = [mx_ref.quantize(np.ascontiguousarray(v[r])) for r in range(N)]
    return np.stack([a for a, b in q]), np.stack([mx_ref.plane(b, rng) for a, b in q])
def values_of_codes():
    e, c = np.zeros((128, 128, 4), np.float32), np.zeros((128, 2, 4), np.uint8)
    e[np.arange(128), np.arange(128), 0] = 1
    c[:127, :, 0] = np.arange(256).reshape(2, 128).T[:127]
    return mx_ref.matmul(mx_ref.quantize(e.reshape(128, 512).astype(BF)), (c.reshape(128, 8), np.full((16, 2), 127, np.uint8))).T.reshape(-1).astype(np.float64)
CODE_VALUE, SCALE_VALUE = values_of_codes(), 2.0 ** (np.arange(256) - 127.0)
def decode(q):
    return (CODE_VALUE[q[0]].reshape(16, 8, -1, 4) * SCALE_VALUE[q[1]][:, None, :, None] + 0.0).reshape(128, -1).astype(np.float32)
def f(rng, *shape):
    return mx_ref.flush((rng.standard_normal(shape, dtype=np.float32) * np.exp2(rng.integers(-2, 3, shape[:-1] + (1,)))).astype(BF))
def wide(rng, *shape, cols=0):
    v = rng.standard_normal(shape, dtype=np.float32) * np.exp2(rng.integers(-12, 13, shape)).astype(np.float32)
    if cols: v *= np.repeat(np.exp2(rng.integers(-cols, cols + 1, shape[:-2] + (1, shape[-1] // 4))) * (rng.random(shape[:-2] + (1, shape[-1] // 4)) > 0.0625), 4, axis=-1).astype(np.float32)
    return mx_ref.flush(v.astype(BF))
C, K, R = 224, 48, 3
def rings(o):
    e = np.zeros((N, 8, C), int)
    np.put_along_axis(e, o, np.roll(o, -1, axis=2), axis=2)
    return np.stack([gtable(e[r]) for r in range(N)])
def orders(rng):
    return np.argsort(rng.random((N, 8, C)), axis=2)
def numbers_of(rng):
    return {"x": np.array(f(rng, N, 128, 4 * C)), "u": np.array(f(rng, N, 128, 512)), "v": np.array(f(rng, N, 128, 512))}
def layers(rng):
    return np.array(f(rng, N, 128, 2048)).reshape(N, 8, 16, 4, 8, 16, 4)
def carry(source, size):
    w = np.zeros((N, 128, 4, 128, 4), np.float32)
    i = np.arange(128)
    for b in range(4): w[:, i - i % 16 + np.array(source)[i % 16], b, i, b] = 32 * np.resize(size, 128)
    return w.astype(BF)
def weights(rng, w):
    c, p = packed(np.ascontiguousarray(w).reshape(N, 128, 2048), rng)
    return {"wc": c, "ws": p}
def signs(rng):
    return np.stack([rng.permutation(8) % 2 * 2.0 - 1.0 for r in range(N)])
def setup_inputs(rng):
    return {**numbers_of(rng), **weights(rng, layers(rng)), "nx": rings(orders(rng))}
def setup_inputs_ties(rng):
    d = numbers_of(rng)
    x = d["x"].astype(np.float32).reshape(N, 8, 16, C, 4)
    e = (rng.integers(N) + np.arange(N)) % N
    w = layers(rng)
    o = orders(rng)
    for i in range(N):
        r = e[i]
        k = np.stack([rng.permutation(C) % 3 - 1 for g in range(8)])
        if i < 2: k[:] = i
        x[r][:, :8] = np.abs(x[r][:, :8, :1]) * k[:, None, :, None]
        if i >= 3 and i % 2 == 1: w[r][:, :, :, :, :8] = 0
        g = rng.permutation(8)
        o[r, g[0]] = np.arange(C)
        o[r, g[1]] = np.arange(C)[::-1]
    u = d["u"].astype(np.float32).reshape(N, 8, 16, 8, 16, 4)
    k = np.abs(u)
    u[:, :, :, :, 0] = 0
    for g in range(8): u[:, g, :8, g, 0] = k[:, g, :8, g, 0]
    return {"x": x.reshape(N, 128, 4 * C).astype(BF), "u": u.reshape(N, 128, 512).astype(BF), "v": d["v"], **weights(rng, w), "nx": rings(o)}
def setup_inputs_near(rng):
    d = numbers_of(rng)
    x = d["x"].astype(np.float32).reshape(N, 8, 16, C, 4)
    x[:, :, :2] = 0
    u = d["u"].reshape(N, 128, 128, 4)
    u[:, :, ::16] = 0
    e = rng.permutation(8)
    for g in range(8):
        if e[g] < 4:
            s, size, k = rng.integers(-2, 3, (N, 2, C)), 2.0 ** -30, 2.0 ** -30
        else:
            s, size, k = rng.integers(0, 16, (N, 2, C)), 2.0 ** -23, 1.0
            x[:, g, 0, :, 0] = rng.choice([-1.0, 1.0], (N, C))
            x[:, g, 1, :, 0] = e[g] % 2 * 2.0 - 1.0
        x[:, g, 8:10] = ((np.abs(s)[..., None] >> np.arange(4)) & 1) * np.sign(s)[..., None] * np.exp2(np.arange(4.0)) * size
        x[:, g, 10:] = rng.integers(4, 8, (N, 6, C, 4)) * 2 * size
        u[:, 16 * g, 16 * g, 0] = k
        u[:, 16 * g + 8, 16 * g] = k
    times = np.resize(np.array([1.0, 1.0] + [0.75] * 6 + [1.0, 1.0] + [0.75] * 6), (8, 16))
    times[e < 4, 8:10] = 2.0 ** -7
    w = carry([1, 1, 2, 3, 4, 5, 6, 7, 9, 8, 10, 11, 12, 13, 14, 15], times)
    return {"x": x.reshape(N, 128, 4 * C).astype(BF), "u": u.reshape(N, 128, 512), "v": d["v"], **weights(rng, w), "nx": rings(orders(rng))}
def setup_inputs_huge(rng):
    d = numbers_of(rng)
    x = 2.0 ** 30 * (0.8 + 0.2 * rng.random((N, 8, 16, C, 4)))
    for r in range(N): x[r, :, :8] *= (rng.permutation(C) % 2 * 2.0 - 1.0)[:, None]
    u = d["u"].reshape(N, 8, 16, 8, 16, 4)
    u[:, :, :, :, 0] = 0
    a = 2.0 ** 30 * (0.8 + 0.2 * rng.random((N, 8, 8, 8, 4))) * signs(rng)[:, None, None, :, None]
    u[:, :, :8, :, 0] = a.astype(np.float32).astype(BF)
    w = carry([8, 9, 10, 11, 12, 13, 14, 15, 0, 1, 2, 3, 4, 5, 6, 7], [0.875] * 16)
    o = np.zeros((N, 8, C), int) + rng.permutation(C)
    return {"x": x.astype(np.float32).reshape(N, 128, 4 * C).astype(BF), "u": u.reshape(N, 128, 512), "v": d["v"], **weights(rng, w), "nx": rings(o)}
def setup_inputs_slots(rng):
    d = numbers_of(rng)
    n = [0, 1, C // 2, K + 1, K, K - 1, K, K + 1]
    e = rng.permutation(8)
    o = orders(rng)
    x = d["x"].astype(np.float32).reshape(N, 8, 16, C, 4)
    for r in range(N):
        for g in range(8):
            turns = np.sort(rng.permutation(C)[:2 * n[(e[g] + r) % 8]])
            s = (np.searchsorted(turns, np.arange(C), side="right") + rng.integers(2)) % 2
            x[r, g, 0][o[r, g], 0] = 2.0 * s - 1.0
    u = d["u"].reshape(N, 128, 128, 4)
    u[:, :, ::16] = 0
    for h in range(0, 128, 16): u[:, h, h, 0] = 1
    return {"x": x.reshape(N, 128, 4 * C).astype(BF), "u": u.reshape(N, 128, 512), "v": d["v"], **weights(rng, layers(rng)), "nx": rings(o)}
def setup_inputs_spread(rng):
    d = setup_inputs(rng)
    d["x"] = wide(rng, N, 128, 4 * C, cols=6)
    return d
def check_inputs(d):
    b = []
    for k in ("x", "u", "v"):
        a = np.abs(d[k].astype(np.float32))
        if not (np.isfinite(a).all() and ((a == 0) | (a >= 2.0 ** -30) & (a <= 2.0 ** 30)).all()): b.append("a value of " + k)
    if ((d["wc"] & 0x7F) == 0x7F).any(): b.append("a code of wc that is no number")
    z = np.zeros((128, 4, 4), np.float32)
    z[:, 1] = 2.0 ** -30
    z[:, 2] = 2.0 ** 30
    c, s = emit(mx_ref.quantize(z.reshape(128, 16).astype(BF)))
    for r in range(N):
        p = mx_ref.live(d["ws"][r])
        if not ((p == s[0, 0]) | (p >= s[0, 1]) & (p <= s[0, 2])).all(): b.append("a scale of ws")
        e = gentries(d["nx"][r])
        good = bool(((e >= 0) & (e < C)).all())
        j = np.zeros(8, int)
        for i in range(C):
            if good:
                j = e[np.arange(8), j]
                good = bool(((j == 0) == (i == C - 1)).all())
        if not good: b.append("a ring of nx")
    return b
def reference(x, u, v, wc, ws, nx):
    qu = [mx_ref.quantize(u[r]) for r in range(N)]
    lay = [pk(wc[r], ws[r]) for r in range(N)]
    after = [gentries(nx[r]) for r in range(N)]
    before = [np.argsort(after[r], axis=1) for r in range(N)]
    now = [x[r] for r in range(N)]
    for t in range(R):
        forward, parts, sent, count = [], [], [], []
        for r in range(N):
            q = mx_ref.quantize(now[r])
            a = mx_ref.matmul(qu[r], q)[::16] > 0
            p = decode(q).astype(BF)
            e, n = np.full((8, 2 * K), -1), np.zeros(8, int)
            for g in range(8):
                j = np.flatnonzero(a[g] & ~a[g][after[r][g]])[:K]
                n[g] = len(j)
                e[g, 0:2 * len(j):2] = j
                e[g, 1:2 * len(j):2] = after[r][g][j]
            forward.append(a)
            parts.append(p)
            sent.append(mx_ref.quantize(gcols(p, e)))
            count.append(n)
        made, lists = [], []
        for r in range(N):
            z, n = sent[r - 1], count[r - 1]
            h = tile([mx_ref.matmul(pick(lay[r], np.arange(128 * b, 128 * b + 128)), z) * np.float32(0.03125) for b in range(4)])
            p = mx_ref.matmul(qu[r], mx_ref.quantize(h))[::16]
            swap = (p[:, 1::2] > p[:, 0::2]).astype(int)
            e = np.where(forward[r], before[r], after[r])
            for g in range(8):
                a, o = forward[r][g], after[r][g]
                j = np.flatnonzero(~a & a[o])
                e[g, j] = j
                e[g, o[j]] = o[j]
                j = j[:n[g]]
                k = np.arange(len(j))
                e[g, j] = C + 2 * k + swap[g, k]
                e[g, o[j]] = C + 2 * k + 1 - swap[g, k]
            made.append(gcols(np.concatenate([parts[r], h], axis=1), e))
            lists.append(e)
        now = made
    y, ot = np.zeros((N, 128, C), np.float32), np.zeros((N, 8, C), np.float32)
    oc, osc = np.zeros((N, 128, 4 * C), np.uint8), np.zeros((N, 16, C), np.uint8)
    for r in range(N):
        q = mx_ref.quantize(now[r])
        y[r] = mx_ref.matmul(mx_ref.quantize(v[r]), q)
        ot[r] = lists[r]
        oc[r], osc[r] = emit(q)
    return {"y": y, "ot": ot, "oc": oc, "osc": osc}

@@ -1,0 +1,290 @@
+from concourse.mybir import dt, AluOpType as Op, ActivationFunctionType as Act
+
+C, K, R = 224, 48, 3
+PL = 448
+BIG = 65536.0
+CODE, PLANE = "float8_e4m3fn_x4", "uint8"
+
+
+def _sb(n, d):
+    return ("sbuf", [128, n], d)
+
+
+SCRATCH = {
+    "x0": _sb(896, "bfloat16"), "ut": _sb(512, "bfloat16"), "vt": _sb(512, "bfloat16"), "nxi": _sb(16, "int32"),
+    "qu": _sb(128, CODE), "su": _sb(128, PLANE), "qur": _sb(128, CODE), "sur": _sb(128, PLANE),
+    "qv": _sb(128, CODE), "sv": _sb(128, PLANE), "qw": _sb(512, CODE), "sw": _sb(512, PLANE),
+    "ez": _sb(528, "bfloat16"), "qe": _sb(512, CODE), "se": _sb(512, PLANE),
+    "qx": _sb(512, CODE), "sx": _sb(512, PLANE), "xt": _sb(896, "bfloat16"), "tw": _sb(4 * PL, "bfloat16"),
+    "at": _sb(512, "bfloat16"), "qa": _sb(384, CODE), "sa": _sb(384, PLANE),
+    "ht": _sb(512, "bfloat16"), "qh": _sb(128, CODE), "sh": _sb(128, PLANE),
+    "fb": _sb(C, "bfloat16"), "f2": _sb(C, "bfloat16"), "mb": _sb(C, "bfloat16"), "cb": _sb(R * C, "bfloat16"),
+    "ub": _sb(3 * C, "bfloat16"),
+    "cn": _sb(336, "bfloat16"), "la": _sb(4, "uint16"), "nb": _sb(K, "bfloat16"), "nw": _sb(K, "bfloat16"),
+    "lb": _sb(4, "uint16"), "nin": _sb(8 * R, "bfloat16"), "thr": _sb(1, "float32"),
+    "hb": _sb(240, "bfloat16"), "zb": _sb(240, "bfloat16"), "zp": _sb(C, "bfloat16"), "wr": _sb(3 * C, "bfloat16"),
+    "zi": _sb(42, "int32"), "od": _sb(28, "int32"), "tq": _sb(28, "float32"), "qq": _sb(14, "float32"),
+    "kk": _sb(14, "float32"), "zf": _sb(14, "float32"), "y1": _sb(14, "float32"), "y2": _sb(14, "float32"),
+    "pn": _sb(14, "float32"), "x1": _sb(14, "float32"), "l1": _sb(14, "float32"), "l16": _sb(14, "uint16"),
+    "gw": _sb(864, "bfloat16"), "fw": _sb(864, "bfloat16"), "h0": _sb(C, "bfloat16"), "hv": _sb(C, "bfloat16"),
+    "hw": _sb(C, "bfloat16"), "lx": _sb(14, "uint16"), "pa": _sb(K, "float32"),
+    "rt": _sb(PL, "float32"), "kt": _sb(C, "bfloat16"), "k16": _sb(16, "bfloat16"), "k1": _sb(16, "float32"),
+    "k2": _sb(16, "float32"), "pi": _sb(14, "int32"), "c16": _sb(14, "int32"), "pmi": _sb(14, "int32"),
+    "pcol": _sb(1, "float32"), "ul": _sb(8, "uint16"), "pm16": _sb(14, "uint16"), "jw": _sb(14, "float32"),
+    "jm": _sb(14, "float32"), "sc": _sb(1, "float32"), "nx16": _sb(14, "uint16"), "pv16": _sb(14, "uint16"),
+    "ys": _sb(C, "float32"), "ots": _sb(C, "float32"),
+    "ps": ("psum", [128, 512], "float32"), "pd": ("psum", [128, 2048], "float32"), "pp": ("psum", [128, 512], "float32"),
+}
+DMAS = ["du", "dn", "dx", "dwc", "dws", "dv", "doc", "ds0", "ds1", "ds2", "ds3", "dy", "dot"]
+SEMAPHORES = ["cv", "cs", "ct", "cg", "sent"] + DMAS + ["arr%d" % t for t in range(R)] + ["cnt%d" % t for t in range(R)]
+
+
+def _emit(g, T, ops, sent):
+    eng = {"v": g.vector, "s": g.scalar, "t": g.tensor, "g": g, "y": g.sync}
+    own = {"v": "cv", "s": "cs", "t": "ct", "g": "cg"}
+    count = {}
+    known = {q: {} for q in eng}
+    writer, readers, mark = {}, {}, []
+    for i, (q, fn, reads, writes, kind) in enumerate(ops):
+        deps = set()
+        for k in reads:
+            if k in writer:
+                deps.add(writer[k])
+            if k.startswith("p:"):
+                deps.update(j for j in readers.get(k, []) if ops[j][0] != q)
+        for k in writes:
+            if k in writer:
+                deps.add(writer[k])
+            deps.update(readers.get(k, []))
+        for k in reads:
+            readers.setdefault(k, []).append(i)
+        for k in writes:
+            writer[k] = i
+            readers[k] = []
+        if q is None:
+            mark.append((kind[0], kind[1], {}))
+            count[kind[0]] = kind[1]
+            continue
+        for j in sorted(deps, reverse=True):
+            sem, n, seen = mark[j]
+            if sem is None or known[q].get(sem, 0) >= n:
+                continue
+            eng[q].wait_ge(T.sem[sem], n)
+            known[q][sem] = n
+            for s, m in seen.items():
+                known[q][s] = max(known[q].get(s, 0), m)
+        ins = fn()
+        if kind == "remote":
+            mark.append((None, 0, {}))
+            continue
+        sem, step = (own[q], 1) if kind is None else (kind, 16)
+        count[sem] = count.get(sem, 0) + step
+        ins.then_inc(T.sem[sem], step)
+        mark.append((sem, count[sem], dict(known[q])))
+    count["sent"] = sent
+    for sem in SEMAPHORES:
+        if count.get(sem, 0) > known["g"].get(sem, 0):
+            g.wait_ge(T.sem[sem], count[sem])
+
+
+def rank_program(g, core, T, topo):
+    rank = T.rank_of(core)
+    if rank is None:
+        return
+    nxt = T.cores[(rank + 1) % len(T.cores)]
+    prv = T.cores[rank - 1]
+    rid, pid = topo.addr(nxt, core)
+    mask = topo.mask(core, nxt)
+    ne_out, ne_in = len(topo.engines(core, nxt)), len(topo.engines(prv, core))
+    V, S, PE = g.vector, g.scalar, g.tensor
+    ops = []
+    sent = [0]
+
+    def op(q, fn, reads, writes, kind=None):
+        ops.append((q, fn, reads, writes, kind))
+
+    def ts(out, in0, a, b, o0, o1, reads, writes):
+        if o1 is None:
+            op("v", lambda: V.tensor_scalar(out, in0, a, None, o0), reads, writes)
+        else:
+            op("v", lambda: V.tensor_scalar(out, in0, a, b, o0, o1), reads, writes)
+
+    def tt(out, in0, in1, o, reads, writes):
+        op("v", lambda: V.tensor_tensor(out, in0, in1, o), reads, writes)
+
+    def cp(q, out, in_, reads, writes):
+        if q == "v":
+            op("v", lambda: V.tensor_copy(out, in_), reads, writes)
+        else:
+            op("s", lambda: S.activation(out, in_, Act.Copy), reads, writes)
+
+    def scan(out, d0, d1, init, o0, o1, reads, writes):
+        op("v", lambda: V.tensor_tensor_scan(out, d0, d1, init, o0, o1), reads, writes)
+
+    def wrap(out, in_, n, reads, writes):
+        scan(out, T.kt[:, 0:n], in_, 0.0, Op.mult, Op.max, reads + ["kt"], writes)
+
+    def quant(q, s, in_, reads, writes):
+        op("v", lambda: V.quantize_mx(q, s, in_), reads, writes)
+
+    def mm(out, a, sa, b, sb, reads, writes):
+        op("t", lambda: PE.matmul_mx(out, a, sa, b, sb, True, True), reads, writes)
+
+    def fill(ap, val, writes):
+        op("v", lambda: V.memset(ap, val), [], writes)
+
+    def iota(out, pattern, base, mult, writes, small=False):
+        if small:
+            op("g", lambda: g.iota(out, pattern, base, mult, allow_small_or_imprecise_dtypes=True), [], writes)
+        else:
+            op("g", lambda: g.iota(out, pattern, base, mult), [], writes)
+
+    def dma(q, out, in_, reads, writes, sem):
+        e = g.sync if q == "y" else S
+        op(q, lambda: e.dma_start(out, in_), reads, writes, sem)
+
+    def send(out, in_, sem, reads):
+        sent[0] += ne_out
+        op("g", lambda: g.remote_dma(out, in_, T.sem[sem], T.sem.sent, pid, rid, mask), reads, [], "remote")
+
+    dma("y", T.ut[:], T.u[:], [], ["ut"], "du")
+    dma("s", T.x0[:], T.x[:], [], ["x0"], "dx")
+    dma("y", T.nxi[:, 0:14], T.nx[:], [], ["nxi"], "dn")
+    dma("y", T.qw[:].bitcast(dt.uint8), T.wc[:], ["x0"], ["qw"], "dwc")
+    dma("y", T.sw[:], T.ws[:], [], ["sw"], "dws")
+    dma("y", T.vt[:], T.v[:], [], ["vt"], "dv")
+
+    iota(T.pi[:], [[0, 14]], 0, 1, ["pi"])
+    iota(T.c16[:], [[16, 14]], 0, 0, ["c16"])
+    iota(T.pcol[:], [[0, 1]], 0, 1, ["pcol"], True)
+    iota(T.rt[:, 0:256], [[1, 256]], -16, 0, ["rt"], True)
+    iota(T.gw[:, C:320], [[2, K], [0, 2]], 128, 0, ["g_slot"], True)
+    iota(T.rt[:, 256:PL], [[1, 2 * K], [0, 2]], C, 0, ["rt2"], True)
+    fill(T.ez[:], 0.0, ["ez"])
+    fill(T.fw[:], 0.0, ["fw"])
+    ts(T.pmi[:], T.pi[:], 15, None, Op.bitwise_and, None, ["pi"], ["pmi"])
+    cp("v", T.ul[:], T.c16[:, 0:8], ["c16"], ["ul"])
+    fill(T.at[:, 384:512], 0.0, ["at_pad"])
+    fill(T.ht[:, 384:512], 0.0, ["ht_pad"])
+    tt(T.jw[:], T.c16[:], T.pmi[:], Op.add, ["c16", "pmi"], ["jw"])
+    cp("v", T.pm16[:], T.pmi[:], ["pmi"], ["pm16"])
+    fill(T.tw[:, 240:4 * PL:PL], 0.0, ["tw_zero"])
+    fill(T.hb[:, 0:16], 0.0, ["hb_pad"])
+    fill(T.gw[:, 544:560], 120.0, ["g_end"])
+    ts(T.ez[:, 3:515:4], T.rt[:, 16:144], T.pcol[:], None, Op.is_equal, None, ["rt", "pcol"], ["ez"])
+    ts(T.k1[:], T.rt[:, 15:31], T.jw[:, 0:1], BIG, Op.is_equal, Op.mult, ["rt", "jw"], ["k1"])
+    ts(T.k2[:], T.rt[:, 16:32], T.jw[:, 0:1], None, Op.not_equal, None, ["rt", "jw"], ["k2"])
+    ts(T.sc[:], T.jw[:, 0:1], 15.0, 1.0 / BIG, Op.is_equal, Op.max, ["jw"], ["sc"])
+    tt(T.k16[:], T.k1[:], T.k2[:], Op.max, ["k1", "k2"], ["k16"])
+    for b in range(4):
+        quant(T.qe[:, 128 * b:128 * b + 128], T.se[:, 128 * b:128 * b + 128], T.ez[:, 3 - b:515 - b], ["ez"], ["qe%d" % b])
+    op("s", lambda: S.activation(T.gw[:, 0:C], T.rt[:, 16:240], Act.Identity, bias=8.0, scale=0.5), ["rt"], ["g_own"])
+    cp("s", T.kt[:], T.k16[:].indirect(T.pm16[:]), ["k16", "pm16"], ["kt"])
+
+    quant(T.qu[:], T.su[:], T.ut[:], ["ut"], ["qu"])
+    cp("v", T.nx16[:], T.nxi[:, 0:14], ["nxi"], ["nx16"])
+    cp("v", T.qur[:].bitcast(dt.uint32), T.qu[:].bitcast(dt.uint32).indirect(T.ul[:]), ["qu", "ul"], ["qur"])
+    cp("s", T.sur[:], T.su[:].indirect(T.ul[:]), ["qu", "ul"], ["sur"])
+    cp("s", T.gw[:, 320:544], T.gw[:, 0:C].indirect(T.nx16[:]), ["g_own", "nx16"], ["g_next"])
+
+    xkeys = ["x0"]
+    for t in range(R):
+        op(None, None, [], ["nin%d" % t], ("cnt%d" % t, ne_in))
+        op(None, None, [], ["arr%d" % t], ("arr%d" % t, 2 * ne_in))
+        quant(T.qx[:, 0:C], T.sx[:, 0:C], (T.x0 if t == 0 else T.xt)[:], xkeys, ["qx"])
+        mm(T.ps[:, 0:C], T.qur[:], T.sur[:], T.qx[:, 0:C], T.sx[:, 0:C], ["qur", "sur", "qx"], ["p:s"])
+        for b in range(4):
+            mm(T.pd[:, 512 * b:512 * b + C], T.qe[:, 128 * b:128 * b + 128], T.se[:, 128 * b:128 * b + 128],
+               T.qx[:, 0:C], T.sx[:, 0:C], ["qe%d" % b, "qx"], ["p:d%d" % b])
+        for b in range(4):
+            cp("s", T.tw[:, PL * b + 16:PL * b + 240], T.pd[:, 512 * b:512 * b + C], ["p:d%d" % b], ["T%d" % b])
+        ts(T.fb[:], T.ps[:, 0:C], 0.0, 1.0, Op.is_gt, Op.add, ["p:s"], ["fb"])
+        cp("v", T.f2[:], T.fb[:], ["fb"], ["f2"])
+        tt(T.mb[:], T.fb[:].indirect(T.nx16[:]), T.f2[:], Op.is_lt, ["fb", "f2", "nx16"], ["mb"])
+        cc = T.cb[:, C * t:C * t + C]
+        scan(cc, T.mb[:], T.mb[:], 0.0, Op.add, Op.max, ["mb"], ["c%d" % t])
+        send(T.nin[:, 8 * t:8 * t + 8], T.cb[:, C * t + C - 8:C * t + C], "cnt%d" % t, ["c%d" % t])
+        for r in range(3):
+            ts(T.ub[:, C * r:C * r + C], cc, T.jw[:, r:r + 1], None, Op.is_le, None, ["c%d" % t, "jw"], ["u%d" % r])
+        for r in range(3):
+            scan(T.cn[:, 112 * r:112 * r + 112], T.ub[:, C * r:C * r + 112], T.ub[:, C * r + 112:C * r + C], 16.0,
+                 Op.add, Op.add, ["u%d" % r], ["cn%d" % r])
+        ts(T.la[:, 0:3], T.cn[:, 111:336:112], 0.0, None, Op.add, None, ["cn0", "cn1", "cn2"], ["la"])
+        cp("v", T.nb[:], T.gw[:, 304:560].indirect(T.la[:, 0:3]), ["la", "g_slot", "g_next", "g_end"], ["nb"])
+        for b in range(4):
+            cp("s", T.at[:, b:384:8], T.tw[:, PL * b:PL * b + 256].indirect(T.la[:, 0:3]),
+               ["la", "T%d" % b, "tw_zero"], ["Aa%d" % b])
+        wrap(T.nw[:], T.nb[:], K, ["nb"], ["nw"])
+        ts(T.lb[:, 0:3], T.nw[:, 15:K:16], T.sc[:], 2.0, Op.mult, Op.mult, ["nw", "sc"], ["lb"])
+        for b in range(4):
+            cp("v" if b < 3 else "s", T.at[:, 4 + b:384:8], T.tw[:, PL * b:PL * b + 256].indirect(T.lb[:, 0:3]),
+               ["lb", "T%d" % b, "tw_zero"], ["Ab%d" % b])
+        quant(T.qa[:, 128 * t:128 * t + 128], T.sa[:, 128 * t:128 * t + 128], T.at[:],
+              ["at_pad"] + ["Aa%d" % b for b in range(4)] + ["Ab%d" % b for b in range(4)], ["qa%d" % t])
+        lo = C + 2 * K * t
+        send(T.qx[:, lo:lo + 2 * K].bitcast(dt.uint8), T.qa[:, 128 * t:128 * t + 2 * K].bitcast(dt.uint8), "arr%d" % t, ["qa%d" % t])
+        send(T.sx[:, lo:lo + 2 * K], T.sa[:, 128 * t:128 * t + 2 * K], "arr%d" % t, ["qa%d" % t])
+
+        if t == 0:
+            op("v", lambda: V.tensor_copy(T.gw[:, 640:864].indirect(T.nx16[:]), T.gw[:, 0:C]), ["g_own", "nx16"], ["g_prev"])
+            wrap(T.hw[:], T.gw[:, 640:864], C, ["g_prev"], ["hw"])
+            ts(T.jm[:], T.jw[:], -222.0, None, Op.add, None, ["jw"], ["jm"])
+            ts(T.pv16[:], T.hw[:, 15:C:16], T.sc[:], 2.0, Op.mult, Op.mult, ["hw", "sc"], ["pv16"])
+        tt(T.hb[:, 16:240], T.fb[:].indirect(T.nx16[:]), T.f2[:], Op.is_gt, ["fb", "f2", "nx16"], ["hb"])
+        scan(T.zb[:, 16:240], T.hb[:, 16:240], T.hb[:, 15:239], 0.0, Op.add, Op.add, ["hb", "hb_pad"], ["zb"])
+        cp("s", T.zp[:], T.zb[:].indirect(T.pv16[:]), ["zb", "pv16"], ["zp"])
+        wrap(T.wr[:, 2 * C:3 * C], T.fb[:], C, ["fb"], ["w2"])
+        wrap(T.wr[:, 0:C], T.zb[:, 16:240], C, ["zb"], ["w0"])
+        if t == 1:
+            quant(T.qv[:], T.sv[:], T.vt[:], ["vt"], ["qv"])
+        wrap(T.wr[:, C:2 * C], T.zp[:], C, ["zp"], ["w1"])
+        ts(T.zi[:], T.wr[:, 15:3 * C:16], T.sc[:], None, Op.mult, None, ["w0", "w1", "w2", "sc"], ["zi"])
+        ts(T.od[:], T.zi[:, 0:28], 1, None, Op.bitwise_and, None, ["zi"], ["od"])
+        tt(T.tq[:], T.zi[:, 0:28], T.od[:], Op.mult, ["zi", "od"], ["tq"])
+        tt(T.qq[:], T.tq[:, 0:14], T.tq[:, 14:28], Op.add, ["tq"], ["qq"])
+        ts(T.zf[:], T.qq[:], 0.0, 320.0, Op.is_equal, Op.mult, ["qq"], ["zf"])
+        tt(T.kk[:], T.qq[:], T.zi[:, 28:42], Op.add, ["qq", "zi"], ["kk"])
+        ts(T.thr[:], T.nin[:, 8 * t + 7:8 * t + 8], float(K), 2.0, Op.min, Op.mult, ["nin%d" % t], ["thr"])
+        tt(T.y1[:], T.zf[:], T.zi[:, 28:42], Op.mult, ["zf", "zi"], ["y1"])
+        ts(T.pn[:], T.qq[:], T.thr[:], -1000.0, Op.is_gt, Op.mult, ["qq", "thr"], ["pn"])
+        tt(T.y2[:], T.y1[:], T.jm[:], Op.add, ["y1", "jm"], ["y2"])
+        tt(T.x1[:], T.pn[:], T.kk[:], Op.add, ["pn", "kk"], ["x1"])
+        tt(T.l1[:], T.y2[:], T.x1[:], Op.max, ["y2", "x1"], ["l1"])
+        ts(T.l16[:], T.l1[:], 222.0, None, Op.add, None, ["l1"], ["l16"])
+
+        for b in range(4):
+            mm(T.pd[:, 512 * b:512 * b + 128], T.qw[:, 128 * b:128 * b + 128], T.sw[:, 128 * b:128 * b + 128],
+               T.qx[:, lo - 32:lo + 2 * K], T.sx[:, lo - 32:lo + 2 * K],
+               ["qw", "sw", "arr%d" % t, "qx" if t == 0 else "arr%d" % (t - 1)], ["p:d%d" % b])
+        for b in range(4):
+            o, i = T.ht[:, b:384:4], T.pd[:, 512 * b + 32:512 * b + 128]
+            if b % 2 == 0:
+                op("s", lambda o=o, i=i: S.activation(o, i, Act.Copy, scale=0.03125), ["p:d%d" % b], ["H%d" % b])
+            else:
+                ts(o, i, 0.03125, None, Op.mult, None, ["p:d%d" % b], ["H%d" % b])
+        quant(T.qh[:], T.sh[:], T.ht[:], ["ht_pad", "H0", "H1", "H2", "H3"], ["qh"])
+        mm(T.pp[:, 0:128], T.qur[:], T.sur[:], T.qh[:], T.sh[:], ["qur", "sur", "qh"], ["p:p"])
+        cp("s", T.h0[:], T.gw[:].indirect(T.l16[:]), ["l16", "g_own", "g_slot", "g_next", "g_end", "g_prev"], ["h0"])
+        for b in range(4):
+            cp("s", T.tw[:, PL * b + 256:PL * b + PL:2], T.ht[:, b:384:4], ["H%d" % b], ["TH%d" % b])
+        cp("v", T.pa[:], T.pp[:, 0:2 * K:2], ["p:p"], ["pa"])
+        tt(T.fw[:, C:320:2], T.pp[:, 1:2 * K:2], T.pa[:], Op.is_gt, ["p:p", "pa", "fw"], ["gt"])
+        tt(T.fw[:, C + 1:320:2], T.pp[:, 1:2 * K:2], T.pa[:], Op.is_le, ["p:p", "pa", "fw"], ["le"])
+        tt(T.hv[:], T.fw[:].indirect(T.l16[:]), T.h0[:], Op.add, ["gt", "le", "fw", "l16", "h0"], ["hv"])
+        wrap(T.hw[:], T.hv[:], C, ["hv"], ["hw"])
+        ts(T.lx[:], T.hw[:, 15:C:16], T.sc[:], 2.0, Op.mult, Op.mult, ["hw", "sc"], ["lx"])
+        for b in range(4):
+            cp("vs"[b % 2], T.xt[:, b:4 * C:4], T.tw[:, PL * b:PL * b + PL].indirect(T.lx[:]),
+               ["lx", "T%d" % b, "TH%d" % b, "tw_zero"], ["X%d" % b])
+        xkeys = ["X0", "X1", "X2", "X3"]
+
+    cp("s", T.ots[:], T.rt[:].indirect(T.lx[:]), ["rt", "rt2", "lx"], ["ots"])
+    quant(T.qx[:, 0:C], T.sx[:, 0:C], T.xt[:], xkeys, ["qx"])
+    mm(T.ps[:, 0:C], T.qv[:], T.sv[:], T.qx[:, 0:C], T.sx[:, 0:C], ["qv", "qx"], ["p:s"])
+    cp("v", T.ys[:], T.ps[:, 0:C], ["p:s"], ["ys"])
+    dma("y", T.oc[:], T.qx[:, 0:C].bitcast(dt.uint8), ["qx"], [], "doc")
+    dma("s", T.ot[:], T.ots[0:128:16, :], ["ots"], [], "dot")
+    for k in range(4):
+        dma("ys"[k % 2], T.osc[4 * k:4 * k + 4, :], T.sx[32 * k:32 * k + 4, 0:C], ["qx"], [], "ds%d" % k)
+    dma("y", T.y[:], T.ys[:], ["ys"], [], "dy")
+    _emit(g, T, ops, sent[0])

@@ -3,38 +3,19 @@ from concourse.mybir import dt, AluOpType as Op, ActivationFunctionType as Act
 C, K, R = 224, 48, 3
 PL = 448
 BIG = 65536.0
-CODE, PLANE = "float8_e4m3fn_x4", "uint8"
-
-
-def _sb(n, d):
-    return ("sbuf", [128, n], d)
-
-
-SCRATCH = {
-    "x0": _sb(896, "bfloat16"), "ut": _sb(512, "bfloat16"), "vt": _sb(512, "bfloat16"), "nxi": _sb(16, "int32"),
-    "qu": _sb(128, CODE), "su": _sb(128, PLANE), "qur": _sb(128, CODE), "sur": _sb(128, PLANE),
-    "qv": _sb(128, CODE), "sv": _sb(128, PLANE), "qw": _sb(512, CODE), "sw": _sb(512, PLANE),
-    "ez": _sb(528, "bfloat16"), "qe": _sb(512, CODE), "se": _sb(512, PLANE),
-    "qx": _sb(512, CODE), "sx": _sb(512, PLANE), "xt": _sb(896, "bfloat16"), "tw": _sb(4 * PL, "bfloat16"),
-    "at": _sb(512, "bfloat16"), "qa": _sb(384, CODE), "sa": _sb(384, PLANE),
-    "ht": _sb(512, "bfloat16"), "qh": _sb(128, CODE), "sh": _sb(128, PLANE),
-    "fb": _sb(C, "bfloat16"), "f2": _sb(C, "bfloat16"), "mb": _sb(C, "bfloat16"), "cb": _sb(R * C, "bfloat16"),
-    "ub": _sb(3 * C, "bfloat16"),
-    "cn": _sb(336, "bfloat16"), "la": _sb(4, "uint16"), "nb": _sb(K, "bfloat16"), "nw": _sb(K, "bfloat16"),
-    "lb": _sb(4, "uint16"), "nin": _sb(8 * R, "bfloat16"), "thr": _sb(1, "float32"),
-    "hb": _sb(240, "bfloat16"), "zb": _sb(240, "bfloat16"), "zp": _sb(C, "bfloat16"), "wr": _sb(3 * C, "bfloat16"),
-    "zi": _sb(42, "int32"), "od": _sb(28, "int32"), "tq": _sb(28, "float32"), "qq": _sb(14, "float32"),
-    "kk": _sb(14, "float32"), "zf": _sb(14, "float32"), "y1": _sb(14, "float32"), "y2": _sb(14, "float32"),
-    "pn": _sb(14, "float32"), "x1": _sb(14, "float32"), "l1": _sb(14, "float32"), "l16": _sb(14, "uint16"),
-    "gw": _sb(864, "bfloat16"), "fw": _sb(864, "bfloat16"), "h0": _sb(C, "bfloat16"), "hv": _sb(C, "bfloat16"),
-    "hw": _sb(C, "bfloat16"), "lx": _sb(14, "uint16"), "pa": _sb(K, "float32"),
-    "rt": _sb(PL, "float32"), "kt": _sb(C, "bfloat16"), "k16": _sb(16, "bfloat16"), "k1": _sb(16, "float32"),
-    "k2": _sb(16, "float32"), "pi": _sb(14, "int32"), "c16": _sb(14, "int32"), "pmi": _sb(14, "int32"),
-    "pcol": _sb(1, "float32"), "ul": _sb(8, "uint16"), "pm16": _sb(14, "uint16"), "jw": _sb(14, "float32"),
-    "jm": _sb(14, "float32"), "sc": _sb(1, "float32"), "nx16": _sb(14, "uint16"), "pv16": _sb(14, "uint16"),
-    "ys": _sb(C, "float32"), "ots": _sb(C, "float32"),
-    "ps": ("psum", [128, 512], "float32"), "pd": ("psum", [128, 2048], "float32"), "pp": ("psum", [128, 512], "float32"),
+_B = {
+    "bfloat16": dict(x0=896, ut=512, vt=512, ez=528, xt=896, tw=4 * PL, tn=1024, at=512, ht=512, fb=C, f2=C, sg=C, mb=C, cb=R * C,
+                     ub=3 * C, cn=3 * C, one=C, dk=C, nin=8 * R, hb=240, zb=240, zp=C, wf=C, wz=C, gw=864, fw=864, h0=C, hv=C,
+                     hw=C, kt=C, k16=16),
+    "float32": dict(thr=1, qq=14, fi=14, f3=14, fj=14, s1=14, s2=14, dp=14, dq=14, pvf=14, t1=14, fp=14, y1=14, pn=14, x1=14, l1=14,
+                    pa=K, rt=PL, k1=16, k2=16, pcol=1, jw=14, jm=14, j16=14, nk=4, sc=1, ys=C, ots=C),
+    "int32": dict(nxi=16, zi=14, od=14, pi=14, c16=14, pmi=14),
+    "uint16": dict(la=4, l16=14, lx=14, ul=8, pm16=14, nx16=14, nxp=14, sel=14),
+    "float8_e4m3fn_x4": dict(qu=128, qur=128, qv=128, qw=512, qe=512, qx=512, qa=384, qh=128),
+    "uint8": dict(su=128, sur=128, sv=128, sw=512, se=512, sx=512, sa=384, sh=128),
 }
+SCRATCH = {k: ("sbuf", [128, n], d) for d, b in _B.items() for k, n in b.items()}
+SCRATCH.update({k: ("psum", [128, n], "float32") for k, n in (("ps", 512), ("pd", 2048), ("pp", 512))})
 DMAS = ["du", "dn", "dx", "dwc", "dws", "dv", "doc", "ds0", "ds1", "ds2", "ds3", "dy", "dot"]
 SEMAPHORES = ["cv", "cs", "ct", "cg", "sent"] + DMAS + ["arr%d" % t for t in range(R)] + ["cnt%d" % t for t in range(R)]
 
@@ -46,6 +27,7 @@ def _emit(g, T, ops, sent):
     known = {q: {} for q in eng}
     writer, readers, mark = {}, {}, []
     for i, (q, fn, reads, writes, kind) in enumerate(ops):
+        reads, writes = reads.split(), writes.split()
         deps = set()
         for k in reads:
             if k in writer:
@@ -100,191 +82,214 @@ def rank_program(g, core, T, topo):
     ops = []
     sent = [0]
 
-    def op(q, fn, reads, writes, kind=None):
-        ops.append((q, fn, reads, writes, kind))
+    def op(q, fn, r, w, kind=None):
+        ops.append((q, fn, r, w, kind))
 
-    def ts(out, in0, a, b, o0, o1, reads, writes):
+    def ts(out, in0, a, b, o0, o1, r, w):
         if o1 is None:
-            op("v", lambda: V.tensor_scalar(out, in0, a, None, o0), reads, writes)
+            op("v", lambda: V.tensor_scalar(out, in0, a, None, o0), r, w)
         else:
-            op("v", lambda: V.tensor_scalar(out, in0, a, b, o0, o1), reads, writes)
+            op("v", lambda: V.tensor_scalar(out, in0, a, b, o0, o1), r, w)
 
-    def tt(out, in0, in1, o, reads, writes):
-        op("v", lambda: V.tensor_tensor(out, in0, in1, o), reads, writes)
+    def tt(out, in0, in1, o, r, w):
+        op("v", lambda: V.tensor_tensor(out, in0, in1, o), r, w)
 
-    def cp(q, out, in_, reads, writes):
+    def cp(q, out, in_, r, w):
         if q == "v":
-            op("v", lambda: V.tensor_copy(out, in_), reads, writes)
+            op("v", lambda: V.tensor_copy(out, in_), r, w)
         else:
-            op("s", lambda: S.activation(out, in_, Act.Copy), reads, writes)
+            op("s", lambda: S.activation(out, in_, Act.Copy), r, w)
 
-    def scan(out, d0, d1, init, o0, o1, reads, writes):
-        op("v", lambda: V.tensor_tensor_scan(out, d0, d1, init, o0, o1), reads, writes)
+    def scan(out, d0, d1, init, o0, o1, r, w):
+        op("v", lambda: V.tensor_tensor_scan(out, d0, d1, init, o0, o1), r, w)
 
-    def wrap(out, in_, n, reads, writes):
-        scan(out, T.kt[:, 0:n], in_, 0.0, Op.mult, Op.max, reads + ["kt"], writes)
+    def wrap(out, in_, n, r, w):
+        scan(out, T.kt[:, 0:n], in_, 0.0, Op.mult, Op.max, r + " kt", w)
 
-    def quant(q, s, in_, reads, writes):
-        op("v", lambda: V.quantize_mx(q, s, in_), reads, writes)
+    def quant(q, s, in_, r, w):
+        op("v", lambda: V.quantize_mx(q, s, in_), r, w)
 
-    def mm(out, a, sa, b, sb, reads, writes):
-        op("t", lambda: PE.matmul_mx(out, a, sa, b, sb, True, True), reads, writes)
+    def mm(out, a, sa, b, sb, r, w):
+        op("t", lambda: PE.matmul_mx(out, a, sa, b, sb, True, True), r, w)
 
-    def fill(ap, val, writes):
-        op("v", lambda: V.memset(ap, val), [], writes)
+    def fill(ap, val, w):
+        op("v", lambda: V.memset(ap, val), "", w)
 
-    def iota(out, pattern, base, mult, writes, small=False):
+    def iota(out, pattern, base, mult, w, small=False):
         if small:
-            op("g", lambda: g.iota(out, pattern, base, mult, allow_small_or_imprecise_dtypes=True), [], writes)
+            op("g", lambda: g.iota(out, pattern, base, mult, allow_small_or_imprecise_dtypes=True), "", w)
         else:
-            op("g", lambda: g.iota(out, pattern, base, mult), [], writes)
+            op("g", lambda: g.iota(out, pattern, base, mult), "", w)
 
-    def dma(q, out, in_, reads, writes, sem):
+    def dma(q, out, in_, r, w, sem):
         e = g.sync if q == "y" else S
-        op(q, lambda: e.dma_start(out, in_), reads, writes, sem)
+        op(q, lambda: e.dma_start(out, in_), r, w, sem)
 
-    def send(out, in_, sem, reads):
+    def send(out, in_, sem, r):
         sent[0] += ne_out
-        op("g", lambda: g.remote_dma(out, in_, T.sem[sem], T.sem.sent, pid, rid, mask), reads, [], "remote")
+        op("g", lambda: g.remote_dma(out, in_, T.sem[sem], T.sem.sent, pid, rid, mask), r, "", "remote")
 
-    dma("y", T.ut[:], T.u[:], [], ["ut"], "du")
-    dma("s", T.x0[:], T.x[:], [], ["x0"], "dx")
-    dma("y", T.nxi[:, 0:14], T.nx[:], [], ["nxi"], "dn")
-    dma("y", T.qw[:].bitcast(dt.uint8), T.wc[:], ["x0"], ["qw"], "dwc")
-    dma("y", T.sw[:], T.ws[:], [], ["sw"], "dws")
-    dma("y", T.vt[:], T.v[:], [], ["vt"], "dv")
+    dma("y", T.ut[:], T.u[:], "", "ut", "du")
+    dma("s", T.x0[:], T.x[:], "", "x0", "dx")
+    dma("y", T.nxi[:, 0:14], T.nx[:], "", "nxi", "dn")
+    dma("y", T.qw[:].bitcast(dt.uint8), T.wc[:], "x0", "qw", "dwc")
+    dma("y", T.sw[:], T.ws[:], "", "sw", "dws")
+    dma("y", T.vt[:], T.v[:], "", "vt", "dv")
 
-    iota(T.pi[:], [[0, 14]], 0, 1, ["pi"])
-    iota(T.c16[:], [[16, 14]], 0, 0, ["c16"])
-    iota(T.pcol[:], [[0, 1]], 0, 1, ["pcol"], True)
-    iota(T.rt[:, 0:256], [[1, 256]], -16, 0, ["rt"], True)
-    iota(T.gw[:, C:320], [[2, K], [0, 2]], 128, 0, ["g_slot"], True)
-    iota(T.rt[:, 256:PL], [[1, 2 * K], [0, 2]], C, 0, ["rt2"], True)
-    fill(T.ez[:], 0.0, ["ez"])
-    fill(T.fw[:], 0.0, ["fw"])
-    ts(T.pmi[:], T.pi[:], 15, None, Op.bitwise_and, None, ["pi"], ["pmi"])
-    cp("v", T.ul[:], T.c16[:, 0:8], ["c16"], ["ul"])
-    fill(T.at[:, 384:512], 0.0, ["at_pad"])
-    fill(T.ht[:, 384:512], 0.0, ["ht_pad"])
-    tt(T.jw[:], T.c16[:], T.pmi[:], Op.add, ["c16", "pmi"], ["jw"])
-    cp("v", T.pm16[:], T.pmi[:], ["pmi"], ["pm16"])
-    fill(T.tw[:, 240:4 * PL:PL], 0.0, ["tw_zero"])
-    fill(T.hb[:, 0:16], 0.0, ["hb_pad"])
-    fill(T.gw[:, 544:560], 120.0, ["g_end"])
-    ts(T.ez[:, 3:515:4], T.rt[:, 16:144], T.pcol[:], None, Op.is_equal, None, ["rt", "pcol"], ["ez"])
-    ts(T.k1[:], T.rt[:, 15:31], T.jw[:, 0:1], BIG, Op.is_equal, Op.mult, ["rt", "jw"], ["k1"])
-    ts(T.k2[:], T.rt[:, 16:32], T.jw[:, 0:1], None, Op.not_equal, None, ["rt", "jw"], ["k2"])
-    ts(T.sc[:], T.jw[:, 0:1], 15.0, 1.0 / BIG, Op.is_equal, Op.max, ["jw"], ["sc"])
-    tt(T.k16[:], T.k1[:], T.k2[:], Op.max, ["k1", "k2"], ["k16"])
+    iota(T.pi[:], [[0, 14]], 0, 1, "pi")
+    iota(T.c16[:], [[16, 14]], 0, 0, "c16")
+    iota(T.pcol[:], [[0, 1]], 0, 1, "pcol", True)
+    iota(T.rt[:, 0:256], [[1, 256]], -16, 0, "rt", True)
+    iota(T.dk[:], [[-1, C]], 239, 0, "dk", True)
+    iota(T.gw[:, C:320], [[2, K], [0, 2]], 128, 0, "g_slot", True)
+    iota(T.rt[:, 256:PL], [[1, 2 * K], [0, 2]], C, 0, "rt2", True)
+    fill(T.ez[:], 0.0, "ez")
+    fill(T.fw[:], 0.0, "fw")
+    ts(T.pmi[:], T.pi[:], 15, None, Op.bitwise_and, None, "pi", "pmi")
+    cp("v", T.ul[:], T.c16[:, 0:8], "c16", "ul")
+    fill(T.at[:, 384:512], 0.0, "at_pad")
+    fill(T.ht[:, 384:512], 0.0, "ht_pad")
+    tt(T.jw[:], T.c16[:], T.pmi[:], Op.add, "c16 pmi", "jw")
+    cp("v", T.pm16[:], T.pmi[:], "pmi", "pm16")
+    fill(T.tw[:, 240:4 * PL:PL], 0.0, "tw_zero")
+    fill(T.tn[:, 240:1024:256], 0.0, "tn_zero")
+    fill(T.hb[:, 0:16], 0.0, "hb_pad")
+    fill(T.one[:], 1.0, "one")
+    ts(T.ez[:, 3:515:4], T.rt[:, 16:144], T.pcol[:], None, Op.is_equal, None, "rt pcol", "ez")
+    ts(T.k1[:], T.rt[:, 15:31], T.jw[:, 0:1], BIG, Op.is_equal, Op.mult, "rt jw", "k1")
+    ts(T.k2[:], T.rt[:, 16:32], T.jw[:, 0:1], None, Op.not_equal, None, "rt jw", "k2")
+    ts(T.sc[:], T.jw[:, 0:1], 15.0, 1.0 / BIG, Op.is_equal, Op.max, "jw", "sc")
+    ts(T.nk[:], T.jw[:, 0:4], -1.0, None, Op.mult, None, "jw", "nk")
     for b in range(4):
-        quant(T.qe[:, 128 * b:128 * b + 128], T.se[:, 128 * b:128 * b + 128], T.ez[:, 3 - b:515 - b], ["ez"], ["qe%d" % b])
-    op("s", lambda: S.activation(T.gw[:, 0:C], T.rt[:, 16:240], Act.Identity, bias=8.0, scale=0.5), ["rt"], ["g_own"])
-    cp("s", T.kt[:], T.k16[:].indirect(T.pm16[:]), ["k16", "pm16"], ["kt"])
+        quant(T.qe[:, 128 * b:128 * b + 128], T.se[:, 128 * b:128 * b + 128], T.ez[:, 3 - b:515 - b], "ez", "qe%d" % b)
+        if b == 0:
+            tt(T.k16[:], T.k1[:], T.k2[:], Op.max, "k1 k2", "k16")
+    op("s", lambda: S.activation(T.gw[:, 0:C], T.rt[:, 16:240], Act.Identity, bias=8.0, scale=0.5), "rt", "g_own")
+    cp("s", T.kt[:], T.k16[:].indirect(T.pm16[:]), "k16 pm16", "kt")
 
-    quant(T.qu[:], T.su[:], T.ut[:], ["ut"], ["qu"])
-    cp("v", T.nx16[:], T.nxi[:, 0:14], ["nxi"], ["nx16"])
-    cp("v", T.qur[:].bitcast(dt.uint32), T.qu[:].bitcast(dt.uint32).indirect(T.ul[:]), ["qu", "ul"], ["qur"])
-    cp("s", T.sur[:], T.su[:].indirect(T.ul[:]), ["qu", "ul"], ["sur"])
-    cp("s", T.gw[:, 320:544], T.gw[:, 0:C].indirect(T.nx16[:]), ["g_own", "nx16"], ["g_next"])
+    quant(T.qu[:], T.su[:], T.ut[:], "ut", "qu")
+    cp("v", T.nx16[:], T.nxi[:, 0:14], "nxi", "nx16")
+    ts(T.nxp[:], T.nxi[:, 0:14], 16.0, None, Op.add, None, "nxi", "nxp")
+    cp("v", T.qur[:].bitcast(dt.uint32), T.qu[:].bitcast(dt.uint32).indirect(T.ul[:]), "qu ul", "qur")
+    cp("s", T.sur[:], T.su[:].indirect(T.ul[:]), "qu ul", "sur")
+    cp("s", T.gw[:, 320:544], T.gw[:, 0:C].indirect(T.nx16[:]), "g_own nx16", "g_next")
 
-    xkeys = ["x0"]
+    def tcopy(q, b):
+        cp(q, T.tw[:, PL * b + 16:PL * b + 240], T.pd[:, 512 * b:512 * b + C], "p:d%d" % b, "T%d" % b)
+
+    xkeys = "x0"
     for t in range(R):
-        op(None, None, [], ["nin%d" % t], ("cnt%d" % t, ne_in))
-        op(None, None, [], ["arr%d" % t], ("arr%d" % t, 2 * ne_in))
-        quant(T.qx[:, 0:C], T.sx[:, 0:C], (T.x0 if t == 0 else T.xt)[:], xkeys, ["qx"])
-        mm(T.ps[:, 0:C], T.qur[:], T.sur[:], T.qx[:, 0:C], T.sx[:, 0:C], ["qur", "sur", "qx"], ["p:s"])
+        op(None, None, "", "nin%d" % t, ("cnt%d" % t, ne_in))
+        op(None, None, "", "arr%d" % t, ("arr%d" % t, 2 * ne_in))
+        quant(T.qx[:, 0:C], T.sx[:, 0:C], (T.x0 if t == 0 else T.xt)[:], xkeys, "qx")
+        mm(T.ps[:, 0:C], T.qur[:], T.sur[:], T.qx[:, 0:C], T.sx[:, 0:C], "qur sur qx", "p:s")
+        mm(T.pp[:, 0:C], T.qur[:], T.sur[:], T.qx[:, 0:C], T.sx[:, 0:C], "qur sur qx", "p:p")
         for b in range(4):
             mm(T.pd[:, 512 * b:512 * b + C], T.qe[:, 128 * b:128 * b + 128], T.se[:, 128 * b:128 * b + 128],
-               T.qx[:, 0:C], T.sx[:, 0:C], ["qe%d" % b, "qx"], ["p:d%d" % b])
-        for b in range(4):
-            cp("s", T.tw[:, PL * b + 16:PL * b + 240], T.pd[:, 512 * b:512 * b + C], ["p:d%d" % b], ["T%d" % b])
-        ts(T.fb[:], T.ps[:, 0:C], 0.0, 1.0, Op.is_gt, Op.add, ["p:s"], ["fb"])
-        cp("v", T.f2[:], T.fb[:], ["fb"], ["f2"])
-        tt(T.mb[:], T.fb[:].indirect(T.nx16[:]), T.f2[:], Op.is_lt, ["fb", "f2", "nx16"], ["mb"])
-        cc = T.cb[:, C * t:C * t + C]
-        scan(cc, T.mb[:], T.mb[:], 0.0, Op.add, Op.max, ["mb"], ["c%d" % t])
-        send(T.nin[:, 8 * t:8 * t + 8], T.cb[:, C * t + C - 8:C * t + C], "cnt%d" % t, ["c%d" % t])
+               T.qx[:, 0:C], T.sx[:, 0:C], "qe%d qx" % b, "p:d%d" % b)
+        ts(T.fb[:], T.ps[:, 0:C], 0.0, 1.0, Op.is_gt, Op.add, "p:s", "fb")
+        op("s", lambda: S.activation(T.sg[:], T.pp[:, 0:C], Act.Sign), "p:p", "sg")
+        tcopy("v", 0)
+        tcopy("s", 2)
+        tcopy("s", 3)
+        tt(T.mb[:], T.fb[:].indirect(T.nx16[:]), T.sg[:], Op.is_le, "fb sg nx16", "mb")
+        tcopy("v", 1)
+        for b in (2, 3, 0, 1):
+            cp("s", T.tn[:, 256 * b + 16:256 * b + 240], T.tw[:, PL * b:PL * b + 256].indirect(T.nxp[:]), "nxp tw_zero T%d" % b, "N%d" % b)
         for r in range(3):
-            ts(T.ub[:, C * r:C * r + C], cc, T.jw[:, r:r + 1], None, Op.is_le, None, ["c%d" % t, "jw"], ["u%d" % r])
+            scan(T.ub[:, C * r:C * r + C], T.mb[:], T.one[:], T.nk[:, r:r + 1], Op.add, Op.min, "mb one nk", "u%d" % r)
         for r in range(3):
-            scan(T.cn[:, 112 * r:112 * r + 112], T.ub[:, C * r:C * r + 112], T.ub[:, C * r + 112:C * r + C], 16.0,
-                 Op.add, Op.add, ["u%d" % r], ["cn%d" % r])
-        ts(T.la[:, 0:3], T.cn[:, 111:336:112], 0.0, None, Op.add, None, ["cn0", "cn1", "cn2"], ["la"])
-        cp("v", T.nb[:], T.gw[:, 304:560].indirect(T.la[:, 0:3]), ["la", "g_slot", "g_next", "g_end"], ["nb"])
+            scan(T.cn[:, C * r:C * r + C], T.ub[:, C * r:C * r + C], T.dk[:], 240.0, Op.mult, Op.max, "dk u%d" % r, "cn%d" % r)
+        cc, ck = T.cb[:, C * t:C * t + C], "c%d" % t
+        scan(cc, T.mb[:], T.mb[:], 0.0, Op.add, Op.max, "mb", ck)
+        send(T.nin[:, 8 * t:8 * t + 8], T.cb[:, C * t + C - 8:C * t + C], "cnt%d" % t, ck)
+        ts(T.la[:, 0:3], T.cn[:, C - 1:3 * C:C], -1.0, 256.0, Op.mult, Op.add, "cn0 cn1 cn2", "la")
+        wrap(T.wf[:], T.fb[:], C, "fb", "wf")
         for b in range(4):
-            cp("s", T.at[:, b:384:8], T.tw[:, PL * b:PL * b + 256].indirect(T.la[:, 0:3]),
-               ["la", "T%d" % b, "tw_zero"], ["Aa%d" % b])
-        wrap(T.nw[:], T.nb[:], K, ["nb"], ["nw"])
-        ts(T.lb[:, 0:3], T.nw[:, 15:K:16], T.sc[:], 2.0, Op.mult, Op.mult, ["nw", "sc"], ["lb"])
-        for b in range(4):
-            cp("v" if b < 3 else "s", T.at[:, 4 + b:384:8], T.tw[:, PL * b:PL * b + 256].indirect(T.lb[:, 0:3]),
-               ["lb", "T%d" % b, "tw_zero"], ["Ab%d" % b])
+            cp("v", T.at[:, b:384:8], T.tw[:, PL * b:PL * b + 256].indirect(T.la[:, 0:3]), "la T%d tw_zero" % b, "Aa%d" % b)
+        for b in (2, 3, 0, 1):
+            cp("s", T.at[:, 4 + b:384:8], T.tn[:, 256 * b:256 * b + 256].indirect(T.la[:, 0:3]), "la N%d tn_zero" % b, "Ab%d" % b)
+        cp("v", T.f2[:], T.fb[:], "fb", "f2")
+        ts(T.fi[:], T.wf[:, 15:C:16], T.sc[:], None, Op.mult, None, "wf sc", "fi")
         quant(T.qa[:, 128 * t:128 * t + 128], T.sa[:, 128 * t:128 * t + 128], T.at[:],
-              ["at_pad"] + ["Aa%d" % b for b in range(4)] + ["Ab%d" % b for b in range(4)], ["qa%d" % t])
+              "at_pad Aa0 Aa1 Aa2 Aa3 Ab0 Ab1 Ab2 Ab3", "qa%d" % t)
         lo = C + 2 * K * t
-        send(T.qx[:, lo:lo + 2 * K].bitcast(dt.uint8), T.qa[:, 128 * t:128 * t + 2 * K].bitcast(dt.uint8), "arr%d" % t, ["qa%d" % t])
-        send(T.sx[:, lo:lo + 2 * K], T.sa[:, 128 * t:128 * t + 2 * K], "arr%d" % t, ["qa%d" % t])
+        send(T.qx[:, lo:lo + 2 * K].bitcast(dt.uint8), T.qa[:, 128 * t:128 * t + 2 * K].bitcast(dt.uint8), "arr%d" % t, "qa%d" % t)
+        send(T.sx[:, lo:lo + 2 * K], T.sa[:, 128 * t:128 * t + 2 * K], "arr%d" % t, "qa%d" % t)
 
         if t == 0:
-            op("v", lambda: V.tensor_copy(T.gw[:, 640:864].indirect(T.nx16[:]), T.gw[:, 0:C]), ["g_own", "nx16"], ["g_prev"])
-            wrap(T.hw[:], T.gw[:, 640:864], C, ["g_prev"], ["hw"])
-            ts(T.jm[:], T.jw[:], -222.0, None, Op.add, None, ["jw"], ["jm"])
-            ts(T.pv16[:], T.hw[:, 15:C:16], T.sc[:], 2.0, Op.mult, Op.mult, ["hw", "sc"], ["pv16"])
-        tt(T.hb[:, 16:240], T.fb[:].indirect(T.nx16[:]), T.f2[:], Op.is_gt, ["fb", "f2", "nx16"], ["hb"])
-        scan(T.zb[:, 16:240], T.hb[:, 16:240], T.hb[:, 15:239], 0.0, Op.add, Op.add, ["hb", "hb_pad"], ["zb"])
-        cp("s", T.zp[:], T.zb[:].indirect(T.pv16[:]), ["zb", "pv16"], ["zp"])
-        wrap(T.wr[:, 2 * C:3 * C], T.fb[:], C, ["fb"], ["w2"])
-        wrap(T.wr[:, 0:C], T.zb[:, 16:240], C, ["zb"], ["w0"])
+            op("v", lambda: V.tensor_copy(T.gw[:, 640:864].indirect(T.nx16[:]), T.gw[:, 0:C]), "g_own nx16", "g_prev")
+            ts(T.jm[:], T.jw[:], -222.0, None, Op.add, None, "jw", "jm")
+            ts(T.j16[:], T.jw[:], 16.0, None, Op.add, None, "jw", "j16")
+            wrap(T.hw[:], T.gw[:, 640:864], C, "g_prev", "hw")
+        tt(T.hb[:, 16:240], T.fb[:].indirect(T.nx16[:]), T.f2[:], Op.is_gt, "fb f2 nx16", "hb")
+        if t == 0:
+            ts(T.pvf[:], T.hw[:, 15:C:16], T.sc[:], 2.0, Op.mult, Op.mult, "hw sc", "pvf")
+            ts(T.f3[:], T.fi[:], 320.0, None, Op.mult, None, "fi", "f3")
+            tt(T.dp[:], T.pvf[:], T.j16[:], Op.subtract, "pvf j16", "dp")
+            scan(T.zb[:, 16:240], T.hb[:, 16:240], T.hb[:, 15:239], 0.0, Op.add, Op.add, "hb hb_pad", "zb")
+            tt(T.dq[:], T.j16[:], T.dp[:], Op.subtract, "dp j16", "dq")
+            tt(T.s1[:], T.fi[:], T.dp[:], Op.mult, "fi dp", "s1")
+            tt(T.fj[:], T.f3[:], T.jm[:], Op.add, "f3 jm", "fj")
+        else:
+            tt(T.s1[:], T.fi[:], T.dp[:], Op.mult, "fi dp", "s1")
+            ts(T.f3[:], T.fi[:], 320.0, None, Op.mult, None, "fi", "f3")
+            scan(T.zb[:, 16:240], T.hb[:, 16:240], T.hb[:, 15:239], 0.0, Op.add, Op.add, "hb hb_pad", "zb")
+        tt(T.s2[:], T.s1[:], T.dq[:], Op.add, "s1 dq", "s2")
+        if t > 0:
+            tt(T.fj[:], T.f3[:], T.jm[:], Op.add, "f3 jm", "fj")
         if t == 1:
-            quant(T.qv[:], T.sv[:], T.vt[:], ["vt"], ["qv"])
-        wrap(T.wr[:, C:2 * C], T.zp[:], C, ["zp"], ["w1"])
-        ts(T.zi[:], T.wr[:, 15:3 * C:16], T.sc[:], None, Op.mult, None, ["w0", "w1", "w2", "sc"], ["zi"])
-        ts(T.od[:], T.zi[:, 0:28], 1, None, Op.bitwise_and, None, ["zi"], ["od"])
-        tt(T.tq[:], T.zi[:, 0:28], T.od[:], Op.mult, ["zi", "od"], ["tq"])
-        tt(T.qq[:], T.tq[:, 0:14], T.tq[:, 14:28], Op.add, ["tq"], ["qq"])
-        ts(T.zf[:], T.qq[:], 0.0, 320.0, Op.is_equal, Op.mult, ["qq"], ["zf"])
-        tt(T.kk[:], T.qq[:], T.zi[:, 28:42], Op.add, ["qq", "zi"], ["kk"])
-        ts(T.thr[:], T.nin[:, 8 * t + 7:8 * t + 8], float(K), 2.0, Op.min, Op.mult, ["nin%d" % t], ["thr"])
-        tt(T.y1[:], T.zf[:], T.zi[:, 28:42], Op.mult, ["zf", "zi"], ["y1"])
-        ts(T.pn[:], T.qq[:], T.thr[:], -1000.0, Op.is_gt, Op.mult, ["qq", "thr"], ["pn"])
-        tt(T.y2[:], T.y1[:], T.jm[:], Op.add, ["y1", "jm"], ["y2"])
-        tt(T.x1[:], T.pn[:], T.kk[:], Op.add, ["pn", "kk"], ["x1"])
-        tt(T.l1[:], T.y2[:], T.x1[:], Op.max, ["y2", "x1"], ["l1"])
-        ts(T.l16[:], T.l1[:], 222.0, None, Op.add, None, ["l1"], ["l16"])
+            quant(T.qv[:], T.sv[:], T.vt[:], "vt", "qv")
+        cp("v", T.sel[:], T.s2[:], "s2", "sel")
+        cp("v", T.zp[:], T.zb[:].indirect(T.sel[:]), "zb sel", "zp")
+        wrap(T.wz[:], T.zp[:], C, "zp", "wz")
+        ts(T.thr[:], T.nin[:, 8 * t + 7:8 * t + 8], float(K), 2.0, Op.min, Op.mult, "nin%d" % t, "thr")
+        ts(T.zi[:], T.wz[:, 15:C:16], T.sc[:], None, Op.mult, None, "wz sc", "zi")
+        ts(T.od[:], T.zi[:], 1, None, Op.bitwise_and, None, "zi", "od")
+        ts(T.pn[:], T.zi[:], T.thr[:], -1000.0, Op.is_gt, Op.mult, "zi thr", "pn")
+        tt(T.qq[:], T.zi[:], T.od[:], Op.mult, "zi od", "qq")
+        tt(T.t1[:], T.f3[:], T.od[:], Op.mult, "f3 od", "t1")
+        tt(T.fp[:], T.fi[:], T.pn[:], Op.add, "fi pn", "fp")
+        tt(T.y1[:], T.fj[:], T.t1[:], Op.subtract, "fj t1", "y1")
+        tt(T.x1[:], T.qq[:], T.fp[:], Op.add, "qq fp", "x1")
+        tt(T.l1[:], T.y1[:], T.x1[:], Op.max, "y1 x1", "l1")
+        ts(T.l16[:], T.l1[:], 222.0, None, Op.add, None, "l1", "l16")
+        cp("s", T.h0[:], T.gw[:].indirect(T.l16[:]), "l16 g_own g_slot g_next g_prev", "h0")
 
         for b in range(4):
             mm(T.pd[:, 512 * b:512 * b + 128], T.qw[:, 128 * b:128 * b + 128], T.sw[:, 128 * b:128 * b + 128],
                T.qx[:, lo - 32:lo + 2 * K], T.sx[:, lo - 32:lo + 2 * K],
-               ["qw", "sw", "arr%d" % t, "qx" if t == 0 else "arr%d" % (t - 1)], ["p:d%d" % b])
+               "qw sw arr%d " % t + ("qx" if t == 0 else "arr%d" % (t - 1)), "p:d%d" % b)
+        h0op = ops.pop(-5)
         for b in range(4):
             o, i = T.ht[:, b:384:4], T.pd[:, 512 * b + 32:512 * b + 128]
             if b % 2 == 0:
-                op("s", lambda o=o, i=i: S.activation(o, i, Act.Copy, scale=0.03125), ["p:d%d" % b], ["H%d" % b])
+                op("s", lambda o=o, i=i: S.activation(o, i, Act.Copy, scale=0.03125), "p:d%d" % b, "H%d" % b)
             else:
-                ts(o, i, 0.03125, None, Op.mult, None, ["p:d%d" % b], ["H%d" % b])
-        quant(T.qh[:], T.sh[:], T.ht[:], ["ht_pad", "H0", "H1", "H2", "H3"], ["qh"])
-        mm(T.pp[:, 0:128], T.qur[:], T.sur[:], T.qh[:], T.sh[:], ["qur", "sur", "qh"], ["p:p"])
-        cp("s", T.h0[:], T.gw[:].indirect(T.l16[:]), ["l16", "g_own", "g_slot", "g_next", "g_end", "g_prev"], ["h0"])
+                ts(o, i, 0.03125, None, Op.mult, None, "p:d%d" % b, "H%d" % b)
+        quant(T.qh[:], T.sh[:], T.ht[:], "ht_pad H0 H1 H2 H3", "qh")
+        mm(T.pp[:, 0:128], T.qur[:], T.sur[:], T.qh[:], T.sh[:], "qur sur qh", "p:p")
+        ops.append(h0op)
         for b in range(4):
-            cp("s", T.tw[:, PL * b + 256:PL * b + PL:2], T.ht[:, b:384:4], ["H%d" % b], ["TH%d" % b])
-        cp("v", T.pa[:], T.pp[:, 0:2 * K:2], ["p:p"], ["pa"])
-        tt(T.fw[:, C:320:2], T.pp[:, 1:2 * K:2], T.pa[:], Op.is_gt, ["p:p", "pa", "fw"], ["gt"])
-        tt(T.fw[:, C + 1:320:2], T.pp[:, 1:2 * K:2], T.pa[:], Op.is_le, ["p:p", "pa", "fw"], ["le"])
-        tt(T.hv[:], T.fw[:].indirect(T.l16[:]), T.h0[:], Op.add, ["gt", "le", "fw", "l16", "h0"], ["hv"])
-        wrap(T.hw[:], T.hv[:], C, ["hv"], ["hw"])
-        ts(T.lx[:], T.hw[:, 15:C:16], T.sc[:], 2.0, Op.mult, Op.mult, ["hw", "sc"], ["lx"])
+            cp("s", T.tw[:, PL * b + 256:PL * b + PL:2], T.ht[:, b:384:4], "H%d" % b, "TH%d" % b)
+        cp("v", T.pa[:], T.pp[:, 0:2 * K:2], "p:p", "pa")
+        tt(T.fw[:, C:320:2], T.pp[:, 1:2 * K:2], T.pa[:], Op.is_gt, "p:p pa fw", "gt")
+        tt(T.fw[:, C + 1:320:2], T.pp[:, 1:2 * K:2], T.pa[:], Op.is_le, "p:p pa fw", "le")
+        tt(T.hv[:], T.fw[:].indirect(T.l16[:]), T.h0[:], Op.add, "gt le fw l16 h0", "hv")
+        wrap(T.hw[:], T.hv[:], C, "hv", "hw")
+        ts(T.lx[:], T.hw[:, 15:C:16], T.sc[:], 2.0, Op.mult, Op.mult, "hw sc", "lx")
         for b in range(4):
             cp("vs"[b % 2], T.xt[:, b:4 * C:4], T.tw[:, PL * b:PL * b + PL].indirect(T.lx[:]),
-               ["lx", "T%d" % b, "TH%d" % b, "tw_zero"], ["X%d" % b])
-        xkeys = ["X0", "X1", "X2", "X3"]
+               "lx T%d TH%d tw_zero" % (b, b), "X%d" % b)
+        xkeys = "X0 X1 X2 X3"
 
-    cp("s", T.ots[:], T.rt[:].indirect(T.lx[:]), ["rt", "rt2", "lx"], ["ots"])
-    quant(T.qx[:, 0:C], T.sx[:, 0:C], T.xt[:], xkeys, ["qx"])
-    mm(T.ps[:, 0:C], T.qv[:], T.sv[:], T.qx[:, 0:C], T.sx[:, 0:C], ["qv", "qx"], ["p:s"])
-    cp("v", T.ys[:], T.ps[:, 0:C], ["p:s"], ["ys"])
-    dma("y", T.oc[:], T.qx[:, 0:C].bitcast(dt.uint8), ["qx"], [], "doc")
-    dma("s", T.ot[:], T.ots[0:128:16, :], ["ots"], [], "dot")
+    cp("s", T.ots[:], T.rt[:].indirect(T.lx[:]), "rt rt2 lx", "ots")
+    quant(T.qx[:, 0:C], T.sx[:, 0:C], T.xt[:], xkeys, "qx")
+    mm(T.ps[:, 0:C], T.qv[:], T.sv[:], T.qx[:, 0:C], T.sx[:, 0:C], "qv qx", "p:s")
+    cp("v", T.ys[:], T.ps[:, 0:C], "p:s", "ys")
+    dma("y", T.oc[:], T.qx[:, 0:C].bitcast(dt.uint8), "qx", "", "doc")
+    dma("s", T.ot[:], T.ots[0:128:16, :], "ots", "", "dot")
     for k in range(4):
-        dma("ys"[k % 2], T.osc[4 * k:4 * k + 4, :], T.sx[32 * k:32 * k + 4, 0:C], ["qx"], [], "ds%d" % k)
-    dma("y", T.y[:], T.ys[:], ["ys"], [], "dy")
+        dma("ys"[k % 2], T.osc[4 * k:4 * k + 4, :], T.sx[32 * k:32 * k + 4, 0:C], "qx", "", "ds%d" % k)
+    dma("y", T.y[:], T.ys[:], "ys", "", "dy")
     _emit(g, T, ops, sent[0])

@@ -164,6 +164,8 @@ def rank_program(g, core, T, topo):
         quant(T.qe[:, 128 * b:128 * b + 128], T.se[:, 128 * b:128 * b + 128], T.ez[:, 3 - b:515 - b], "ez", "qe%d" % b)
         if b == 0:
             tt(T.k16[:], T.k1[:], T.k2[:], Op.max, "k1 k2", "k16")
+    ts(T.jm[:], T.jw[:], -222.0, None, Op.add, None, "jw", "jm")
+    ts(T.j16[:], T.jw[:], 16.0, None, Op.add, None, "jw", "j16")
     op("s", lambda: S.activation(T.gw[:, 0:C], T.rt[:, 16:240], Act.Identity, bias=8.0, scale=0.5), "rt", "g_own")
     cp("s", T.kt[:], T.k16[:].indirect(T.pm16[:]), "k16 pm16", "kt")
 
@@ -177,11 +179,18 @@ def rank_program(g, core, T, topo):
     def tcopy(q, b):
         cp(q, T.tw[:, PL * b + 16:PL * b + 240], T.pd[:, 512 * b:512 * b + C], "p:d%d" % b, "T%d" % b)
 
+    def apick(b):
+        cp("v", T.at[:, b:384:8], T.tw[:, PL * b:PL * b + 256].indirect(T.la[:, 0:3]), "la T%d tw_zero" % b, "Aa%d" % b)
+
     xkeys = "x0"
     for t in range(R):
         op(None, None, "", "nin%d" % t, ("cnt%d" % t, ne_in))
         op(None, None, "", "arr%d" % t, ("arr%d" % t, 2 * ne_in))
         quant(T.qx[:, 0:C], T.sx[:, 0:C], (T.x0 if t == 0 else T.xt)[:], xkeys, "qx")
+        if t == 0:
+            op("v", lambda: V.tensor_copy(T.gw[:, 640:864].indirect(T.nx16[:]), T.gw[:, 0:C]), "g_own nx16", "g_prev")
+        if t == 1:
+            quant(T.qv[:], T.sv[:], T.vt[:], "vt", "qv")
         mm(T.ps[:, 0:C], T.qur[:], T.sur[:], T.qx[:, 0:C], T.sx[:, 0:C], "qur sur qx", "p:s")
         mm(T.pp[:, 0:C], T.qur[:], T.sur[:], T.qx[:, 0:C], T.sx[:, 0:C], "qur sur qx", "p:p")
         for b in range(4):
@@ -192,56 +201,49 @@ def rank_program(g, core, T, topo):
         tcopy("v", 0)
         tcopy("s", 2)
         tcopy("s", 3)
+        cp("v", T.f2[:], T.fb[:], "fb", "f2")
         tt(T.mb[:], T.fb[:].indirect(T.nx16[:]), T.sg[:], Op.is_le, "fb sg nx16", "mb")
         tcopy("v", 1)
         for b in (2, 3, 0, 1):
             cp("s", T.tn[:, 256 * b + 16:256 * b + 240], T.tw[:, PL * b:PL * b + 256].indirect(T.nxp[:]), "nxp tw_zero T%d" % b, "N%d" % b)
         for r in range(3):
             scan(T.ub[:, C * r:C * r + C], T.mb[:], T.one[:], T.nk[:, r:r + 1], Op.add, Op.min, "mb one nk", "u%d" % r)
+        if t == 0:
+            wrap(T.hw[:], T.gw[:, 640:864], C, "g_prev", "hw")
         for r in range(3):
             scan(T.cn[:, C * r:C * r + C], T.ub[:, C * r:C * r + C], T.dk[:], 240.0, Op.mult, Op.max, "dk u%d" % r, "cn%d" % r)
         cc, ck = T.cb[:, C * t:C * t + C], "c%d" % t
         scan(cc, T.mb[:], T.mb[:], 0.0, Op.add, Op.max, "mb", ck)
+        if t == 0:
+            ts(T.pvf[:], T.hw[:, 15:C:16], T.sc[:], 2.0, Op.mult, Op.mult, "hw sc", "pvf")
         send(T.nin[:, 8 * t:8 * t + 8], T.cb[:, C * t + C - 8:C * t + C], "cnt%d" % t, ck)
         ts(T.la[:, 0:3], T.cn[:, C - 1:3 * C:C], -1.0, 256.0, Op.mult, Op.add, "cn0 cn1 cn2", "la")
         wrap(T.wf[:], T.fb[:], C, "fb", "wf")
-        for b in range(4):
-            cp("v", T.at[:, b:384:8], T.tw[:, PL * b:PL * b + 256].indirect(T.la[:, 0:3]), "la T%d tw_zero" % b, "Aa%d" % b)
+        if t == 0:
+            tt(T.dp[:], T.pvf[:], T.j16[:], Op.subtract, "pvf j16", "dp")
         for b in (2, 3, 0, 1):
             cp("s", T.at[:, 4 + b:384:8], T.tn[:, 256 * b:256 * b + 256].indirect(T.la[:, 0:3]), "la N%d tn_zero" % b, "Ab%d" % b)
-        cp("v", T.f2[:], T.fb[:], "fb", "f2")
+        apick(0)
+        apick(1)
         ts(T.fi[:], T.wf[:, 15:C:16], T.sc[:], None, Op.mult, None, "wf sc", "fi")
+        apick(2)
+        apick(3)
+        if t == 0:
+            tt(T.dq[:], T.j16[:], T.dp[:], Op.subtract, "dp j16", "dq")
+        tt(T.s1[:], T.fi[:], T.dp[:], Op.mult, "fi dp", "s1")
+        tt(T.hb[:, 16:240], T.fb[:].indirect(T.nx16[:]), T.f2[:], Op.is_gt, "fb f2 nx16", "hb")
+        tt(T.s2[:], T.s1[:], T.dq[:], Op.add, "s1 dq", "s2")
         quant(T.qa[:, 128 * t:128 * t + 128], T.sa[:, 128 * t:128 * t + 128], T.at[:],
               "at_pad Aa0 Aa1 Aa2 Aa3 Ab0 Ab1 Ab2 Ab3", "qa%d" % t)
         lo = C + 2 * K * t
         send(T.qx[:, lo:lo + 2 * K].bitcast(dt.uint8), T.qa[:, 128 * t:128 * t + 2 * K].bitcast(dt.uint8), "arr%d" % t, "qa%d" % t)
         send(T.sx[:, lo:lo + 2 * K], T.sa[:, 128 * t:128 * t + 2 * K], "arr%d" % t, "qa%d" % t)
 
-        if t == 0:
-            op("v", lambda: V.tensor_copy(T.gw[:, 640:864].indirect(T.nx16[:]), T.gw[:, 0:C]), "g_own nx16", "g_prev")
-            ts(T.jm[:], T.jw[:], -222.0, None, Op.add, None, "jw", "jm")
-            ts(T.j16[:], T.jw[:], 16.0, None, Op.add, None, "jw", "j16")
-            wrap(T.hw[:], T.gw[:, 640:864], C, "g_prev", "hw")
-        tt(T.hb[:, 16:240], T.fb[:].indirect(T.nx16[:]), T.f2[:], Op.is_gt, "fb f2 nx16", "hb")
-        if t == 0:
-            ts(T.pvf[:], T.hw[:, 15:C:16], T.sc[:], 2.0, Op.mult, Op.mult, "hw sc", "pvf")
-            ts(T.f3[:], T.fi[:], 320.0, None, Op.mult, None, "fi", "f3")
-            tt(T.dp[:], T.pvf[:], T.j16[:], Op.subtract, "pvf j16", "dp")
-            scan(T.zb[:, 16:240], T.hb[:, 16:240], T.hb[:, 15:239], 0.0, Op.add, Op.add, "hb hb_pad", "zb")
-            tt(T.dq[:], T.j16[:], T.dp[:], Op.subtract, "dp j16", "dq")
-            tt(T.s1[:], T.fi[:], T.dp[:], Op.mult, "fi dp", "s1")
-            tt(T.fj[:], T.f3[:], T.jm[:], Op.add, "f3 jm", "fj")
-        else:
-            tt(T.s1[:], T.fi[:], T.dp[:], Op.mult, "fi dp", "s1")
-            ts(T.f3[:], T.fi[:], 320.0, None, Op.mult, None, "fi", "f3")
-            scan(T.zb[:, 16:240], T.hb[:, 16:240], T.hb[:, 15:239], 0.0, Op.add, Op.add, "hb hb_pad", "zb")
-        tt(T.s2[:], T.s1[:], T.dq[:], Op.add, "s1 dq", "s2")
-        if t > 0:
-            tt(T.fj[:], T.f3[:], T.jm[:], Op.add, "f3 jm", "fj")
-        if t == 1:
-            quant(T.qv[:], T.sv[:], T.vt[:], "vt", "qv")
+        scan(T.zb[:, 16:240], T.hb[:, 16:240], T.hb[:, 15:239], 0.0, Op.add, Op.add, "hb hb_pad", "zb")
         cp("v", T.sel[:], T.s2[:], "s2", "sel")
+        ts(T.f3[:], T.fi[:], 320.0, None, Op.mult, None, "fi", "f3")
         cp("v", T.zp[:], T.zb[:].indirect(T.sel[:]), "zb sel", "zp")
+        tt(T.fj[:], T.f3[:], T.jm[:], Op.add, "f3 jm", "fj")
         wrap(T.wz[:], T.zp[:], C, "zp", "wz")
         ts(T.thr[:], T.nin[:, 8 * t + 7:8 * t + 8], float(K), 2.0, Op.min, Op.mult, "nin%d" % t, "thr")
         ts(T.zi[:], T.wz[:, 15:C:16], T.sc[:], None, Op.mult, None, "wz sc", "zi")
@@ -252,26 +254,25 @@ def rank_program(g, core, T, topo):
         tt(T.fp[:], T.fi[:], T.pn[:], Op.add, "fi pn", "fp")
         tt(T.y1[:], T.fj[:], T.t1[:], Op.subtract, "fj t1", "y1")
         tt(T.x1[:], T.qq[:], T.fp[:], Op.add, "qq fp", "x1")
-        tt(T.l1[:], T.y1[:], T.x1[:], Op.max, "y1 x1", "l1")
-        ts(T.l16[:], T.l1[:], 222.0, None, Op.add, None, "l1", "l16")
-        cp("s", T.h0[:], T.gw[:].indirect(T.l16[:]), "l16 g_own g_slot g_next g_prev", "h0")
 
         for b in range(4):
             mm(T.pd[:, 512 * b:512 * b + 128], T.qw[:, 128 * b:128 * b + 128], T.sw[:, 128 * b:128 * b + 128],
                T.qx[:, lo - 32:lo + 2 * K], T.sx[:, lo - 32:lo + 2 * K],
                "qw sw arr%d " % t + ("qx" if t == 0 else "arr%d" % (t - 1)), "p:d%d" % b)
-        h0op = ops.pop(-5)
         for b in range(4):
             o, i = T.ht[:, b:384:4], T.pd[:, 512 * b + 32:512 * b + 128]
             if b % 2 == 0:
                 op("s", lambda o=o, i=i: S.activation(o, i, Act.Copy, scale=0.03125), "p:d%d" % b, "H%d" % b)
             else:
                 ts(o, i, 0.03125, None, Op.mult, None, "p:d%d" % b, "H%d" % b)
+        tt(T.l1[:], T.y1[:], T.x1[:], Op.max, "y1 x1", "l1")
         quant(T.qh[:], T.sh[:], T.ht[:], "ht_pad H0 H1 H2 H3", "qh")
+        ts(T.l16[:], T.l1[:], 222.0, None, Op.add, None, "l1", "l16")
         mm(T.pp[:, 0:128], T.qur[:], T.sur[:], T.qh[:], T.sh[:], "qur sur qh", "p:p")
-        ops.append(h0op)
         for b in range(4):
             cp("s", T.tw[:, PL * b + 256:PL * b + PL:2], T.ht[:, b:384:4], "H%d" % b, "TH%d" % b)
+            if b == 1:
+                cp("s", T.h0[:], T.gw[:].indirect(T.l16[:]), "l16 g_own g_slot g_next g_prev", "h0")
         cp("v", T.pa[:], T.pp[:, 0:2 * K:2], "p:p", "pa")
         tt(T.fw[:, C:320:2], T.pp[:, 1:2 * K:2], T.pa[:], Op.is_gt, "p:p pa fw", "gt")
         tt(T.fw[:, C + 1:320:2], T.pp[:, 1:2 * K:2], T.pa[:], Op.is_le, "p:p pa fw", "le")

@@ -3,21 +3,38 @@ from concourse.mybir import dt, AluOpType as Op, ActivationFunctionType as Act
 C, K, R = 224, 48, 3
 PL = 448
 BIG = 65536.0
+HS = 0.03125
+STEP = 512.0
+ROUND = 1.5 * 2.0 ** 23 * STEP
 _B = {
-    "bfloat16": dict(x0=896, ut=512, vt=512, ez=528, xt=896, tw=4 * PL, tn=1024, at=512, ht=512, fb=C, f2=C, sg=C, mb=C, cb=R * C,
-                     ub=3 * C, cn=3 * C, one=C, dk=C, nin=8 * R, hb=240, zb=240, zp=C, wf=C, wz=C, gw=864, fw=864, h0=C, hv=C,
-                     hw=C, kt=C, k16=16),
-    "float32": dict(thr=1, qq=14, fi=14, f3=14, fj=14, s1=14, s2=14, dp=14, dq=14, pvf=14, t1=14, fp=14, y1=14, pn=14, x1=14, l1=14,
-                    pa=K, rt=PL, k1=16, k2=16, pcol=1, jw=14, jm=14, j16=14, nk=4, sc=1, ys=C, ots=C),
-    "int32": dict(nxi=16, zi=14, od=14, pi=14, c16=14, pmi=14),
-    "uint16": dict(la=4, l16=14, lx=14, ul=8, pm16=14, nx16=14, nxp=14, sel=14),
-    "float8_e4m3fn_x4": dict(qu=128, qur=128, qv=128, qw=512, qe=512, qx=512, qa=384, qh=128),
-    "uint8": dict(su=128, sur=128, sv=128, sw=512, se=512, sx=512, sa=384, sh=128),
+    "bfloat16": dict(x0=896, ut=512, vt=512, ez=528, df=128, xt=1024, tw=4 * PL, tp=1024, at=512, ht=512, fb=C, sg=C, mb=C,
+                     ub=3 * C, jk=C, one=C, hb=C, c2=C, eb=240, zp=C, wo=3 * C, gw=864, fw=864, h0=C, hv=C, hw=C, hp=C,
+                     kt=C, k16=16, hs=2 * K),
+    "float32": dict(w3=42, z=14, thr=1, nz=14, t1=14, y1=14, pn=14, x2=14, x1=14, l1=14, cn=3 * C, wt=C + 8, ramp=C, hi=3, cnt=2,
+                    rt=PL, k1=16, k2=16, jw=14, jm=14, nk=4, sc=1, ys=C, ots=C),
+    "int32": dict(nxi=16, pi=14, c16=14, pmi=14),
+    "uint16": dict(lo=8 * R, li=8 * R, l16=14, lx=14, ul=8, pm16=14, nx16=14, pv16=14),
+    "float8_e4m3fn_x4": dict(qu=128, qur=128, qv=128, qw=512, qe=512, qx=256 * (R + 1), qy=R * C, qa=128, qh=128 + K),
+    "uint8": dict(su=128, sur=128, sv=128, sw=512, se=512, sx=256 * (R + 1), sy=R * C, sa=128, sh=128 + K),
 }
 SCRATCH = {k: ("sbuf", [128, n], d) for d, b in _B.items() for k, n in b.items()}
-SCRATCH.update({k: ("psum", [128, n], "float32") for k, n in (("ps", 512), ("pd", 2048), ("pp", 512))})
-DMAS = ["du", "dn", "dx", "dwc", "dws", "dv", "doc", "ds0", "ds1", "ds2", "ds3", "dy", "dot"]
-SEMAPHORES = ["cv", "cs", "ct", "cg", "sent"] + DMAS + ["arr%d" % t for t in range(R)] + ["cnt%d" % t for t in range(R)]
+SCRATCH.update({k: ("psum", [128, 2048 if k == "pd" else 512], "float32") for k in ("ps", "pp", "pe", "pf", "pd")})
+DMAS = ["dx", "du", "dn", "dwc", "dws", "dv", "doc", "ds0", "ds1", "ds2", "ds3", "dy", "dot"]
+SEMAPHORES = ["cv", "cs", "ct", "cg", "sent"] + DMAS + ["%s%d" % (k, t) for k in ("arr", "lst") for t in range(R)]
+
+CUTS = ((0, 8), (8, 12), (12, 14))
+FIRST = """dx du dn dws dwc df pi c16 rt xt_pad rt2 ht_pad g_slot wt_end
+    one ez0 ez pmi qe3 jw qe2 sc qe0 k1 qe1 k2 ul k16 qx pm16 qu nx16 qur sendq sends tp_zero cnt_pad fw at_pad
+    g_own sur ramp g_prev mD2 mD1 mD3 mS mD0 mS2 fb wt sg nk T1 T0 g_next T3 hs1 kt hs0 mb T2 cnt jm
+    hb u2 u0 u1 cn0 cn2 cn1 wf hp qh_pad hi c2 ln2 eb pv16 ln0 lc ln1 la we zp sendl wq
+    mN2 mN1 mN0 mN3 N2 N0 N3 w3 N1 A2 A0 thr z A3 A1 qa x2 pn dv nz
+    mW1 x1 t1 H1 mW0 mW2 mW3 H0 H2 y1 H3 l1 qh l16 mP TH1 TH0 TH3 TH2 h0
+    down up hv0 hv1 hw0 hv2 hw1 lx0 hw2 lx1 lx2 X0 Z0 X2 Z2 X3 X1 Z1 Z3"""
+LATER = """qx mS mS2 sg qz sendq sends mZ2 mZ mD2 mD3 mD0 mD1 sg2 fb fb2 mb cnt T3 T2 T1 T0
+    hb u2 u1 u0 lc cn1 cn0 cn2 c2 hi eb la ln1 ln0 ln2 sendl
+    mN1 qv wf we N1 zp wq mN3 mN0 mN2 N3 N0 N2 A1 A3 w3 A0 z A2 thr nz qa x2 pn t1 x1
+    mW0 mW2 mW1 mW3 y1 H0 H2 H1 H3 l1 qh l16 mP TH0 TH2 TH1 h0 TH3
+    up down hv0 hv1 hw0 hv2 hw1 lx0 lx1 hw2 X0 lx2 X2 Z0 Z2 X3 X1 Z1 Z3"""
 
 
 def _emit(g, T, ops, sent):
@@ -79,11 +96,15 @@ def rank_program(g, core, T, topo):
     mask = topo.mask(core, nxt)
     ne_out, ne_in = len(topo.engines(core, nxt)), len(topo.engines(prv, core))
     V, S, PE = g.vector, g.scalar, g.tensor
-    ops = []
-    sent = [0]
+    ops, steps = [], {}
 
-    def op(q, fn, r, w, kind=None):
-        ops.append((q, fn, r, w, kind))
+    def op(q, fn, r, w, kind=None, name=None):
+        steps[name or w.split()[0]] = (q, fn, r, w, kind)
+
+    def issue(order):
+        names = [n for n in order if n in steps]
+        assert len(names) == len(steps)
+        ops.extend(steps.pop(n) for n in names)
 
     def ts(out, in0, a, b, o0, o1, r, w):
         if o1 is None:
@@ -94,28 +115,31 @@ def rank_program(g, core, T, topo):
     def tt(out, in0, in1, o, r, w):
         op("v", lambda: V.tensor_tensor(out, in0, in1, o), r, w)
 
+    def act(out, in_, func, r, w, **k):
+        op("s", lambda: S.activation(out, in_, func, **k), r, w)
+
     def cp(q, out, in_, r, w):
         if q == "v":
             op("v", lambda: V.tensor_copy(out, in_), r, w)
         else:
-            op("s", lambda: S.activation(out, in_, Act.Copy), r, w)
+            act(out, in_, Act.Copy, r, w)
 
     def scan(out, d0, d1, init, o0, o1, r, w):
         op("v", lambda: V.tensor_tensor_scan(out, d0, d1, init, o0, o1), r, w)
 
-    def wrap(out, in_, n, r, w):
-        scan(out, T.kt[:, 0:n], in_, 0.0, Op.mult, Op.max, r + " kt", w)
+    def wrap(out, in_, r, w):
+        scan(out, T.kt[:], in_, 0.0, Op.mult, Op.max, r + " kt", w)
 
-    def quant(q, s, in_, r, w):
-        op("v", lambda: V.quantize_mx(q, s, in_), r, w)
+    def quant(q, s, in_, r, w, name=None):
+        op("v", lambda: V.quantize_mx(q, s, in_), r, w, None, name)
 
-    def mm(out, a, sa, b, sb, r, w):
-        op("t", lambda: PE.matmul_mx(out, a, sa, b, sb, True, True), r, w)
+    def mm(out, a, sa, b, sb, r, w, name):
+        op("t", lambda: PE.matmul_mx(out, a, sa, b, sb, True, True), r, w, None, name)
 
-    def fill(ap, val, w):
-        op("v", lambda: V.memset(ap, val), "", w)
+    def fill(ap, val, w, name=None):
+        op("v", lambda: V.memset(ap, val), "", w, None, name)
 
-    def iota(out, pattern, base, mult, w, small=False):
+    def iota(out, pattern, base, mult, w, small=True):
         if small:
             op("g", lambda: g.iota(out, pattern, base, mult, allow_small_or_imprecise_dtypes=True), "", w)
         else:
@@ -123,174 +147,170 @@ def rank_program(g, core, T, topo):
 
     def dma(q, out, in_, r, w, sem):
         e = g.sync if q == "y" else S
-        op(q, lambda: e.dma_start(out, in_), r, w, sem)
+        op(q, lambda: e.dma_start(out, in_), r, w, sem, sem)
 
-    def send(out, in_, sem, r):
-        sent[0] += ne_out
-        op("g", lambda: g.remote_dma(out, in_, T.sem[sem], T.sem.sent, pid, rid, mask), r, "", "remote")
+    def send(out, in_, sem, r, name):
+        op("g", lambda: g.remote_dma(out, in_, T.sem[sem], T.sem.sent, pid, rid, mask), r, "", "remote", name)
 
-    dma("y", T.ut[:], T.u[:], "", "ut", "du")
-    dma("s", T.x0[:], T.x[:], "", "x0", "dx")
-    dma("y", T.nxi[:, 0:14], T.nx[:], "", "nxi", "dn")
-    dma("y", T.qw[:].bitcast(dt.uint8), T.wc[:], "x0", "qw", "dwc")
-    dma("y", T.sw[:], T.ws[:], "", "sw", "dws")
-    dma("y", T.vt[:], T.v[:], "", "vt", "dv")
+    def unpack(q, s, key, name):
+        for b in range(4):
+            mm(T.pd[:, 512 * b:512 * b + C], T.qe[:, 128 * b:128 * b + 128], T.se[:, 128 * b:128 * b + 128], q, s,
+               "qe%d %s" % (b, key), "p:d%d" % b, name + str(b))
 
-    iota(T.pi[:], [[0, 14]], 0, 1, "pi")
-    iota(T.c16[:], [[16, 14]], 0, 0, "c16")
-    iota(T.pcol[:], [[0, 1]], 0, 1, "pcol", True)
-    iota(T.rt[:, 0:256], [[1, 256]], -16, 0, "rt", True)
-    iota(T.dk[:], [[-1, C]], 239, 0, "dk", True)
-    iota(T.gw[:, C:320], [[2, K], [0, 2]], 128, 0, "g_slot", True)
-    iota(T.rt[:, 256:PL], [[1, 2 * K], [0, 2]], C, 0, "rt2", True)
-    fill(T.ez[:], 0.0, "ez")
-    fill(T.fw[:], 0.0, "fw")
-    ts(T.pmi[:], T.pi[:], 15, None, Op.bitwise_and, None, "pi", "pmi")
-    cp("v", T.ul[:], T.c16[:, 0:8], "c16", "ul")
-    fill(T.at[:, 384:512], 0.0, "at_pad")
-    fill(T.ht[:, 384:512], 0.0, "ht_pad")
-    tt(T.jw[:], T.c16[:], T.pmi[:], Op.add, "c16 pmi", "jw")
-    cp("v", T.pm16[:], T.pmi[:], "pmi", "pm16")
-    fill(T.tw[:, 240:4 * PL:PL], 0.0, "tw_zero")
-    fill(T.tn[:, 240:1024:256], 0.0, "tn_zero")
-    fill(T.hb[:, 0:16], 0.0, "hb_pad")
+    def scores():
+        PE.matmul_mx(T.pp[:, 0:128], T.qur[:], T.sur[:], T.qh[:, 0:128], T.sh[:, 0:128], True, False)
+        return PE.matmul_mx(T.pp[:, 0:128], T.qur[:], T.sur[:], T.qh[:, K:K + 128], T.sh[:, K:K + 128], False, True)
+
+    dma("s", T.nxi[:, 0:14], T.nx[:], "", "nxi", "dn")
+    dma("y", T.x0[:], T.x[:], "", "x0", "dx")
+    dma("s", T.ut[:], T.u[:], "", "ut", "du")
+    dma("y", T.qw[:].bitcast(dt.uint8), T.wc[:], "x0 ut", "qw", "dwc")
+    dma("y", T.sw[:], T.ws[:], "x0 ut", "sw", "dws")
+    dma("y", T.vt[:], T.v[:], "qa", "vt", "dv")
+
+    hkeys = "ht_pad H0 H1 H2 H3"
+    iota(T.df[:], [[1, 128]], 0, -1, "df")
+    iota(T.pi[:], [[0, 14]], 0, 1, "pi", False)
+    iota(T.c16[:], [[16, 14]], 0, 0, "c16", False)
+    iota(T.rt[:, 0:256], [[1, 256]], -16, 0, "rt")
+    iota(T.rt[:, 256:PL], [[1, 2], [2, K], [0, 2]], C, 0, "rt2")
+    iota(T.gw[:, C:320], [[1, K], [K, 2]], 128, 0, "g_slot")
+    iota(T.wt[:, C:C + 1], [[0, 1]], int(STEP) * 16 + 240, 0, "wt_end")
+    for ap, n, key in ((T.tp[:, 240:1024:256], 4, "tp_zero"), (T.cnt[:, 0:1], 1, "cnt_pad"), (T.at[:, 384:512], 128, "at_pad"),
+                       (T.xt[:, 896:1024], 128, "xt_pad"), (T.ht[:], 512, hkeys), (T.fw[:], 864, "fw")):
+        iota(ap, [[0, n]], 0, 0, key)
+    fill(T.ez[:], 0.0, "ez", "ez0")
     fill(T.one[:], 1.0, "one")
-    ts(T.ez[:, 3:515:4], T.rt[:, 16:144], T.pcol[:], None, Op.is_equal, None, "rt pcol", "ez")
-    ts(T.k1[:], T.rt[:, 15:31], T.jw[:, 0:1], BIG, Op.is_equal, Op.mult, "rt jw", "k1")
-    ts(T.k2[:], T.rt[:, 16:32], T.jw[:, 0:1], None, Op.not_equal, None, "rt jw", "k2")
-    ts(T.sc[:], T.jw[:, 0:1], 15.0, 1.0 / BIG, Op.is_equal, Op.max, "jw", "sc")
-    ts(T.nk[:], T.jw[:, 0:4], -1.0, None, Op.mult, None, "jw", "nk")
+    ts(T.ez[:, 3:515:4], T.df[:], 0.0, None, Op.is_equal, None, "df", "ez")
     for b in range(4):
         quant(T.qe[:, 128 * b:128 * b + 128], T.se[:, 128 * b:128 * b + 128], T.ez[:, 3 - b:515 - b], "ez", "qe%d" % b)
-        if b == 0:
-            tt(T.k16[:], T.k1[:], T.k2[:], Op.max, "k1 k2", "k16")
-    ts(T.jm[:], T.jw[:], -222.0, None, Op.add, None, "jw", "jm")
-    ts(T.j16[:], T.jw[:], 16.0, None, Op.add, None, "jw", "j16")
-    op("s", lambda: S.activation(T.gw[:, 0:C], T.rt[:, 16:240], Act.Identity, bias=8.0, scale=0.5), "rt", "g_own")
+    ts(T.pmi[:], T.pi[:], 15, None, Op.bitwise_and, None, "pi", "pmi")
+    tt(T.jw[:], T.c16[:], T.pmi[:], Op.add, "c16 pmi", "jw")
+    cp("v", T.ul[:], T.c16[:, 0:8], "c16", "ul")
+    cp("v", T.pm16[:], T.pmi[:], "pmi", "pm16")
+    ts(T.k1[:], T.rt[:, 15:31], T.jw[:, 0:1], BIG, Op.is_equal, Op.mult, "rt jw", "k1")
+    ts(T.k2[:], T.rt[:, 16:32], T.jw[:, 0:1], None, Op.not_equal, None, "rt jw", "k2")
+    tt(T.k16[:], T.k1[:], T.k2[:], Op.max, "k1 k2", "k16")
     cp("s", T.kt[:], T.k16[:].indirect(T.pm16[:]), "k16 pm16", "kt")
-
-    quant(T.qu[:], T.su[:], T.ut[:], "ut", "qu")
+    ts(T.sc[:], T.jw[:, 0:1], 15.0, 1.0 / BIG, Op.is_equal, Op.max, "jw", "sc")
+    act(T.nk[:], T.jw[:, 0:4], Act.Copy, "jw", "nk", scale=-1.0)
+    act(T.jm[:], T.jw[:], Act.Identity, "jw", "jm", bias=-221.0)
+    act(T.hs[:, 0:K], T.one[:, 0:K], Act.Copy, "one", "hs0", scale=-HS)
+    act(T.hs[:, K:2 * K], T.one[:, 0:K], Act.Copy, "one", "hs1", scale=HS)
+    quant(T.qh[:, K:K + 128], T.sh[:, K:K + 128], T.ht[:], hkeys, "qh_pad qh")
     cp("v", T.nx16[:], T.nxi[:, 0:14], "nxi", "nx16")
-    ts(T.nxp[:], T.nxi[:, 0:14], 16.0, None, Op.add, None, "nxi", "nxp")
+    act(T.gw[:, 0:C], T.rt[:, 16:240], Act.Identity, "rt", "g_own", bias=8.0, scale=0.5)
+    cp("s", T.gw[:, 320:544], T.gw[:, 0:C].indirect(T.nx16[:]), "g_own nx16", "g_next")
+    op("v", lambda: V.tensor_copy(T.gw[:, 640:864].indirect(T.nx16[:]), T.gw[:, 0:C]), "g_own nx16", "g_prev")
+    wrap(T.hp[:], T.gw[:, 640:864], "g_prev", "hp")
+    ts(T.pv16[:], T.hp[:, 15:C:16], T.sc[:], 2.0, Op.mult, Op.mult, "hp sc", "pv16")
+    act(T.ramp[:], T.rt[:, 16:240], Act.Identity, "rt", "ramp", bias=STEP * 240, scale=-STEP)
+    tt(T.wt[:, 0:C], T.rt[:, 32:256].indirect(T.nx16[:]), T.ramp[:], Op.add, "rt nx16 ramp", "wt")
+    quant(T.qu[:], T.su[:], T.ut[:], "ut", "qu")
     cp("v", T.qur[:].bitcast(dt.uint32), T.qu[:].bitcast(dt.uint32).indirect(T.ul[:]), "qu ul", "qur")
     cp("s", T.sur[:], T.su[:].indirect(T.ul[:]), "qu ul", "sur")
-    cp("s", T.gw[:, 320:544], T.gw[:, 0:C].indirect(T.nx16[:]), "g_own nx16", "g_next")
 
-    def tcopy(q, b):
-        cp(q, T.tw[:, PL * b + 16:PL * b + 240], T.pd[:, 512 * b:512 * b + C], "p:d%d" % b, "T%d" % b)
+    def halves(t):
+        a, b = [(T.qx[:, 256 * t + c:256 * t + c + 128], T.sx[:, 256 * t + c:256 * t + c + 128]) for c in (0, 128)]
+        quant(a[0], a[1], T.xt[:, 0:512], "X0 X1 X2 X3", "qx%d" % t, "qx")
+        quant(b[0], b[1], T.xt[:, 512:1024], "Z0 Z1 Z2 Z3 xt_pad", "qz%d" % t, "qz")
+        return a, b
 
-    def apick(b):
-        cp("v", T.at[:, b:384:8], T.tw[:, PL * b:PL * b + 256].indirect(T.la[:, 0:3]), "la T%d tw_zero" % b, "Aa%d" % b)
+    def signs(q, key, c, n, banks, names):
+        for (bank, pk), name in zip(banks, names[:2]):
+            mm(bank[:, 0:max(n, 128)], T.qur[:], T.sur[:], q[0], q[1], "qur sur " + key, pk, name)
+        ts(T.fb[:, c:c + n], banks[0][0][:, 0:n], 0.0, 1.0, Op.is_gt, Op.add, banks[0][1], names[2])
+        act(T.sg[:, c:c + n], banks[1][0][:, 0:n], Act.Sign, banks[1][1], names[3])
 
-    xkeys = "x0"
     for t in range(R):
-        op(None, None, "", "nin%d" % t, ("cnt%d" % t, ne_in))
-        op(None, None, "", "arr%d" % t, ("arr%d" % t, 2 * ne_in))
-        quant(T.qx[:, 0:C], T.sx[:, 0:C], (T.x0 if t == 0 else T.xt)[:], xkeys, "qx")
-        if t == 0:
-            op("v", lambda: V.tensor_copy(T.gw[:, 640:864].indirect(T.nx16[:]), T.gw[:, 0:C]), "g_own nx16", "g_prev")
+        qx, sx, qk = T.qx[:, 256 * t:256 * t + C], T.sx[:, 256 * t:256 * t + C], "qx%d qz%d" % (t, t)
+        qy, sy = T.qy[:, C * t:C * t + C], T.sy[:, C * t:C * t + C]
+        lo, arr, lst = 8 * t, "arr%d" % t, "lst%d" % t
+        ops.append((None, None, "", arr, (arr, 2 * ne_in)))
+        ops.append((None, None, "", lst, (lst, ne_in)))
         if t == 1:
             quant(T.qv[:], T.sv[:], T.vt[:], "vt", "qv")
-        mm(T.ps[:, 0:C], T.qur[:], T.sur[:], T.qx[:, 0:C], T.sx[:, 0:C], "qur sur qx", "p:s")
-        mm(T.pp[:, 0:C], T.qur[:], T.sur[:], T.qx[:, 0:C], T.sx[:, 0:C], "qur sur qx", "p:p")
+        front, back = ((T.ps, "p:s"), (T.pp, "p:p")), ((T.pe, "p:e"), (T.pf, "p:f"))
+        if t:
+            a, b = halves(t)
+            signs(a, "qx%d" % t, 0, 128, front, ("mS", "mS2", "fb", "sg"))
+            signs(b, "qz%d" % t, 128, C - 128, back, ("mZ", "mZ2", "fb2", "sg2"))
+        else:
+            quant(qx, sx, T.x0[:], "x0", qk, "qx")
+            signs((qx, sx), qk, 0, C, front, ("mS", "mS2", "fb fb2", "sg sg2"))
+        send(qy.bitcast(dt.uint8), qx.bitcast(dt.uint8), arr, qk, "sendq")
+        send(sy, sx, arr, qk, "sends")
+        unpack(qx, sx, qk, "mD")
         for b in range(4):
-            mm(T.pd[:, 512 * b:512 * b + C], T.qe[:, 128 * b:128 * b + 128], T.se[:, 128 * b:128 * b + 128],
-               T.qx[:, 0:C], T.sx[:, 0:C], "qe%d qx" % b, "p:d%d" % b)
-        ts(T.fb[:], T.ps[:, 0:C], 0.0, 1.0, Op.is_gt, Op.add, "p:s", "fb")
-        op("s", lambda: S.activation(T.sg[:], T.pp[:, 0:C], Act.Sign), "p:p", "sg")
-        tcopy("v", 0)
-        tcopy("s", 2)
-        tcopy("s", 3)
-        cp("v", T.f2[:], T.fb[:], "fb", "f2")
-        tt(T.mb[:], T.fb[:].indirect(T.nx16[:]), T.sg[:], Op.is_le, "fb sg nx16", "mb")
-        tcopy("v", 1)
-        for b in (2, 3, 0, 1):
-            cp("s", T.tn[:, 256 * b + 16:256 * b + 240], T.tw[:, PL * b:PL * b + 256].indirect(T.nxp[:]), "nxp tw_zero T%d" % b, "N%d" % b)
+            cp("s", T.tw[:, PL * b + 16:PL * b + 240], T.pd[:, 512 * b:512 * b + C], "p:d%d" % b, "T%d" % b)
+        tt(T.mb[:], T.fb[:].indirect(T.nx16[:]), T.sg[:], Op.is_le, "fb fb2 sg sg2 nx16", "mb")
+        act(T.jk[:], T.mb[:], Act.Identity, "mb", "cnt jk", scale=2.0, accum_out=T.cnt[:, 1:2])
+        ts(T.lo[:, lo:lo + 2], T.cnt[:], 240.0, None, Op.add, None, "cnt cnt_pad", "lc")
         for r in range(3):
-            scan(T.ub[:, C * r:C * r + C], T.mb[:], T.one[:], T.nk[:, r:r + 1], Op.add, Op.min, "mb one nk", "u%d" % r)
-        if t == 0:
-            wrap(T.hw[:], T.gw[:, 640:864], C, "g_prev", "hw")
-        for r in range(3):
-            scan(T.cn[:, C * r:C * r + C], T.ub[:, C * r:C * r + C], T.dk[:], 240.0, Op.mult, Op.max, "dk u%d" % r, "cn%d" % r)
-        cc, ck = T.cb[:, C * t:C * t + C], "c%d" % t
-        scan(cc, T.mb[:], T.mb[:], 0.0, Op.add, Op.max, "mb", ck)
-        if t == 0:
-            ts(T.pvf[:], T.hw[:, 15:C:16], T.sc[:], 2.0, Op.mult, Op.mult, "hw sc", "pvf")
-        send(T.nin[:, 8 * t:8 * t + 8], T.cb[:, C * t + C - 8:C * t + C], "cnt%d" % t, ck)
-        ts(T.la[:, 0:3], T.cn[:, C - 1:3 * C:C], -1.0, 256.0, Op.mult, Op.add, "cn0 cn1 cn2", "la")
-        wrap(T.wf[:], T.fb[:], C, "fb", "wf")
-        if t == 0:
-            tt(T.dp[:], T.pvf[:], T.j16[:], Op.subtract, "pvf j16", "dp")
-        for b in (2, 3, 0, 1):
-            cp("s", T.at[:, 4 + b:384:8], T.tn[:, 256 * b:256 * b + 256].indirect(T.la[:, 0:3]), "la N%d tn_zero" % b, "Ab%d" % b)
-        apick(0)
-        apick(1)
-        ts(T.fi[:], T.wf[:, 15:C:16], T.sc[:], None, Op.mult, None, "wf sc", "fi")
-        apick(2)
-        apick(3)
-        if t == 0:
-            tt(T.dq[:], T.j16[:], T.dp[:], Op.subtract, "dp j16", "dq")
-        tt(T.s1[:], T.fi[:], T.dp[:], Op.mult, "fi dp", "s1")
-        tt(T.hb[:, 16:240], T.fb[:].indirect(T.nx16[:]), T.f2[:], Op.is_gt, "fb f2 nx16", "hb")
-        tt(T.s2[:], T.s1[:], T.dq[:], Op.add, "s1 dq", "s2")
-        quant(T.qa[:, 128 * t:128 * t + 128], T.sa[:, 128 * t:128 * t + 128], T.at[:],
-              "at_pad Aa0 Aa1 Aa2 Aa3 Ab0 Ab1 Ab2 Ab3", "qa%d" % t)
-        lo = C + 2 * K * t
-        send(T.qx[:, lo:lo + 2 * K].bitcast(dt.uint8), T.qa[:, 128 * t:128 * t + 2 * K].bitcast(dt.uint8), "arr%d" % t, "qa%d" % t)
-        send(T.sx[:, lo:lo + 2 * K], T.sa[:, 128 * t:128 * t + 2 * K], "arr%d" % t, "qa%d" % t)
+            ub, last = T.ub[:, C * r:C * r + C], T.cn[:, C * r + C - 1:C * r + C]
+            scan(ub, T.mb[:], T.one[:], T.nk[:, r:r + 1], Op.add, Op.min, "mb one nk", "u%d" % r)
+            scan(T.cn[:, C * r:C * r + C], ub, T.wt[:, 1:C + 1], T.wt[:, 0:1], Op.mult, Op.max, "wt wt_end u%d" % r, "cn%d" % r)
+            ts(T.lo[:, lo + 5 + r:lo + 6 + r], last, T.hi[:, r:r + 1], None, Op.subtract, None, "cn%d hi" % r, "ln%d" % r)
+        ts(T.hi[:], T.cn[:, C - 1:3 * C:C], ROUND, ROUND, Op.add, Op.subtract, "cn0 cn1 cn2", "hi")
+        ts(T.lo[:, lo + 2:lo + 5], T.cn[:, C - 1:3 * C:C], -1.0 / STEP, 256.5, Op.mult, Op.add, "cn0 cn1 cn2", "la")
+        send(T.li[:, lo:lo + 8], T.lo[:, lo:lo + 8], lst, "lc la ln0 ln1 ln2", "sendl")
 
-        scan(T.zb[:, 16:240], T.hb[:, 16:240], T.hb[:, 15:239], 0.0, Op.add, Op.add, "hb hb_pad", "zb")
-        cp("v", T.sel[:], T.s2[:], "s2", "sel")
-        ts(T.f3[:], T.fi[:], 320.0, None, Op.mult, None, "fi", "f3")
-        cp("v", T.zp[:], T.zb[:].indirect(T.sel[:]), "zb sel", "zp")
-        tt(T.fj[:], T.f3[:], T.jm[:], Op.add, "f3 jm", "fj")
-        wrap(T.wz[:], T.zp[:], C, "zp", "wz")
-        ts(T.thr[:], T.nin[:, 8 * t + 7:8 * t + 8], float(K), 2.0, Op.min, Op.mult, "nin%d" % t, "thr")
-        ts(T.zi[:], T.wz[:, 15:C:16], T.sc[:], None, Op.mult, None, "wz sc", "zi")
-        ts(T.od[:], T.zi[:], 1, None, Op.bitwise_and, None, "zi", "od")
-        ts(T.pn[:], T.zi[:], T.thr[:], -1000.0, Op.is_gt, Op.mult, "zi thr", "pn")
-        tt(T.qq[:], T.zi[:], T.od[:], Op.mult, "zi od", "qq")
-        tt(T.t1[:], T.f3[:], T.od[:], Op.mult, "f3 od", "t1")
-        tt(T.fp[:], T.fi[:], T.pn[:], Op.add, "fi pn", "fp")
-        tt(T.y1[:], T.fj[:], T.t1[:], Op.subtract, "fj t1", "y1")
-        tt(T.x1[:], T.qq[:], T.fp[:], Op.add, "qq fp", "x1")
-
-        for b in range(4):
-            mm(T.pd[:, 512 * b:512 * b + 128], T.qw[:, 128 * b:128 * b + 128], T.sw[:, 128 * b:128 * b + 128],
-               T.qx[:, lo - 32:lo + 2 * K], T.sx[:, lo - 32:lo + 2 * K],
-               "qw sw arr%d " % t + ("qx" if t == 0 else "arr%d" % (t - 1)), "p:d%d" % b)
-        for b in range(4):
-            o, i = T.ht[:, b:384:4], T.pd[:, 512 * b + 32:512 * b + 128]
-            if b % 2 == 0:
-                op("s", lambda o=o, i=i: S.activation(o, i, Act.Copy, scale=0.03125), "p:d%d" % b, "H%d" % b)
-            else:
-                ts(o, i, 0.03125, None, Op.mult, None, "p:d%d" % b, "H%d" % b)
+        tt(T.hb[:], T.sg[:].indirect(T.nx16[:]), T.fb[:], Op.is_ge, "fb fb2 sg sg2 nx16", "hb")
+        scan(T.c2[:], T.hb[:], T.hb[:], 0.0, Op.add, Op.add, "hb", "c2")
+        scan(T.eb[:, 16:240], T.c2[:], T.hb[:], 0.0, Op.max, Op.mult, "hb c2", "eb")
+        cp("s", T.zp[:], T.eb[:].indirect(T.pv16[:]), "eb pv16", "zp")
+        wrap(T.wo[:, 0:C], T.fb[:], "fb fb2", "wf")
+        wrap(T.wo[:, C:2 * C], T.eb[:, 16:240], "eb", "we")
+        wrap(T.wo[:, 2 * C:3 * C], T.zp[:], "zp", "wq")
+        ts(T.w3[:], T.wo[:, 15:3 * C:16], T.sc[:], None, Op.mult, None, "wf we wq sc", "w3")
+        f, z = T.w3[:, 0:14], T.z[:]
+        tt(z, T.w3[:, 14:28], T.w3[:, 28:42], Op.add, "w3", "z")
+        ts(T.nz[:], z, 0.5, 320.0, Op.is_lt, Op.mult, "z", "nz")
+        tt(T.t1[:], T.nz[:], f, Op.mult, "nz w3", "t1")
+        tt(T.y1[:], T.t1[:], T.jm[:], Op.add, "t1 jm", "y1")
+        tt(T.x2[:], z, f, Op.add, "z w3", "x2")
+        ts(T.thr[:], T.li[:, lo + 1:lo + 2], 240.0 + 2 * K, 239.5, Op.min, Op.subtract, lst, "thr")
+        ts(T.pn[:], z, T.thr[:], -1000.0, Op.is_gt, Op.mult, "z thr", "pn")
+        tt(T.x1[:], T.x2[:], T.pn[:], Op.add, "x2 pn", "x1")
         tt(T.l1[:], T.y1[:], T.x1[:], Op.max, "y1 x1", "l1")
-        quant(T.qh[:], T.sh[:], T.ht[:], "ht_pad H0 H1 H2 H3", "qh")
-        ts(T.l16[:], T.l1[:], 222.0, None, Op.add, None, "l1", "l16")
-        mm(T.pp[:, 0:128], T.qur[:], T.sur[:], T.qh[:], T.sh[:], "qur sur qh", "p:p")
-        for b in range(4):
-            cp("s", T.tw[:, PL * b + 256:PL * b + PL:2], T.ht[:, b:384:4], "H%d" % b, "TH%d" % b)
-            if b == 1:
-                cp("s", T.h0[:], T.gw[:].indirect(T.l16[:]), "l16 g_own g_slot g_next g_prev", "h0")
-        cp("v", T.pa[:], T.pp[:, 0:2 * K:2], "p:p", "pa")
-        tt(T.fw[:, C:320:2], T.pp[:, 1:2 * K:2], T.pa[:], Op.is_gt, "p:p pa fw", "gt")
-        tt(T.fw[:, C + 1:320:2], T.pp[:, 1:2 * K:2], T.pa[:], Op.is_le, "p:p pa fw", "le")
-        tt(T.hv[:], T.fw[:].indirect(T.l16[:]), T.h0[:], Op.add, "gt le fw l16 h0", "hv")
-        wrap(T.hw[:], T.hv[:], C, "hv", "hw")
-        ts(T.lx[:], T.hw[:, 15:C:16], T.sc[:], 2.0, Op.mult, Op.mult, "hw sc", "lx")
-        for b in range(4):
-            cp("vs"[b % 2], T.xt[:, b:4 * C:4], T.tw[:, PL * b:PL * b + PL].indirect(T.lx[:]),
-               "lx T%d TH%d tw_zero" % (b, b), "X%d" % b)
-        xkeys = "X0 X1 X2 X3"
+        ts(T.l16[:], T.l1[:], 221.0, None, Op.add, None, "l1", "l16")
+        cp("s", T.h0[:], T.gw[:].indirect(T.l16[:]), "l16 g_own g_slot g_next g_prev", "h0")
 
-    cp("s", T.ots[:], T.rt[:].indirect(T.lx[:]), "rt rt2 lx", "ots")
-    quant(T.qx[:, 0:C], T.sx[:, 0:C], T.xt[:], xkeys, "qx")
-    mm(T.ps[:, 0:C], T.qv[:], T.sv[:], T.qx[:, 0:C], T.sx[:, 0:C], "qv qx", "p:s")
-    cp("v", T.ys[:], T.ps[:, 0:C], "p:s", "ys")
-    dma("y", T.oc[:], T.qx[:, 0:C].bitcast(dt.uint8), "qx", "", "doc")
+        unpack(qy, sy, arr, "mN")
+        for b in range(4):
+            p, plane = 512 * b, T.tw[:, PL * b:PL * b + PL]
+            cp("svsv"[b], T.tp[:, 256 * b + 16:256 * b + 240], T.pd[:, p:p + C], "p:d%d" % b, "N%d" % b)
+            cp("vsvs"[b], T.at[:, b:384:4], T.tp[:, 256 * b:256 * b + 256].indirect(T.li[:, lo + 2:lo + 8]),
+               "%s N%d tp_zero" % (lst, b), "A%d" % b)
+            mm(T.pd[:, p:p + 128], T.qw[:, 128 * b:128 * b + 128], T.sw[:, 128 * b:128 * b + 128], T.qa[:], T.sa[:],
+               "qw sw qa", "p:d%d" % b, "mW%d" % b)
+            tt(T.ht[:, b:8 * K:4], T.pd[:, p:p + 2 * K], T.hs[:], Op.mult, "p:d%d hs0 hs1" % b, "H%d" % b)
+            act(T.tw[:, PL * b + 256:PL * b + PL:2], T.pd[:, p:p + 2 * K], Act.Copy, "p:d%d" % b, "TH%d" % b, scale=HS)
+            cp("vsvs"[b], T.xt[:, b:512:4], plane.indirect(T.lx[:, 0:8]), "lx0 T%d TH%d" % (b, b), "X%d" % b)
+            cp("vsvs"[b], T.xt[:, 512 + b:4 * C:4], plane.indirect(T.lx[:, 8:14]), "lx1 lx2 T%d TH%d" % (b, b), "Z%d" % b)
+        quant(T.qa[:], T.sa[:], T.at[:], "at_pad A0 A1 A2 A3", "qa")
+        quant(T.qh[:, 0:128], T.sh[:, 0:128], T.ht[:], hkeys, "qh")
+        op("t", scores, "qur sur qh qh_pad", "p:p", None, "mP")
+        ts(T.fw[:, C:320:2], T.pp[:, 0:K], 0.0, float(K), Op.is_gt, Op.mult, "p:p fw", "up")
+        ts(T.fw[:, C + 1:320:2], T.pp[:, 0:K], 0.0, -float(K), Op.is_gt, Op.mult, "p:p fw", "down")
+        for i, (c, d) in enumerate(CUTS):
+            hv, hw = T.hv[:, 16 * c:16 * d], T.hw[:, 16 * c:16 * d]
+            tt(hv, T.fw[:].indirect(T.l16[:, c:d]), T.h0[:, 16 * c:16 * d], Op.add, "up down fw l16 h0", "hv%d" % i)
+            scan(hw, T.kt[:, 0:16 * (d - c)], hv, 0.0, Op.mult, Op.max, "hv%d kt" % i, "hw%d" % i)
+            ts(T.lx[:, c:d], T.hw[:, 16 * c + 15:16 * d:16], T.sc[:], 2.0, Op.mult, Op.mult, "hw%d sc" % i, "lx%d" % i)
+        issue((LATER if t else FIRST).split())
+
+    lo = 256 * R
+    cp("s", T.ots[:], T.rt[:].indirect(T.lx[:]), "rt rt2 lx0 lx1 lx2", "ots")
+    a, b = halves(R)
+    mm(T.ps[:, 0:128], T.qv[:], T.sv[:], a[0], a[1], "qv qx3", "p:s", "mY")
+    mm(T.pp[:, 0:128], T.qv[:], T.sv[:], b[0], b[1], "qv qz3", "p:p", "mY2")
+    cp("v", T.ys[:, 0:128], T.ps[:, 0:128], "p:s", "ys")
+    cp("v", T.ys[:, 128:C], T.pp[:, 0:C - 128], "p:p", "ys2")
+    dma("y", T.oc[:], T.qx[:, lo:lo + C].bitcast(dt.uint8), "qx3 qz3", "", "doc")
     dma("s", T.ot[:], T.ots[0:128:16, :], "ots", "", "dot")
     for k in range(4):
-        dma("ys"[k % 2], T.osc[4 * k:4 * k + 4, :], T.sx[32 * k:32 * k + 4, 0:C], "qx", "", "ds%d" % k)
-    dma("y", T.y[:], T.ys[:], "ys", "", "dy")
-    _emit(g, T, ops, sent[0])
+        dma("ys"[k % 2], T.osc[4 * k:4 * k + 4, :], T.sx[32 * k:32 * k + 4, lo:lo + C], "qx3 qz3", "", "ds%d" % k)
+    dma("y", T.y[:], T.ys[:], "ys ys2", "", "dy")
+    issue(list(steps))
+    _emit(g, T, ops, 3 * R * ne_out)

@@ -4,14 +4,15 @@ C, K, R = 224, 48, 3
 PL = 448
 BIG = 65536.0
 HS = 0.03125
-STEP = 512.0
-ROUND = 1.5 * 2.0 ** 23 * STEP
+UNIT = 65536.0
+ROUND = 1.5 * 2.0 ** 23 * 512 / UNIT
+WL = 232
 _B = {
     "bfloat16": dict(x0=896, ut=512, vt=512, ez=528, df=128, xt=1024, tw=4 * PL, tp=1024, at=512, ht=512, fb=C, sg=C, mb=C,
-                     ub=3 * C, jk=C, one=C, hb=C, c2=C, eb=240, zp=C, wo=3 * C, gw=864, fw=864, h0=C, hv=C, hw=C, hp=C,
+                     cb=240, fn=C, hb=C, c2=C, eb=240, zp=C, wo=3 * C, gw=864, fw=864, h0=C, hv=C, hw=C, hp=C,
                      kt=C, k16=16, hs=2 * K),
-    "float32": dict(w3=42, z=14, thr=1, nz=14, t1=14, y1=14, pn=14, x2=14, x1=14, l1=14, cn=3 * C, wt=C + 8, ramp=C, hi=3, cnt=2,
-                    rt=PL, k1=16, k2=16, jw=14, jm=14, nk=4, sc=1, ys=C, ots=C),
+    "float32": dict(m1=14, q=14, thr=1, t1=14, y1=14, pn=14, x1=14, l1=14, cn=3 * WL, wt=3 * WL, ramp=C, nt=C, hi=3,
+                    rt=PL, k1=16, k2=16, jw=14, jm=14, j2=14, nk=2, sc=4, ys=C, ots=C),
     "int32": dict(nxi=16, pi=14, c16=14, pmi=14),
     "uint16": dict(lo=8 * R, li=8 * R, l16=14, lx=14, ul=8, pm16=14, nx16=14, pv16=14),
     "float8_e4m3fn_x4": dict(qu=128, qur=128, qv=128, qw=512, qe=512, qx=256 * (R + 1), qy=R * C, qa=128, qh=128 + K),
@@ -19,22 +20,24 @@ _B = {
 }
 SCRATCH = {k: ("sbuf", [128, n], d) for d, b in _B.items() for k, n in b.items()}
 SCRATCH.update({k: ("psum", [128, 2048 if k == "pd" else 512], "float32") for k in ("ps", "pp", "pe", "pf", "pd")})
-DMAS = ["dx", "du", "dn", "dwc", "dws", "dv", "doc", "ds0", "ds1", "ds2", "ds3", "dy", "dot"]
+WK = ("x0", "ca")
+DMAS = ["dx", "du", "dn", "dwa", "dwb", "dws", "dv", "doc", "ds0", "ds1", "ds2", "ds3", "dy", "dot"]
 SEMAPHORES = ["cv", "cs", "ct", "cg", "sent"] + DMAS + ["%s%d" % (k, t) for k in ("arr", "lst") for t in range(R)]
 
 CUTS = ((0, 8), (8, 12), (12, 14))
-FIRST = """dx du dn dws dwc df pi c16 rt xt_pad rt2 ht_pad g_slot wt_end
-    one ez0 ez pmi qe3 jw qe2 sc qe0 k1 qe1 k2 ul k16 qx pm16 qu nx16 qur sendq sends tp_zero cnt_pad fw at_pad
-    g_own sur ramp g_prev mD2 mD1 mD3 mS mD0 mS2 fb wt sg nk T1 T0 g_next T3 hs1 kt hs0 mb T2 cnt jm
-    hb u2 u0 u1 cn0 cn2 cn1 wf hp qh_pad hi c2 ln2 eb pv16 ln0 lc ln1 la we zp sendl wq
-    mN2 mN1 mN0 mN3 N2 N0 N3 w3 N1 A2 A0 thr z A3 A1 qa x2 pn dv nz
-    mW1 x1 t1 H1 mW0 mW2 mW3 H0 H2 y1 H3 l1 qh l16 mP TH1 TH0 TH3 TH2 h0
-    down up hv0 hv1 hw0 hv2 hw1 lx0 hw2 lx1 lx2 X0 Z0 X2 Z2 X3 X1 Z1 Z3"""
-LATER = """qx mS mS2 sg qz sendq sends mZ2 mZ mD2 mD3 mD0 mD1 sg2 fb fb2 mb cnt T3 T2 T1 T0
-    hb u2 u1 u0 lc cn1 cn0 cn2 c2 hi eb la ln1 ln0 ln2 sendl
-    mN1 qv wf we N1 zp wq mN3 mN0 mN2 N3 N0 N2 A1 A3 w3 A0 z A2 thr nz qa x2 pn t1 x1
-    mW0 mW2 mW1 mW3 y1 H0 H2 H1 H3 l1 qh l16 mP TH0 TH2 TH1 h0 TH3
-    up down hv0 hv1 hw0 hv2 hw1 lx0 lx1 hw2 X0 lx2 X2 Z0 Z2 X3 X1 Z1 Z3"""
+TQ, NQ, AQ, HQ = "ssss", "svsv", "svsv", "vvvv"
+FIRST = """dx dn du c16 pi rt df ez0 pmi jw wt_end nt pm16 ul ramp sm k2 k1 nk1 nk k16 qx g_own nx16 j2 hs0 hs1 wt0 qu ez cb_end
+    sur qur mS2 wt1 isc g_prev mS dwa dws sendq sends rt2 g_slot tp_zero at_pad ht_pad fb sg kt qe2
+    mba mbb wt2 ca sc qe0 cb n1a n2a n0a n1b n2b lc mD2 n0b hi2 s3 hi1 la1 hi0 fn la2 mD0 ln1 ln2 la0 mN2 ln0
+    hb hp dwb c2 mN0 qe1 pv16 eb qe3 mN1 we sendl fw xt_pad wf g_next N1 mN3 N2 zp m1 N3 wq
+    A1 A3 q N0 A2 thr A0 qa mW0 dv qh_pad T0 pn jm mW2 t1 x1 H0 mW1 mW3 mD1 H2 H1 y1 mD3 H3 T1 l1 qh l16 T2 mP h0
+    up TH0 TH2 down hv0 TH1 hv1 T3 hw0 hv2 hw1 lx0 TH3 X1 hw2 lx1 X3 X0 lx2 X2 Z3 Z0 Z2 Z1"""
+LATER = """qx mS2 mS qz sendq sends mZ mZ2 sg sg2 fb fb2 fn mD2 mD0 mD3 mD1 T1 T0 T2 T3
+    mba mbb ca wf cb n0a n1a n2a hb n0b n1b n2b c2 hi0 hi1 hi2 la1 la2 la0 ln0 ln1 ln2 lc sendl
+    eb zp qv we mN1 mN0 mN3 mN2 N1 N0 N3 N2 m1 wq A1 A3 A0 A2 q thr qa t1 pn x1 y1
+    mW0 mW2 mW1 mW3 H0 H2 H1 H3 l1 qh mP l16 TH0 TH2 h0 TH1 TH3
+    up down hv0 hv1 hw0 hv2 hw1 lx0 hw2 lx1 X1 X0 X3 lx2 Z1 X2 Z2 Z3 Z0"""
+LAST = "ots qx qz mY mY2 ys ys2 doc dot ds0 ds1 ds2 ds3 dy"
 
 
 def _emit(g, T, ops, sent):
@@ -152,35 +155,38 @@ def rank_program(g, core, T, topo):
     def send(out, in_, sem, r, name):
         op("g", lambda: g.remote_dma(out, in_, T.sem[sem], T.sem.sent, pid, rid, mask), r, "", "remote", name)
 
-    def unpack(q, s, key, name):
-        for b in range(4):
-            mm(T.pd[:, 512 * b:512 * b + C], T.qe[:, 128 * b:128 * b + 128], T.se[:, 128 * b:128 * b + 128], q, s,
-               "qe%d %s" % (b, key), "p:d%d" % b, name + str(b))
+    def unpack(banks, q, s, key, name):
+        for b, (bank, pk) in enumerate(banks):
+            mm(bank, T.qe[:, 128 * b:128 * b + 128], T.se[:, 128 * b:128 * b + 128], q, s, "qe%d %s" % (b, key), pk, name + str(b))
 
     def scores():
         PE.matmul_mx(T.pp[:, 0:128], T.qur[:], T.sur[:], T.qh[:, 0:128], T.sh[:, 0:128], True, False)
         return PE.matmul_mx(T.pp[:, 0:128], T.qur[:], T.sur[:], T.qh[:, K:K + 128], T.sh[:, K:K + 128], False, True)
 
-    dma("s", T.nxi[:, 0:14], T.nx[:], "", "nxi", "dn")
+    dma("y", T.nxi[:, 0:14], T.nx[:], "", "nxi", "dn")
+    dma("y", T.ut[:], T.u[:], "", "ut", "du")
     dma("y", T.x0[:], T.x[:], "", "x0", "dx")
-    dma("s", T.ut[:], T.u[:], "", "ut", "du")
-    dma("y", T.qw[:].bitcast(dt.uint8), T.wc[:], "x0 ut", "qw", "dwc")
-    dma("y", T.sw[:], T.ws[:], "x0 ut", "sw", "dws")
+    dma("y", T.qw[:, 0:256].bitcast(dt.uint8), T.wc[:, 0:1024], WK[0], "qw0 qw1", "dwa")
+    dma("y", T.sw[:], T.ws[:], WK[0], "sw", "dws")
+    dma("y", T.qw[:, 256:512].bitcast(dt.uint8), T.wc[:, 1024:2048], WK[1], "qw2 qw3", "dwb")
     dma("y", T.vt[:], T.v[:], "qa", "vt", "dv")
 
-    hkeys = "ht_pad H0 H1 H2 H3"
+    hkeys = "ht_pad H0 H1 H2 H3 G0 G1 G2 G3"
+    sc, isc, s3 = T.sc[:, 0:1], T.sc[:, 1:2], T.sc[:, 2:3]
     iota(T.df[:], [[1, 128]], 0, -1, "df")
     iota(T.pi[:], [[0, 14]], 0, 1, "pi", False)
     iota(T.c16[:], [[16, 14]], 0, 0, "c16", False)
     iota(T.rt[:, 0:256], [[1, 256]], -16, 0, "rt")
     iota(T.rt[:, 256:PL], [[1, 2], [2, K], [0, 2]], C, 0, "rt2")
-    iota(T.gw[:, C:320], [[1, K], [K, 2]], 128, 0, "g_slot")
-    iota(T.wt[:, C:C + 1], [[0, 1]], int(STEP) * 16 + 240, 0, "wt_end")
-    for ap, n, key in ((T.tp[:, 240:1024:256], 4, "tp_zero"), (T.cnt[:, 0:1], 1, "cnt_pad"), (T.at[:, 384:512], 128, "at_pad"),
+    iota(T.gw[:, C:320], [[1, K], [-K, 2]], 128 + K, 0, "g_slot")
+    for ap, n, key in ((T.tp[:, 240:1024:256], 4, "tp_zero"), (T.at[:, 384:512], 128, "at_pad"),
                        (T.xt[:, 896:1024], 128, "xt_pad"), (T.ht[:], 512, hkeys), (T.fw[:], 864, "fw")):
         iota(ap, [[0, n]], 0, 0, key)
     fill(T.ez[:], 0.0, "ez", "ez0")
-    fill(T.one[:], 1.0, "one")
+    fill(T.cb[:, C:C + 1], 256.0, "cb_end")
+    fill(T.wt[:, C:C + 1], 2.0 - 513 * 240 / UNIT, "wt_end")
+    fill(T.hs[:, 0:K], -HS, "hs0")
+    fill(T.hs[:, K:2 * K], HS, "hs1")
     ts(T.ez[:, 3:515:4], T.df[:], 0.0, None, Op.is_equal, None, "df", "ez")
     for b in range(4):
         quant(T.qe[:, 128 * b:128 * b + 128], T.se[:, 128 * b:128 * b + 128], T.ez[:, 3 - b:515 - b], "ez", "qe%d" % b)
@@ -192,20 +198,26 @@ def rank_program(g, core, T, topo):
     ts(T.k2[:], T.rt[:, 16:32], T.jw[:, 0:1], None, Op.not_equal, None, "rt jw", "k2")
     tt(T.k16[:], T.k1[:], T.k2[:], Op.max, "k1 k2", "k16")
     cp("s", T.kt[:], T.k16[:].indirect(T.pm16[:]), "k16 pm16", "kt")
-    ts(T.sc[:], T.jw[:, 0:1], 15.0, 1.0 / BIG, Op.is_equal, Op.max, "jw", "sc")
-    act(T.nk[:], T.jw[:, 0:4], Act.Copy, "jw", "nk", scale=-1.0)
-    act(T.jm[:], T.jw[:], Act.Identity, "jw", "jm", bias=-221.0)
-    act(T.hs[:, 0:K], T.one[:, 0:K], Act.Copy, "one", "hs0", scale=-HS)
-    act(T.hs[:, K:2 * K], T.one[:, 0:K], Act.Copy, "one", "hs1", scale=HS)
+    ts(T.sc[:, 3:4], T.jw[:, 0:1], 15.0, BIG - 1.0, Op.not_equal, Op.mult, "jw", "sm")
+    act(sc, T.sc[:, 3:4], Act.Identity, "sm", "sc", bias=2.0, scale=-2.0 / BIG)
+    act(isc, T.sc[:, 3:4], Act.Identity, "sm", "isc", bias=0.5, scale=0.5)
+    act(s3, T.sc[:, 3:4], Act.Identity, "sm", "s3", bias=3.0, scale=3.0)
+    act(T.nk[:, 0:1], T.jw[:, 0:1], Act.Copy, "jw", "nk", scale=-2.0)
+    act(T.nk[:, 1:2], T.jw[:, 0:1], Act.Identity, "jw", "nk1", scale=2.0, bias=6.0)
+    act(T.j2[:], T.jw[:], Act.Identity, "jw", "j2", bias=742.0)
+    act(T.jm[:], T.j2[:], Act.Copy, "j2 isc", "jm", scale=isc)
     quant(T.qh[:, K:K + 128], T.sh[:, K:K + 128], T.ht[:], hkeys, "qh_pad qh")
     cp("v", T.nx16[:], T.nxi[:, 0:14], "nxi", "nx16")
     act(T.gw[:, 0:C], T.rt[:, 16:240], Act.Identity, "rt", "g_own", bias=8.0, scale=0.5)
-    cp("s", T.gw[:, 320:544], T.gw[:, 0:C].indirect(T.nx16[:]), "g_own nx16", "g_next")
-    op("v", lambda: V.tensor_copy(T.gw[:, 640:864].indirect(T.nx16[:]), T.gw[:, 0:C]), "g_own nx16", "g_prev")
-    wrap(T.hp[:], T.gw[:, 640:864], "g_prev", "hp")
-    ts(T.pv16[:], T.hp[:, 15:C:16], T.sc[:], 2.0, Op.mult, Op.mult, "hp sc", "pv16")
-    act(T.ramp[:], T.rt[:, 16:240], Act.Identity, "rt", "ramp", bias=STEP * 240, scale=-STEP)
-    tt(T.wt[:, 0:C], T.rt[:, 32:256].indirect(T.nx16[:]), T.ramp[:], Op.add, "rt nx16 ramp", "wt")
+    cp("s", T.gw[:, 640:864], T.gw[:, 0:C].indirect(T.nx16[:]), "g_own nx16", "g_next")
+    op("v", lambda: V.tensor_copy(T.gw[:, 320:544].indirect(T.nx16[:]), T.gw[:, 0:C]), "g_own nx16", "g_prev")
+    wrap(T.hp[:], T.gw[:, 320:544], "g_prev", "hp")
+    ts(T.pv16[:], T.hp[:, 15:C:16], sc, None, Op.mult, None, "hp sc", "pv16")
+    act(T.ramp[:], T.rt[:, 16:240], Act.Identity, "rt", "ramp", bias=2.0 - 512 * 16 / UNIT, scale=-512 / UNIT)
+    act(T.nt[:], T.rt[:, 32:256], Act.Copy, "rt", "nt", scale=-1.0 / UNIT)
+    tt(T.wt[:, 0:C], T.nt[:].indirect(T.nx16[:]), T.ramp[:], Op.add, "nt nx16 ramp", "wt0")
+    for r in (1, 2):
+        act(T.wt[:, WL * r:WL * r + C + 1], T.wt[:, 0:C + 1], Act.Identity, "wt0 wt_end", "wt%d" % r, bias=32.0 * r)
     quant(T.qu[:], T.su[:], T.ut[:], "ut", "qu")
     cp("v", T.qur[:].bitcast(dt.uint32), T.qu[:].bitcast(dt.uint32).indirect(T.ul[:]), "qu ul", "qur")
     cp("s", T.sur[:], T.su[:].indirect(T.ul[:]), "qu ul", "sur")
@@ -240,64 +252,73 @@ def rank_program(g, core, T, topo):
             signs((qx, sx), qk, 0, C, front, ("mS", "mS2", "fb fb2", "sg sg2"))
         send(qy.bitcast(dt.uint8), qx.bitcast(dt.uint8), arr, qk, "sendq")
         send(sy, sx, arr, qk, "sends")
-        unpack(qx, sx, qk, "mD")
-        for b in range(4):
-            cp("s", T.tw[:, PL * b + 16:PL * b + 240], T.pd[:, 512 * b:512 * b + C], "p:d%d" % b, "T%d" % b)
-        tt(T.mb[:], T.fb[:].indirect(T.nx16[:]), T.sg[:], Op.is_le, "fb fb2 sg sg2 nx16", "mb")
-        act(T.jk[:], T.mb[:], Act.Identity, "mb", "cnt jk", scale=2.0, accum_out=T.cnt[:, 1:2])
-        ts(T.lo[:, lo:lo + 2], T.cnt[:], 240.0, None, Op.add, None, "cnt cnt_pad", "lc")
+        own = [(bank[:, 0:C], pk) for bank, pk in front + back]
+        unpack(own, qx, sx, qk, "mD")
+        for b, (bank, pk) in enumerate(own):
+            cp(TQ[b], T.tw[:, PL * b + 16:PL * b + 240], bank, pk, "T%d" % b)
+        for h, c, d in (("a", 0, 128), ("b", 128, C)):
+            nx = T.nx16[:, c // 16:d // 16]
+            tt(T.mb[:, c:d], T.fb[:].indirect(nx), T.sg[:, c:d], Op.is_le, "fb fb2 nx16 " + ("sg2" if c else "sg"), "mb" + h)
+            scan(T.cb[:, c:d], T.mb[:, c:d], T.mb[:, c:d], T.cb[:, c - 1:c] if c else T.nk[:, 0:1], Op.add, Op.add,
+                 "mb%s %s" % (h, "ca" if c else "nk"), "c" + h)
+            for r in range(3):
+                w = WL * r
+                i, j = (c, d + 1) if c else (16 * r, d)
+                scan(T.cn[:, w + i:w + j], T.wt[:, w + i:w + j], T.cb[:, i:j], T.cn[:, w + c - 1:w + c] if c else -100.0,
+                     Op.max, Op.min, "wt%d wt_end cb_end c%s %s" % (r, h, "n%da" % r if c else ""), "n%d%s" % (r, h))
+        ts(T.lo[:, lo:lo + 2], T.cb[:, C - 2:C], T.nk[:, 1:2], None, Op.add, None, "cb nk1", "lc")
         for r in range(3):
-            ub, last = T.ub[:, C * r:C * r + C], T.cn[:, C * r + C - 1:C * r + C]
-            scan(ub, T.mb[:], T.one[:], T.nk[:, r:r + 1], Op.add, Op.min, "mb one nk", "u%d" % r)
-            scan(T.cn[:, C * r:C * r + C], ub, T.wt[:, 1:C + 1], T.wt[:, 0:1], Op.mult, Op.max, "wt wt_end u%d" % r, "cn%d" % r)
-            ts(T.lo[:, lo + 5 + r:lo + 6 + r], last, T.hi[:, r:r + 1], None, Op.subtract, None, "cn%d hi" % r, "ln%d" % r)
-        ts(T.hi[:], T.cn[:, C - 1:3 * C:C], ROUND, ROUND, Op.add, Op.subtract, "cn0 cn1 cn2", "hi")
-        ts(T.lo[:, lo + 2:lo + 5], T.cn[:, C - 1:3 * C:C], -1.0 / STEP, 256.5, Op.mult, Op.add, "cn0 cn1 cn2", "la")
-        send(T.li[:, lo:lo + 8], T.lo[:, lo:lo + 8], lst, "lc la ln0 ln1 ln2", "sendl")
+            last = T.cn[:, WL * r + C:WL * r + C + 1]
+            ts(T.hi[:, r:r + 1], last, ROUND, ROUND, Op.add, Op.subtract, "n%db" % r, "hi%d" % r)
+            ts(T.lo[:, lo + 2 + r:lo + 3 + r], last, 32.0 * r + 2.0, -UNIT / 512, Op.subtract, Op.mult, "n%db" % r, "la%d" % r)
+            ts(T.lo[:, lo + 5 + r:lo + 6 + r], last, T.hi[:, r:r + 1], -UNIT, Op.subtract, Op.mult, "n%db hi%d" % (r, r), "ln%d" % r)
+        send(T.li[:, lo:lo + 8], T.lo[:, lo:lo + 8], lst, "lc la0 la1 la2 ln0 ln1 ln2", "sendl")
 
-        tt(T.hb[:], T.sg[:].indirect(T.nx16[:]), T.fb[:], Op.is_ge, "fb fb2 sg sg2 nx16", "hb")
-        scan(T.c2[:], T.hb[:], T.hb[:], 0.0, Op.add, Op.add, "hb", "c2")
+        cp("s", T.fn[:], T.fb[:].indirect(T.nx16[:]), "fb fb2 nx16", "fn")
+        scan(T.hb[:], T.fn[:], T.fb[:], 0.0, Op.max, Op.subtract, "fn fb fb2", "hb")
+        scan(T.c2[:], T.hb[:], T.mb[:], 2.5, Op.add, Op.add, "hb mba mbb", "c2")
         scan(T.eb[:, 16:240], T.c2[:], T.hb[:], 0.0, Op.max, Op.mult, "hb c2", "eb")
-        cp("s", T.zp[:], T.eb[:].indirect(T.pv16[:]), "eb pv16", "zp")
+        act(T.zp[:], T.eb[:].indirect(T.pv16[:]), Act.Identity, "eb pv16", "zp", bias=-0.5)
         wrap(T.wo[:, 0:C], T.fb[:], "fb fb2", "wf")
         wrap(T.wo[:, C:2 * C], T.eb[:, 16:240], "eb", "we")
         wrap(T.wo[:, 2 * C:3 * C], T.zp[:], "zp", "wq")
-        ts(T.w3[:], T.wo[:, 15:3 * C:16], T.sc[:], None, Op.mult, None, "wf we wq sc", "w3")
-        f, z = T.w3[:, 0:14], T.z[:]
-        tt(z, T.w3[:, 14:28], T.w3[:, 28:42], Op.add, "w3", "z")
-        ts(T.nz[:], z, 0.5, 320.0, Op.is_lt, Op.mult, "z", "nz")
-        tt(T.t1[:], T.nz[:], f, Op.mult, "nz w3", "t1")
+        tt(T.m1[:], T.wo[:, 15:C:16], T.wo[:, C + 15:2 * C:16], Op.max, "wf we", "m1")
+        tt(T.q[:], T.m1[:], T.wo[:, 2 * C + 15:3 * C:16], Op.max, "m1 wq", "q")
+        ts(T.t1[:], T.q[:], s3, -160.0, Op.min, Op.mult, "q s3", "t1")
         tt(T.y1[:], T.t1[:], T.jm[:], Op.add, "t1 jm", "y1")
-        tt(T.x2[:], z, f, Op.add, "z w3", "x2")
-        ts(T.thr[:], T.li[:, lo + 1:lo + 2], 240.0 + 2 * K, 239.5, Op.min, Op.subtract, lst, "thr")
-        ts(T.pn[:], z, T.thr[:], -1000.0, Op.is_gt, Op.mult, "z thr", "pn")
-        tt(T.x1[:], T.x2[:], T.pn[:], Op.add, "x2 pn", "x1")
+        ts(T.thr[:], T.li[:, lo + 1:lo + 2], 6.0 + 2 * K, isc, Op.min, Op.mult, lst + " isc", "thr")
+        ts(T.pn[:], T.q[:], T.thr[:], -1000.0 * BIG, Op.is_ge, Op.mult, "q thr", "pn")
+        tt(T.x1[:], T.q[:], T.pn[:], Op.add, "q pn", "x1")
         tt(T.l1[:], T.y1[:], T.x1[:], Op.max, "y1 x1", "l1")
-        ts(T.l16[:], T.l1[:], 221.0, None, Op.add, None, "l1", "l16")
+        ts(T.l16[:], T.l1[:], sc, 218.0, Op.mult, Op.add, "l1 sc", "l16")
         cp("s", T.h0[:], T.gw[:].indirect(T.l16[:]), "l16 g_own g_slot g_next g_prev", "h0")
 
-        unpack(qy, sy, arr, "mN")
+        unpack([(T.pd[:, 512 * b:512 * b + C], "p:d%d" % b) for b in range(4)], qy, sy, arr, "mN")
         for b in range(4):
             p, plane = 512 * b, T.tw[:, PL * b:PL * b + PL]
-            cp("svsv"[b], T.tp[:, 256 * b + 16:256 * b + 240], T.pd[:, p:p + C], "p:d%d" % b, "N%d" % b)
-            cp("vsvs"[b], T.at[:, b:384:4], T.tp[:, 256 * b:256 * b + 256].indirect(T.li[:, lo + 2:lo + 8]),
+            cp(NQ[b], T.tp[:, 256 * b + 16:256 * b + 240], T.pd[:, p:p + C], "p:d%d" % b, "N%d" % b)
+            cp(AQ[b], T.at[:, b:384:4], T.tp[:, 256 * b:256 * b + 256].indirect(T.li[:, lo + 2:lo + 8]),
                "%s N%d tp_zero" % (lst, b), "A%d" % b)
             mm(T.pd[:, p:p + 128], T.qw[:, 128 * b:128 * b + 128], T.sw[:, 128 * b:128 * b + 128], T.qa[:], T.sa[:],
-               "qw sw qa", "p:d%d" % b, "mW%d" % b)
-            tt(T.ht[:, b:8 * K:4], T.pd[:, p:p + 2 * K], T.hs[:], Op.mult, "p:d%d hs0 hs1" % b, "H%d" % b)
+               "qw%d sw qa" % b, "p:d%d" % b, "mW%d" % b)
+            if HQ[b] == "v":
+                tt(T.ht[:, b:8 * K:4], T.pd[:, p:p + 2 * K], T.hs[:], Op.mult, "p:d%d hs0 hs1" % b, "H%d G%d" % (b, b))
+            else:
+                act(T.ht[:, b:4 * K:4], T.pd[:, p:p + K], Act.Copy, "p:d%d" % b, "H%d" % b, scale=-HS)
+                act(T.ht[:, 4 * K + b:8 * K:4], T.pd[:, p + K:p + 2 * K], Act.Copy, "p:d%d" % b, "G%d" % b, scale=HS)
             act(T.tw[:, PL * b + 256:PL * b + PL:2], T.pd[:, p:p + 2 * K], Act.Copy, "p:d%d" % b, "TH%d" % b, scale=HS)
             cp("vsvs"[b], T.xt[:, b:512:4], plane.indirect(T.lx[:, 0:8]), "lx0 T%d TH%d" % (b, b), "X%d" % b)
             cp("vsvs"[b], T.xt[:, 512 + b:4 * C:4], plane.indirect(T.lx[:, 8:14]), "lx1 lx2 T%d TH%d" % (b, b), "Z%d" % b)
         quant(T.qa[:], T.sa[:], T.at[:], "at_pad A0 A1 A2 A3", "qa")
         quant(T.qh[:, 0:128], T.sh[:, 0:128], T.ht[:], hkeys, "qh")
         op("t", scores, "qur sur qh qh_pad", "p:p", None, "mP")
-        ts(T.fw[:, C:320:2], T.pp[:, 0:K], 0.0, float(K), Op.is_gt, Op.mult, "p:p fw", "up")
-        ts(T.fw[:, C + 1:320:2], T.pp[:, 0:K], 0.0, -float(K), Op.is_gt, Op.mult, "p:p fw", "down")
+        ts(T.fw[:, C + 1:320:2], T.pp[:, 0:K], 0.0, float(K), Op.is_gt, Op.mult, "p:p fw", "up")
+        ts(T.fw[:, C:320:2], T.pp[:, 0:K], 0.0, -float(K), Op.is_gt, Op.mult, "p:p fw", "down")
         for i, (c, d) in enumerate(CUTS):
             hv, hw = T.hv[:, 16 * c:16 * d], T.hw[:, 16 * c:16 * d]
             tt(hv, T.fw[:].indirect(T.l16[:, c:d]), T.h0[:, 16 * c:16 * d], Op.add, "up down fw l16 h0", "hv%d" % i)
             scan(hw, T.kt[:, 0:16 * (d - c)], hv, 0.0, Op.mult, Op.max, "hv%d kt" % i, "hw%d" % i)
-            ts(T.lx[:, c:d], T.hw[:, 16 * c + 15:16 * d:16], T.sc[:], 2.0, Op.mult, Op.mult, "hw%d sc" % i, "lx%d" % i)
+            ts(T.lx[:, c:d], T.hw[:, 16 * c + 15:16 * d:16], sc, None, Op.mult, None, "hw%d sc" % i, "lx%d" % i)
         issue((LATER if t else FIRST).split())
 
     lo = 256 * R
@@ -312,5 +333,5 @@ def rank_program(g, core, T, topo):
     for k in range(4):
         dma("ys"[k % 2], T.osc[4 * k:4 * k + 4, :], T.sx[32 * k:32 * k + 4, lo:lo + C], "qx3 qz3", "", "ds%d" % k)
     dma("y", T.y[:], T.ys[:], "ys ys2", "", "dy")
-    issue(list(steps))
+    issue(LAST.split())
     _emit(g, T, ops, 3 * R * ne_out)

@@ -1,49 +1,89 @@
 from concourse.mybir import dt, AluOpType as Op, ActivationFunctionType as Act
 
 C, K, R = 224, 48, 3
-PL = 448
+MID = 64.0
 BIG = 65536.0
 HS = 0.03125
 UNIT = 65536.0
 ROUND = 1.5 * 2.0 ** 23 * 512 / UNIT
 WL = 232
+NEXT, PREV, SLOT, GW = 240, 464, 688, 688 + 8 * K
+E0 = (SLOT - C) // 8
 _B = {
-    "bfloat16": dict(x0=896, ut=512, vt=512, ez=528, df=128, xt=1024, tw=4 * PL, tp=1024, at=512, ht=512, fb=C, sg=C, mb=C,
-                     cb=240, fn=C, hb=C, c2=C, eb=240, zp=C, wo=3 * C, gw=864, fw=864, h0=C, hv=C, hw=C, hp=C,
-                     kt=C, k16=16, hs=2 * K),
-    "float32": dict(m1=14, q=14, thr=1, t1=14, y1=14, pn=14, x1=14, l1=14, cn=3 * WL, wt=3 * WL, ramp=C, nt=C, hi=3,
-                    rt=PL, k1=16, k2=16, jw=14, jm=14, j2=14, nk=2, sc=4, ys=C, ots=C),
-    "int32": dict(nxi=16, pi=14, c16=14, pmi=14),
-    "uint16": dict(lo=8 * R, li=8 * R, l16=14, lx=14, ul=8, pm16=14, nx16=14, pv16=14),
-    "float8_e4m3fn_x4": dict(qu=128, qur=128, qv=128, qw=512, qe=512, qx=256 * (R + 1), qy=R * C, qa=128, qh=128 + K),
-    "uint8": dict(su=128, sur=128, sv=128, sw=512, se=512, sx=256 * (R + 1), sy=R * C, sa=128, sh=128 + K),
+    "bfloat16": dict(x0=896, ut=512, vt=512, ez=528, df=128, xt=1024, tw=4 * (C + 2 * K), tp=1024, at=512, ht=512, fb=C, sg=C,
+                     mb=C, ca=128, cb=240, fn=C, hb=C, c2=C, eb=C, zp=C, wo=3 * C, gw=GW, fw=GW, hd=2 * C, hw=2 * C, hp=C,
+                     kt=C, kq=C, kk=32, r4=32, hs=2 * K, zz=K),
+    "float32": dict(m1=14, thr=1, t1=14, y1=14, ya=28, yb=28, yo=28, cn=3 * WL, wt=3 * WL, ramp=C, nt=C, hi=3,
+                    k1=32, k2=32, jw=14, jm=14, j2=14, nk=2, sc=8, pf=2, ys=C, ots=C),
+    "int32": dict(nxi=16, pi=14, c16=14, pmi=14, pq=2),
+    "uint16": dict(lo=8 * R, li=8 * R, l16=14, lx=56, ul=8, pm16=14, nx16=14, pv16=14),
+    "float8_e4m3fn_x4": dict(qu=128, qur=128, qv=128, qw=512, qe=512, qx=256 * (R + 1), qy=R * C, qh=256),
+    "uint8": dict(su=128, sur=128, sv=128, sw=512, se=512, sx=256 * (R + 1), sy=R * C, sh=256),
 }
 SCRATCH = {k: ("sbuf", [128, n], d) for d, b in _B.items() for k, n in b.items()}
-SCRATCH.update({k: ("psum", [128, 2048 if k == "pd" else 512], "float32") for k in ("ps", "pp", "pe", "pf", "pd")})
-WK = ("x0", "ca")
-DMAS = ["dx", "du", "dn", "dwa", "dwb", "dws", "dv", "doc", "ds0", "ds1", "ds2", "ds3", "dy", "dot"]
-SEMAPHORES = ["cv", "cs", "ct", "cg", "sent"] + DMAS + ["%s%d" % (k, t) for k in ("arr", "lst") for t in range(R)]
+SCRATCH.update({k: ("psum", [128, 2048 if k == "pd" else 512], "float32") for k in ("ps", "pp", "pe", "pg", "pd")})
+WK = ("", "qur")
+DMAS = ["dx", "du", "dn", "dwa", "dwb", "dws", "dv", "dz", "ds0", "ds1", "ds2", "ds3", "doc", "dot", "dy"]
+SEMAPHORES = ["cv", "cs", "ct", "cg", "sent"] + ["%s%d" % (k, t) for k in ("arr", "lst") for t in range(R)] + DMAS
 
-CUTS = ((0, 8), (8, 12), (12, 14))
-TQ, NQ, AQ, HQ = "ssss", "svsv", "svsv", "vvvv"
-FIRST = """dx dn du c16 pi rt df ez0 pmi jw wt_end nt pm16 ul ramp sm k2 k1 nk1 nk k16 qx g_own nx16 j2 hs0 hs1 wt0 qu ez cb_end
-    sur qur mS2 wt1 isc g_prev mS dwa dws sendq sends rt2 g_slot tp_zero at_pad ht_pad fb sg kt qe2
+CUTS = (0, 64, 128, 224)
+HALF = 128
+PCUT = (0, 224)
+HQ = "vvvv"
+DQ = "vsv"
+PICKS = (("s", 0, 64), ("v", 64, 128), ("v", 128, 176), ("s", 176, 224))
+TQ, NQ, AQ = "ssss", "svsv", "svsv"
+FIRST = """dn dx du pi c16 g_own r4 df g_slot ez0 pmi pq0 pq1 jw pf wt_end nt pm16 ul ramp sm sm4 k2 k1 k24 k14 nk1 nk kk nx16 g_prev
+    qx j2 hs0 hs1 wt0 qu ez cb_end sur qur mS2 wt1 isc mS dwa dws sendq sends tp_zero at_pad ht_pad fb sg kt qe2
     mba mbb wt2 ca sc qe0 cb n1a n2a n0a n1b n2b lc mD2 n0b hi2 s3 hi1 la1 hi0 fn la2 mD0 ln1 ln2 la0 mN2 ln0
-    hb hp dwb c2 mN0 qe1 pv16 eb qe3 mN1 we sendl fw xt_pad wf g_next N1 mN3 N2 zp m1 N3 wq
-    A1 A3 q N0 A2 thr A0 qa mW0 dv qh_pad T0 pn jm mW2 t1 x1 H0 mW1 mW3 mD1 H2 H1 y1 mD3 H3 T1 l1 qh l16 T2 mP h0
-    up TH0 TH2 down hv0 TH1 hv1 T3 hw0 hv2 hw1 lx0 TH3 X1 hw2 lx1 X3 X0 lx2 X2 Z3 Z0 Z2 Z1"""
+    hb hp dwb c2 mN0 qe1 sc1 pv16 eb qe3 mN1 we sendl fw xt_pad wf g_next N1 mN3 N2 zp m1 N3 wq ya kq sc4 b4
+    A1 thr A3 q N0 A2 A0 t1 pn qa mW0 dv T0 jm mW2 y1 yo H0 mW1 mW3 mD1 H2 H1 mD3 l16 H3 T1 qh h0 T2 mP
+    up TH0 TI0 TH2 TI2 down hv0 TH1 TI1 hv1 T3 hv2 TH3 TI3 hw0 hw1 hw2 lx0 lx1 lx2 X0 X1 X2 X3"""
 LATER = """qx mS2 mS qz sendq sends mZ mZ2 sg sg2 fb fb2 fn mD2 mD0 mD3 mD1 T1 T0 T2 T3
-    mba mbb ca wf cb n0a n1a n2a hb n0b n1b n2b c2 hi0 hi1 hi2 la1 la2 la0 ln0 ln1 ln2 lc sendl
-    eb zp qv we mN1 mN0 mN3 mN2 N1 N0 N3 N2 m1 wq A1 A3 A0 A2 q thr qa t1 pn x1 y1
-    mW0 mW2 mW1 mW3 H0 H2 H1 H3 l1 qh mP l16 TH0 TH2 h0 TH1 TH3
-    up down hv0 hv1 hw0 hv2 hw1 lx0 hw2 lx1 X1 X0 X3 lx2 Z1 X2 Z2 Z3 Z0"""
-LAST = "ots qx qz mY mY2 ys ys2 doc dot ds0 ds1 ds2 ds3 dy"
+    mba mbb ca hb cb n0a n1a n2a n0b n1b n2b c2 hi0 hi1 la0 hi2 la1 la2 ln0 ln1 lc ln2 sendl
+    eb wf zp qv we mN1 mN0 mN3 mN2 N1 N0 N3 N2 m1 wq A1 thr A3 A0 A2 q qa t1 pn y1
+    mW0 mW2 mW1 mW3 yo H0 H2 H1 l16 H3 qh mP h0 TH0 TI0 TH2 TI2 TH1 TI1 TH3 TI3
+    up down hv0 hv1 hv2 hw0 hw1 hw2 lx0 lx1 lx2 X0 X1 X2 X3"""
+LAST = "qx ots qz mY mY2 ys ys2 doc dzc dot ds0 ds1 ds2 ds3 dy dz"
+FIRST = """wt_end ez0 hs1 pi pmi dn pq0 pq1 hs0 nx16 dx c16 ul jw g_own pm16 df du g_prev qx nt r4 qu pf k2 sendq k1 ez qur ramp sends
+    wt0 k14 nk sur tp_zero mS2 sm qe1 mS dws k24 ht_pad cb_end fb kk sg mD1 wt1 qe0 nk1 sm4 kt mba wt2 mbb qe2 sc1 mN0 mN1 ca cb
+    at_pad mN2 hp n1a dwa n2a n0a fn pv16 isc lc sc n1b T1 g_next n2b sc4 n0b hb hi1 la1 fw j2 hi2 hi0 la0 s3 c2 ln1 la2 b4 ln0
+    jm ln2 sendl qe3 mN3 eb wf N1 we N3 dwb N0 mD3 xt_pad m1 zp N2 mD0 wq A1 A3 g_slot A0 A2 ya thr q qa mD2 T0 t1 mW0 pn mW2 y1
+    mW1 T2 mW3 H0 kq H2 TI0 H1 H3 yo qh l16 h0 TH0 mP TI2 up TH3 down TH1 TI1 hv0 T3 TH2 hv1 dv hv2 TI3 hw0 hw1 lx0 hw2 X0 lx1
+    lx2 X1 X2 X3"""
+LAST = """qx doc qz mY ots ds0 mY2 ys dzc ds3 ds1 dot ys2 ds2 dy dz"""
+LATER = """qx mS qz mS2 sends mZ mZ2 fb sendq sg fb2 mD2 mD1 sg2 fn mba mN0 mbb mN2 wf N0 ca hb cb n0a mN3 n1a n2a lc n0b n1b n2b mN1 c2
+    hi0 la0 hi1 hi2 la2 la1 ln0 ln1 ln2 eb sendl mD0 N1 we zp N2 A0 N3 A2 m1 wq T1 A3 T2 A1 qv q mD3 qa mW0 mW2 t1 thr T3 y1 T0
+    pn H0 H2 mW1 TH2 H1 mW3 H3 yo TI1 qh TI3 l16 TH1 mP down h0 TI0 up TH3 hv0 TH0 hv1 hv2 hw0 hw1 hw2 lx0 lx1 TI2 lx2 X1 X0 X3
+    X2"""
+FIRST = """zz dx df ez0 ez pi pq0 du c16 hs0 pmi pq1 qe2 wt_end qe3 jw nk1 g_own pf ul r4 nk qx k2 ramp mD3 k1 k24 k14 qu nt pm16 dn sur
+    kk kt qur sends nx16 sm qe0 cb_end sendq mS2 sg wt0 hs1 wt2 mS at_pad wt1 mN2 fb qe1 sm4 mba mbb ca wf dws cb n1a s3 n0a fn
+    n2a n1b T3 sc1 b4 n0b tp_zero ht_pad dwa n2b fw isc hb mN1 mN0 hi1 lc hi0 la0 hi2 j2 la2 ln1 la1 mN3 sc4 ln0 ln2 ya g_next sc
+    c2 g_prev sendl kq eb N1 hp N2 jm mD0 mD1 N0 mD2 N3 A2 A0 pv16 A1 t1 zp T1 dwb A3 y1 we qa mW0 jo m1 g_slot wq xt_pad thr mW1
+    q T2 H0 T0 mW2 TI0 mW3 H1 H2 H3 pn qh yo TH2 TH3 l16 TH0 TI3 mP down up dv h0 hv1 TH1 hv0 hv2 hw0 hw1 hw2 TI2 TI1 lx0 lx1 lx2
+    X1 X0 X3 X2"""
+LAST = """qx qz ds2 ramp mY ys ds3 mY2 doc ds0 ds1 ots dot ys2 dy"""
+LATER = """qx mS2 qz mS fb mZ sends mZ2 sg fb2 qv sg2 mba mbb fn wf ca mD2 mD0 hb cb n0a n1a n2a n0b n1b n2b lc la0 hi0 hi1 sendq hi2
+    mN2 la1 la2 ln0 ln1 ln2 mN1 c2 mN0 mD1 eb t1 N2 mN3 N0 sendl we y1 zp N1 N3 mD3 A1 A2 A3 m1 thr A0 T2 wq qa mW3 mW2 T0 q pn
+    H3 H2 mW1 H1 mW0 H0 T1 T3 TI1 yo TH0 qh mP TI3 l16 TI0 down up TH2 h0 TH1 hv0 hv2 hw0 hv1 TI2 hw1 TH3 hw2 lx0 lx1 lx2 X0 X3
+    X1 X2"""
+FIRST = """ez0 pi zz pmi pq1 pq0 hs1 c16 df jw pm16 pf ez g_own nk1 ramp sm ul cb_end sm4 dx qe3 r4 qx k2 k1 du qe2 b4 nk qu sendq mD3 dn qe0 k14 ya wt_end nx16 qur sur mS2 k24 pr0 qe1 sends kk mS nt wt0 fb j2 sg pr1 isc mba mbb mD1 kq wt1 mN2 ca sc at_pad wt2 sc4 sc1 jm pr2 mN1 fn n0a kt cb n1a hs0 n2a n0b s3 g_next g_slot n1b T3 n2b lc la0 tp_zero hi0 mN0 hi2 la2 la1 ln0 ln1 mN3 ln2 N2 hb pr3 fw c2 wf hp N1 eb dws dwa mD2 dwb sendl N3 pv16 ht_pad N0 A1 A3 A2 mD0 A0 zp we t1 qa y1 mW0 wq m1 T0 jo thr T1 H0 mW1 H1 q xt_pad mW2 mW3 H2 H3 pn TI1 T2 TH2 TH0 qh TI0 yo mP l16 TH3 dv up down h0 hv0 hv1 TI2 TH1 hv2 hw0 hw1 TI3 hw2 lx0 X0 lx1 lx2 X1 X3 X2"""
+LAST = """qx ramp qz doc mY ots mY2 ys ys2 dy dot ds0 ds1 ds2 ds3"""
+LATER = """qx qz mS2 sg sendq mS mZ mZ2 sg2 fb fb2 mba mbb ca wf sends cb n0a mD3 n1a mD1 T3 mD0 mD2 n2a fn n0b n1b mN2 T0 mN0 T2 n2b lc T1 la0 hi0 hi2 la2 la1 ln1 ln0 ln2 hb sendl c2 N2 t1 mN1 mN3 eb N3 N1 qv A3 A1 we N0 thr zp A2 y1 A0 qa m1 mW3 wq mW2 mW1 q mW0 H3 H2 H1 H0 pn TI1 qh TI0 TI2 mP yo l16 up TH0 down TH2 h0 hv0 hv2 hw0 hv1 hw1 TI3 hw2 lx0 lx1 TH1 TH3 lx2 X0 X1 X3 X2"""
+FIRST = """zz dx df ez0 ez pi pq0 du c16 hs0 pmi pq1 qe2 wt_end qe3 jw nk1 g_own pf ul r4 nk qx k2 ramp mD3 k1 k24 k14 qu nt pm16 dn dwa dws sur
+    kk kt qur dwb sends nx16 sm qe0 cb_end sendq mS2 sg wt0 hs1 wt2 mS at_pad wt1 mN2 fb qe1 sm4 mba mbb ca wf cb n1a s3 n0a fn
+    n2a n1b T3 sc1 b4 n0b tp_zero ht_pad n2b fw isc hb mN1 mN0 hi1 lc hi0 la0 hi2 j2 la2 ln1 la1 mN3 sc4 ln0 ln2 ya g_next sc
+    c2 pr0 sendl kq eb N1 hp N2 jm mD0 mD1 N0 mD2 N3 A2 A0 pv16 A1 t1 zp T1 A3 y1 we qa mW0 jo m1 g_slot wq xt_pad thr mW1
+    q T2 H0 T0 mW2 TI0 mW3 H1 H2 H3 pn qh yo TH2 TH3 l16 TH0 TI3 mP down up dv h0 hv1 TH1 hv0 hv2 hw0 hw1 hw2 TI2 TI1 lx0 lx1 lx2
+    X1 X0 X3 X2"""
+LAST = "qx qz doc ds0 ds1 ds2 ds3 ramp mY ys mY2 ys2 dy ots dot"
+LATER = """qx qz mS2 qv mS sg mZ fb mZ2 fb2 mba sg2 mbb ca sendq wf sends cb n0a n1a n2a mD1 n0b mN2 mN0 fn n1b mN1 n2b lc hi0 la0 mN3 hi1 hi2 la2 ln0 mD2 la1 ln1 ln2 N2 hb t1 sendl c2 eb mD3 N0 zp N1 N3 A2 we y1 A1 A3 A0 T3 wq mD0 T1 thr m1 qa q mW3 mW2 pn H3 mW1 H2 T0 mW0 T2 TH3 H1 TI1 H0 TH0 yo qh TI0 mP l16 h0 up TH2 down hv0 hv2 hw0 hv1 TI2 TH1 TI3 hw1 hw2 lx0 X0 lx1 lx2 X3 X1 X2"""
 
 
 def _emit(g, T, ops, sent):
     eng = {"v": g.vector, "s": g.scalar, "t": g.tensor, "g": g, "y": g.sync}
     own = {"v": "cv", "s": "cs", "t": "ct", "g": "cg"}
-    count = {}
+    count, waited = {}, {}
     known = {q: {} for q in eng}
     writer, readers, mark = {}, {}, []
     for i, (q, fn, reads, writes, kind) in enumerate(ops):
@@ -73,6 +113,7 @@ def _emit(g, T, ops, sent):
                 continue
             eng[q].wait_ge(T.sem[sem], n)
             known[q][sem] = n
+            waited[sem] = max(waited.get(sem, 0), n)
             for s, m in seen.items():
                 known[q][s] = max(known[q].get(s, 0), m)
         ins = fn()
@@ -85,7 +126,7 @@ def _emit(g, T, ops, sent):
         mark.append((sem, count[sem], dict(known[q])))
     count["sent"] = sent
     for sem in SEMAPHORES:
-        if count.get(sem, 0) > known["g"].get(sem, 0):
+        if count.get(sem, 0) > waited.get(sem, 0):
             g.wait_ge(T.sem[sem], count[sem])
 
 
@@ -106,7 +147,7 @@ def rank_program(g, core, T, topo):
 
     def issue(order):
         names = [n for n in order if n in steps]
-        assert len(names) == len(steps)
+        assert len(names) == len(steps), sorted(set(steps) - set(names))
         ops.extend(steps.pop(n) for n in names)
 
     def ts(out, in0, a, b, o0, o1, r, w):
@@ -130,8 +171,8 @@ def rank_program(g, core, T, topo):
     def scan(out, d0, d1, init, o0, o1, r, w):
         op("v", lambda: V.tensor_tensor_scan(out, d0, d1, init, o0, o1), r, w)
 
-    def wrap(out, in_, r, w):
-        scan(out, T.kt[:], in_, 0.0, Op.mult, Op.max, r + " kt", w)
+    def wrap(out, in_, o, r, w):
+        scan(out, T.kt[:], in_, 0.0, Op.mult, o, r + " kt", w)
 
     def quant(q, s, in_, r, w, name=None):
         op("v", lambda: V.quantize_mx(q, s, in_), r, w, None, name)
@@ -163,6 +204,12 @@ def rank_program(g, core, T, topo):
         PE.matmul_mx(T.pp[:, 0:128], T.qur[:], T.sur[:], T.qh[:, 0:128], T.sh[:, 0:128], True, False)
         return PE.matmul_mx(T.pp[:, 0:128], T.qur[:], T.sur[:], T.qh[:, K:K + 128], T.sh[:, K:K + 128], False, True)
 
+    def pieces(key, c, d):
+        return " ".join(key + str(i) for i in range(len(CUTS) - 1) if CUTS[i] < d and c < CUTS[i + 1])
+
+    def picked(c, d):
+        return " ".join("X%d" % i for i, p in enumerate(PICKS) if p[1] < d and c < p[2])
+
     dma("y", T.nxi[:, 0:14], T.nx[:], "", "nxi", "dn")
     dma("y", T.ut[:], T.u[:], "", "ut", "du")
     dma("y", T.x0[:], T.x[:], "", "x0", "dx")
@@ -171,50 +218,62 @@ def rank_program(g, core, T, topo):
     dma("y", T.qw[:, 256:512].bitcast(dt.uint8), T.wc[:, 1024:2048], WK[1], "qw2 qw3", "dwb")
     dma("y", T.vt[:], T.v[:], "qa", "vt", "dv")
 
-    hkeys = "ht_pad H0 H1 H2 H3 G0 G1 G2 G3"
-    sc, isc, s3 = T.sc[:, 0:1], T.sc[:, 1:2], T.sc[:, 2:3]
+    col = lambda i: T.sc[:, i:i + 1]
+    sc, isc, s3, sc1, sc4, b4 = [col(i) for i in range(6)]
+    place = T.gw[:, 0:C]
     iota(T.df[:], [[1, 128]], 0, -1, "df")
     iota(T.pi[:], [[0, 14]], 0, 1, "pi", False)
     iota(T.c16[:], [[16, 14]], 0, 0, "c16", False)
-    iota(T.rt[:, 0:256], [[1, 256]], -16, 0, "rt")
-    iota(T.rt[:, 256:PL], [[1, 2], [2, K], [0, 2]], C, 0, "rt2")
-    iota(T.gw[:, C:320], [[1, K], [-K, 2]], 128 + K, 0, "g_slot")
+    iota(place, [[1, C]], -int(MID), 0, "g_own")
+    iota(T.r4[:], [[2, 2], [0, 2], [1, 8]], -2, 0, "r4")
+    iota(T.gw[:, SLOT:GW:4], [[2, K], [-1, 2]], C + 1 - int(MID), 0, "g_slot")
     for ap, n, key in ((T.tp[:, 240:1024:256], 4, "tp_zero"), (T.at[:, 384:512], 128, "at_pad"),
-                       (T.xt[:, 896:1024], 128, "xt_pad"), (T.ht[:], 512, hkeys), (T.fw[:], 864, "fw")):
+                       (T.xt[:, 896:1024], 128, "xt_pad"), (T.ht[:, 384:512], 128, "ht_pad"), (T.fw[:, 0:SLOT], SLOT, "fw")):
         iota(ap, [[0, n]], 0, 0, key)
     fill(T.ez[:], 0.0, "ez", "ez0")
-    fill(T.cb[:, C:C + 1], 256.0, "cb_end")
-    fill(T.wt[:, C:C + 1], 2.0 - 513 * 240 / UNIT, "wt_end")
-    fill(T.hs[:, 0:K], -HS, "hs0")
-    fill(T.hs[:, K:2 * K], HS, "hs1")
+    fill(T.zz[:], 0.0, "zz")
+    for ap, n, val, key in ((T.cb[:, C:C + 1], 1, 256.0, "cb_end"), (T.wt[:, C:C + 1], 1, 2.0 - 513 * 240 / UNIT, "wt_end"),
+                            (T.hs[:, 0:K], K, -HS, "hs0"), (T.hs[:, K:2 * K], K, HS, "hs1"), (T.ya[:, 0:28:2], 14, BIG * BIG, "ya")):
+        act(ap, T.zz[:, 0:n], Act.Identity, "zz", key, bias=val)
     ts(T.ez[:, 3:515:4], T.df[:], 0.0, None, Op.is_equal, None, "df", "ez")
     for b in range(4):
         quant(T.qe[:, 128 * b:128 * b + 128], T.se[:, 128 * b:128 * b + 128], T.ez[:, 3 - b:515 - b], "ez", "qe%d" % b)
     ts(T.pmi[:], T.pi[:], 15, None, Op.bitwise_and, None, "pi", "pmi")
+    ts(T.pq[:, 0:1], T.pi[:, 0:1], 1, 6, Op.arith_shift_right, Op.bitwise_and, "pi", "pq0")
+    ts(T.pq[:, 1:2], T.pi[:, 0:1], 3, None, Op.bitwise_and, None, "pi", "pq1")
+    cp("v", T.pf[:], T.pq[:], "pq0 pq1", "pf")
     tt(T.jw[:], T.c16[:], T.pmi[:], Op.add, "c16 pmi", "jw")
     cp("v", T.ul[:], T.c16[:, 0:8], "c16", "ul")
     cp("v", T.pm16[:], T.pmi[:], "pmi", "pm16")
-    ts(T.k1[:], T.rt[:, 15:31], T.jw[:, 0:1], BIG, Op.is_equal, Op.mult, "rt jw", "k1")
-    ts(T.k2[:], T.rt[:, 16:32], T.jw[:, 0:1], None, Op.not_equal, None, "rt jw", "k2")
-    tt(T.k16[:], T.k1[:], T.k2[:], Op.max, "k1 k2", "k16")
-    cp("s", T.kt[:], T.k16[:].indirect(T.pm16[:]), "k16 pm16", "kt")
-    ts(T.sc[:, 3:4], T.jw[:, 0:1], 15.0, BIG - 1.0, Op.not_equal, Op.mult, "jw", "sm")
-    act(sc, T.sc[:, 3:4], Act.Identity, "sm", "sc", bias=2.0, scale=-2.0 / BIG)
-    act(isc, T.sc[:, 3:4], Act.Identity, "sm", "isc", bias=0.5, scale=0.5)
-    act(s3, T.sc[:, 3:4], Act.Identity, "sm", "s3", bias=3.0, scale=3.0)
+    ts(T.k1[:, 0:16], T.gw[:, 63:79], T.jw[:, 0:1], BIG, Op.is_equal, Op.mult, "g_own jw", "k1")
+    ts(T.k2[:, 0:16], T.gw[:, 64:80], T.jw[:, 0:1], None, Op.not_equal, None, "g_own jw", "k2")
+    ts(T.k1[:, 16:32], T.r4[:, 0:16], T.pf[:, 0:1], BIG, Op.is_equal, Op.mult, "r4 pf", "k14")
+    ts(T.k2[:, 16:32], T.r4[:, 16:32], T.pf[:, 0:1], None, Op.not_equal, None, "r4 pf", "k24")
+    tt(T.kk[:], T.k1[:], T.k2[:], Op.max, "k1 k2 k14 k24", "kk")
+    cp("s", T.kt[:], T.kk[:, 0:16].indirect(T.pm16[:]), "kk pm16", "kt")
+    cp("s", T.kq[:], T.kk[:, 16:32].indirect(T.pm16[:]), "kk pm16", "kq")
+    ts(col(6), T.jw[:, 0:1], 15.0, BIG - 1.0, Op.not_equal, Op.mult, "jw", "sm")
+    ts(col(7), T.pf[:, 0:1], 6.0, BIG - 1.0, Op.not_equal, Op.mult, "pf", "sm4")
+    act(sc, col(6), Act.Identity, "sm", "sc", bias=8.0, scale=-8.0 / BIG)
+    act(isc, col(6), Act.Identity, "sm", "isc", bias=0.5, scale=0.5)
+    act(s3, col(6), Act.Identity, "sm", "s3", bias=-2.0, scale=-2.0)
+    act(sc1, col(6), Act.Identity, "sm", "sc1", bias=1.0, scale=-1.0 / BIG)
+    act(sc4, col(7), Act.Identity, "sm4", "sc4", bias=4.0, scale=-4.0 / BIG)
+    act(b4, T.pf[:, 1:2], Act.Identity, "pf", "b4", bias=4 * MID + 0.25)
     act(T.nk[:, 0:1], T.jw[:, 0:1], Act.Copy, "jw", "nk", scale=-2.0)
-    act(T.nk[:, 1:2], T.jw[:, 0:1], Act.Identity, "jw", "nk1", scale=2.0, bias=6.0)
-    act(T.j2[:], T.jw[:], Act.Identity, "jw", "j2", bias=742.0)
+    act(T.nk[:, 1:2], T.jw[:, 0:1], Act.Identity, "jw", "nk1", scale=2.0, bias=2.0 * E0)
+    act(T.j2[:], T.jw[:], Act.Identity, "jw", "j2", bias=(NEXT - 2 * C) / 4, scale=0.25)
     act(T.jm[:], T.j2[:], Act.Copy, "j2 isc", "jm", scale=isc)
-    quant(T.qh[:, K:K + 128], T.sh[:, K:K + 128], T.ht[:], hkeys, "qh_pad qh")
+    act(T.yb[:, 0:28:2], T.jm[:], Act.Identity, "jm s3", "jo", bias=s3)
     cp("v", T.nx16[:], T.nxi[:, 0:14], "nxi", "nx16")
-    act(T.gw[:, 0:C], T.rt[:, 16:240], Act.Identity, "rt", "g_own", bias=8.0, scale=0.5)
-    cp("s", T.gw[:, 640:864], T.gw[:, 0:C].indirect(T.nx16[:]), "g_own nx16", "g_next")
-    op("v", lambda: V.tensor_copy(T.gw[:, 320:544].indirect(T.nx16[:]), T.gw[:, 0:C]), "g_own nx16", "g_prev")
-    wrap(T.hp[:], T.gw[:, 320:544], "g_prev", "hp")
-    ts(T.pv16[:], T.hp[:, 15:C:16], sc, None, Op.mult, None, "hp sc", "pv16")
-    act(T.ramp[:], T.rt[:, 16:240], Act.Identity, "rt", "ramp", bias=2.0 - 512 * 16 / UNIT, scale=-512 / UNIT)
-    act(T.nt[:], T.rt[:, 32:256], Act.Copy, "rt", "nt", scale=-1.0 / UNIT)
+    cp("s", T.gw[:, NEXT:PREV], place.indirect(T.nx16[:]), "g_own nx16", "g_next")
+    for i, (c, d) in enumerate(zip(PCUT, PCUT[1:])):
+        op("v", lambda c=c, d=d: V.tensor_copy(T.gw[:, PREV:SLOT].indirect(T.nx16[:, c // 16:d // 16]), T.gw[:, c:d]),
+           "g_own nx16", "g_prev", None, "pr%d" % i)
+    wrap(T.hp[:], T.gw[:, PREV:SLOT], Op.add, "g_prev", "hp")
+    ts(T.pv16[:], T.hp[:, 15:C:16], sc1, MID + 0.25, Op.mult, Op.add, "hp sc1", "pv16")
+    act(T.ramp[:], place, Act.Identity, "g_own", "ramp", bias=2.0 - 512 * (16 + MID) / UNIT, scale=-512 / UNIT)
+    act(T.nt[:], place, Act.Identity, "g_own", "nt", bias=-(16 + MID) / UNIT, scale=-1.0 / UNIT)
     tt(T.wt[:, 0:C], T.nt[:].indirect(T.nx16[:]), T.ramp[:], Op.add, "nt nx16 ramp", "wt0")
     for r in (1, 2):
         act(T.wt[:, WL * r:WL * r + C + 1], T.wt[:, 0:C + 1], Act.Identity, "wt0 wt_end", "wt%d" % r, bias=32.0 * r)
@@ -224,8 +283,8 @@ def rank_program(g, core, T, topo):
 
     def halves(t):
         a, b = [(T.qx[:, 256 * t + c:256 * t + c + 128], T.sx[:, 256 * t + c:256 * t + c + 128]) for c in (0, 128)]
-        quant(a[0], a[1], T.xt[:, 0:512], "X0 X1 X2 X3", "qx%d" % t, "qx")
-        quant(b[0], b[1], T.xt[:, 512:1024], "Z0 Z1 Z2 Z3 xt_pad", "qz%d" % t, "qz")
+        quant(a[0], a[1], T.xt[:, 0:512], picked(0, 128), "qx%d" % t, "qx")
+        quant(b[0], b[1], T.xt[:, 512:1024], picked(128, C) + " xt_pad", "qz%d" % t, "qz")
         return a, b
 
     def signs(q, key, c, n, banks, names):
@@ -234,6 +293,7 @@ def rank_program(g, core, T, topo):
         ts(T.fb[:, c:c + n], banks[0][0][:, 0:n], 0.0, 1.0, Op.is_gt, Op.add, banks[0][1], names[2])
         act(T.sg[:, c:c + n], banks[1][0][:, 0:n], Act.Sign, banks[1][1], names[3])
 
+    qa, sa = T.qh[:, 128:256], T.sh[:, 128:256]
     for t in range(R):
         qx, sx, qk = T.qx[:, 256 * t:256 * t + C], T.sx[:, 256 * t:256 * t + C], "qx%d qz%d" % (t, t)
         qy, sy = T.qy[:, C * t:C * t + C], T.sy[:, C * t:C * t + C]
@@ -242,7 +302,7 @@ def rank_program(g, core, T, topo):
         ops.append((None, None, "", lst, (lst, ne_in)))
         if t == 1:
             quant(T.qv[:], T.sv[:], T.vt[:], "vt", "qv")
-        front, back = ((T.ps, "p:s"), (T.pp, "p:p")), ((T.pe, "p:e"), (T.pf, "p:f"))
+        front, back = ((T.ps, "p:s"), (T.pp, "p:p")), ((T.pe, "p:e"), (T.pg, "p:g"))
         if t:
             a, b = halves(t)
             signs(a, "qx%d" % t, 0, 128, front, ("mS", "mS2", "fb", "sg"))
@@ -255,16 +315,15 @@ def rank_program(g, core, T, topo):
         own = [(bank[:, 0:C], pk) for bank, pk in front + back]
         unpack(own, qx, sx, qk, "mD")
         for b, (bank, pk) in enumerate(own):
-            cp(TQ[b], T.tw[:, PL * b + 16:PL * b + 240], bank, pk, "T%d" % b)
-        for h, c, d in (("a", 0, 128), ("b", 128, C)):
-            nx = T.nx16[:, c // 16:d // 16]
-            tt(T.mb[:, c:d], T.fb[:].indirect(nx), T.sg[:, c:d], Op.is_le, "fb fb2 nx16 " + ("sg2" if c else "sg"), "mb" + h)
-            scan(T.cb[:, c:d], T.mb[:, c:d], T.mb[:, c:d], T.cb[:, c - 1:c] if c else T.nk[:, 0:1], Op.add, Op.add,
-                 "mb%s %s" % (h, "ca" if c else "nk"), "c" + h)
+            cp(TQ[b], T.tw[:, b:4 * C:4], bank, pk, "T%d" % b)
+        for h, c, d in (("a", 0, HALF), ("b", HALF, C)):
+            nx, cnt = T.nx16[:, c // 16:d // 16], T.cb if c else T.ca
+            tt(T.mb[:, c:d], T.fb[:].indirect(nx), T.sg[:, c:d], Op.is_le, "fb fb2 nx16 sg" + (" sg2" if c else ""), "mb" + h)
+            scan(cnt[:, 0:d], T.mb[:, 0:d], T.mb[:, 0:d], T.nk[:, 0:1], Op.add, Op.add, "mba mb%s nk" % h, "c" + h)
             for r in range(3):
                 w = WL * r
                 i, j = (c, d + 1) if c else (16 * r, d)
-                scan(T.cn[:, w + i:w + j], T.wt[:, w + i:w + j], T.cb[:, i:j], T.cn[:, w + c - 1:w + c] if c else -100.0,
+                scan(T.cn[:, w + i:w + j], T.wt[:, w + i:w + j], cnt[:, i:j], T.cn[:, w + c - 1:w + c] if c else -100.0,
                      Op.max, Op.min, "wt%d wt_end cb_end c%s %s" % (r, h, "n%da" % r if c else ""), "n%d%s" % (r, h))
         ts(T.lo[:, lo:lo + 2], T.cb[:, C - 2:C], T.nk[:, 1:2], None, Op.add, None, "cb nk1", "lc")
         for r in range(3):
@@ -274,64 +333,68 @@ def rank_program(g, core, T, topo):
             ts(T.lo[:, lo + 5 + r:lo + 6 + r], last, T.hi[:, r:r + 1], -UNIT, Op.subtract, Op.mult, "n%db hi%d" % (r, r), "ln%d" % r)
         send(T.li[:, lo:lo + 8], T.lo[:, lo:lo + 8], lst, "lc la0 la1 la2 ln0 ln1 ln2", "sendl")
 
+        q = T.yb[:, 1:28:2]
         cp("s", T.fn[:], T.fb[:].indirect(T.nx16[:]), "fb fb2 nx16", "fn")
         scan(T.hb[:], T.fn[:], T.fb[:], 0.0, Op.max, Op.subtract, "fn fb fb2", "hb")
-        scan(T.c2[:], T.hb[:], T.mb[:], 2.5, Op.add, Op.add, "hb mba mbb", "c2")
-        scan(T.eb[:, 16:240], T.c2[:], T.hb[:], 0.0, Op.max, Op.mult, "hb c2", "eb")
+        scan(T.c2[:], T.hb[:], T.mb[:], E0 - 0.5, Op.add, Op.add, "hb mba mbb", "c2")
+        scan(T.eb[:], T.c2[:], T.hb[:], 0.0, Op.max, Op.mult, "hb c2", "eb")
         act(T.zp[:], T.eb[:].indirect(T.pv16[:]), Act.Identity, "eb pv16", "zp", bias=-0.5)
-        wrap(T.wo[:, 0:C], T.fb[:], "fb fb2", "wf")
-        wrap(T.wo[:, C:2 * C], T.eb[:, 16:240], "eb", "we")
-        wrap(T.wo[:, 2 * C:3 * C], T.zp[:], "zp", "wq")
-        tt(T.m1[:], T.wo[:, 15:C:16], T.wo[:, C + 15:2 * C:16], Op.max, "wf we", "m1")
-        tt(T.q[:], T.m1[:], T.wo[:, 2 * C + 15:3 * C:16], Op.max, "m1 wq", "q")
-        ts(T.t1[:], T.q[:], s3, -160.0, Op.min, Op.mult, "q s3", "t1")
+        wrap(T.wo[:, 0:C], T.fb[:], Op.max, "fb fb2", "wf")
+        wrap(T.wo[:, C:2 * C], T.eb[:], Op.max, "eb", "we")
+        wrap(T.wo[:, 2 * C:3 * C], T.zp[:], Op.max, "zp", "wq")
+        ts(T.t1[:], T.wo[:, 15:C:16], C / 8, None, Op.mult, None, "wf", "t1")
         tt(T.y1[:], T.t1[:], T.jm[:], Op.add, "t1 jm", "y1")
-        ts(T.thr[:], T.li[:, lo + 1:lo + 2], 6.0 + 2 * K, isc, Op.min, Op.mult, lst + " isc", "thr")
-        ts(T.pn[:], T.q[:], T.thr[:], -1000.0 * BIG, Op.is_ge, Op.mult, "q thr", "pn")
-        tt(T.x1[:], T.q[:], T.pn[:], Op.add, "q pn", "x1")
-        tt(T.l1[:], T.y1[:], T.x1[:], Op.max, "y1 x1", "l1")
-        ts(T.l16[:], T.l1[:], sc, 218.0, Op.mult, Op.add, "l1 sc", "l16")
-        cp("s", T.h0[:], T.gw[:].indirect(T.l16[:]), "l16 g_own g_slot g_next g_prev", "h0")
+        tt(T.m1[:], T.y1[:], T.wo[:, C + 15:2 * C:16], Op.max, "y1 we", "m1")
+        tt(q, T.m1[:], T.wo[:, 2 * C + 15:3 * C:16], Op.max, "m1 wq", "q")
+        ts(T.thr[:], T.li[:, lo + 1:lo + 2], 2.0 * (E0 + K), isc, Op.min, Op.mult, lst + " isc", "thr")
+        ts(T.ya[:, 1:28:2], q, T.thr[:], BIG * BIG, Op.is_lt, Op.mult, "q thr", "pn")
+        scan(T.yo[:], T.ya[:], T.yb[:], 0.0, Op.add, Op.min, "ya pn q jo", "yo")
+        ts(T.l16[:], T.yo[:, 1:28:2], sc, C + 0.25, Op.mult, Op.add, "yo sc", "l16")
+        cp("s", T.hd[:, 0:2 * C:2], T.gw[:].indirect(T.l16[:]), "l16 g_own g_slot g_next g_prev", "h0")
 
         unpack([(T.pd[:, 512 * b:512 * b + C], "p:d%d" % b) for b in range(4)], qy, sy, arr, "mN")
         for b in range(4):
-            p, plane = 512 * b, T.tw[:, PL * b:PL * b + PL]
+            p = 512 * b
             cp(NQ[b], T.tp[:, 256 * b + 16:256 * b + 240], T.pd[:, p:p + C], "p:d%d" % b, "N%d" % b)
             cp(AQ[b], T.at[:, b:384:4], T.tp[:, 256 * b:256 * b + 256].indirect(T.li[:, lo + 2:lo + 8]),
                "%s N%d tp_zero" % (lst, b), "A%d" % b)
-            mm(T.pd[:, p:p + 128], T.qw[:, 128 * b:128 * b + 128], T.sw[:, 128 * b:128 * b + 128], T.qa[:], T.sa[:],
+            mm(T.pd[:, p:p + 128], T.qw[:, 128 * b:128 * b + 128], T.sw[:, 128 * b:128 * b + 128], qa, sa,
                "qw%d sw qa" % b, "p:d%d" % b, "mW%d" % b)
             if HQ[b] == "v":
                 tt(T.ht[:, b:8 * K:4], T.pd[:, p:p + 2 * K], T.hs[:], Op.mult, "p:d%d hs0 hs1" % b, "H%d G%d" % (b, b))
             else:
                 act(T.ht[:, b:4 * K:4], T.pd[:, p:p + K], Act.Copy, "p:d%d" % b, "H%d" % b, scale=-HS)
                 act(T.ht[:, 4 * K + b:8 * K:4], T.pd[:, p + K:p + 2 * K], Act.Copy, "p:d%d" % b, "G%d" % b, scale=HS)
-            act(T.tw[:, PL * b + 256:PL * b + PL:2], T.pd[:, p:p + 2 * K], Act.Copy, "p:d%d" % b, "TH%d" % b, scale=HS)
-            cp("vsvs"[b], T.xt[:, b:512:4], plane.indirect(T.lx[:, 0:8]), "lx0 T%d TH%d" % (b, b), "X%d" % b)
-            cp("vsvs"[b], T.xt[:, 512 + b:4 * C:4], plane.indirect(T.lx[:, 8:14]), "lx1 lx2 T%d TH%d" % (b, b), "Z%d" % b)
-        quant(T.qa[:], T.sa[:], T.at[:], "at_pad A0 A1 A2 A3", "qa")
-        quant(T.qh[:, 0:128], T.sh[:, 0:128], T.ht[:], hkeys, "qh")
-        op("t", scores, "qur sur qh qh_pad", "p:p", None, "mP")
-        ts(T.fw[:, C + 1:320:2], T.pp[:, 0:K], 0.0, float(K), Op.is_gt, Op.mult, "p:p fw", "up")
-        ts(T.fw[:, C:320:2], T.pp[:, 0:K], 0.0, -float(K), Op.is_gt, Op.mult, "p:p fw", "down")
-        for i, (c, d) in enumerate(CUTS):
-            hv, hw = T.hv[:, 16 * c:16 * d], T.hw[:, 16 * c:16 * d]
-            tt(hv, T.fw[:].indirect(T.l16[:, c:d]), T.h0[:, 16 * c:16 * d], Op.add, "up down fw l16 h0", "hv%d" % i)
-            scan(hw, T.kt[:, 0:16 * (d - c)], hv, 0.0, Op.mult, Op.max, "hv%d kt" % i, "hw%d" % i)
-            ts(T.lx[:, c:d], T.hw[:, 16 * c + 15:16 * d:16], sc, None, Op.mult, None, "hw%d sc" % i, "lx%d" % i)
+            for s, name in enumerate(("TH", "TI")):
+                act(T.tw[:, 4 * C + 4 * s + b:4 * C + 8 * K:8], T.pd[:, p + K * s:p + K * s + K], Act.Copy, "p:d%d" % b,
+                    name + str(b), scale=HS)
+        quant(qa, sa, T.at[:], "at_pad A0 A1 A2 A3", "qa")
+        quant(T.qh[:, 0:128], T.sh[:, 0:128], T.ht[:], "ht_pad H0 H1 H2 H3 G0 G1 G2 G3", "qh")
+        op("t", scores, "qur sur qh qa", "p:p", None, "mP")
+        ts(T.fw[:, SLOT + 4:GW:8], T.pp[:, 0:K], 0.0, 1.0, Op.is_gt, Op.mult, "p:p", "up")
+        ts(T.fw[:, SLOT:GW:8], T.pp[:, 0:K], 0.0, -1.0, Op.is_gt, Op.mult, "p:p", "down")
+        for i, (c, d) in enumerate(zip(CUTS, CUTS[1:])):
+            cp(DQ[i], T.hd[:, 2 * c + 1:2 * d:2], T.fw[:].indirect(T.l16[:, c // 16:d // 16]), "up down fw l16", "hv%d" % i)
+            scan(T.hw[:, 2 * c:2 * d], T.kq[:, 0:2 * (d - c)], T.hd[:, 2 * c:2 * d], 0.0, Op.mult, Op.add,
+                 "hv%d h0 kq" % i, "hw%d" % i)
+            ts(T.lx[:, c // 4:d // 4], T.hw[:, 2 * c + 7:2 * d:8], sc4, b4, Op.mult, Op.add, "hw%d sc4 b4" % i, "lx%d" % i)
+        for i, (e, c, d) in enumerate(PICKS):
+            cp(e, T.xt[:, 4 * c:4 * d], T.tw[:].indirect(T.lx[:, c // 4:d // 4]),
+               pieces("lx", c, d) + " T0 T1 T2 T3 TH0 TH1 TH2 TH3 TI0 TI1 TI2 TI3", "X%d" % i)
         issue((LATER if t else FIRST).split())
 
     lo = 256 * R
-    cp("s", T.ots[:], T.rt[:].indirect(T.lx[:]), "rt rt2 lx0 lx1 lx2", "ots")
+    tt(T.ramp[:], T.hd[:, 0:2 * C:2], T.hd[:, 1:2 * C:2], Op.add, pieces("hv", 0, C) + " h0", "ramp")
+    act(T.ots[:], T.ramp[:], Act.Identity, "ramp", "ots", bias=MID)
     a, b = halves(R)
     mm(T.ps[:, 0:128], T.qv[:], T.sv[:], a[0], a[1], "qv qx3", "p:s", "mY")
-    mm(T.pp[:, 0:128], T.qv[:], T.sv[:], b[0], b[1], "qv qz3", "p:p", "mY2")
+    mm(T.pe[:, 0:128], T.qv[:], T.sv[:], b[0], b[1], "qv qz3", "p:e", "mY2")
     cp("v", T.ys[:, 0:128], T.ps[:, 0:128], "p:s", "ys")
-    cp("v", T.ys[:, 128:C], T.pp[:, 0:C - 128], "p:p", "ys2")
+    cp("v", T.ys[:, 128:C], T.pe[:, 0:C - 128], "p:e", "ys2")
     dma("y", T.oc[:], T.qx[:, lo:lo + C].bitcast(dt.uint8), "qx3 qz3", "", "doc")
     dma("s", T.ot[:], T.ots[0:128:16, :], "ots", "", "dot")
     for k in range(4):
-        dma("ys"[k % 2], T.osc[4 * k:4 * k + 4, :], T.sx[32 * k:32 * k + 4, lo:lo + C], "qx3 qz3", "", "ds%d" % k)
+        dma("s", T.osc[4 * k:4 * k + 4, :], T.sx[32 * k:32 * k + 4, lo:lo + C], "qx3 qz3", "", "ds%d" % k)
     dma("y", T.y[:], T.ys[:], "ys ys2", "", "dy")
     issue(LAST.split())
     _emit(g, T, ops, 3 * R * ne_out)

from concourse.mybir import dt, AluOpType as Op, ActivationFunctionType as Act

C, K, R = 224, 48, 3
MID = 64.0
BIG = 65536.0
HS = 0.03125
UNIT = 65536.0
ROUND = 1.5 * 2.0 ** 23 * 512 / UNIT
WL = 232
NEXT, PREV, SLOT, GW = 240, 464, 688, 688 + 8 * K
E0 = (SLOT - C) // 8
_B = {
    "bfloat16": dict(x0=896, ut=512, vt=512, ez=528, df=128, xt=1024, tw=4 * (C + 2 * K), tp=1024, at=512, ht=512, fb=C, sg=C,
                     mb=C, ca=128, cb=240, fn=C, hb=C, c2=C, eb=C, zp=C, wo=3 * C, gw=GW, fw=GW, hd=2 * C, hw=2 * C, hp=C,
                     kt=C, kq=C, kk=32, r4=32, hs=2 * K, zz=K),
    "float32": dict(m1=14, thr=1, t1=14, y1=14, ya=28, yb=28, yo=28, cn=3 * WL, wt=3 * WL, ramp=C, nt=C, hi=3,
                    k1=32, k2=32, jw=14, jm=14, j2=14, nk=2, sc=8, pf=2, ys=C, ots=C),
    "int32": dict(nxi=16, pi=14, c16=14, pmi=14, pq=2),
    "uint16": dict(lo=8 * R, li=8 * R, l16=14, lx=56, ul=8, pm16=14, nx16=14, pv16=14),
    "float8_e4m3fn_x4": dict(qu=128, qur=128, qv=128, qw=512, qe=512, qx=256 * (R + 1), qy=R * C, qh=256),
    "uint8": dict(su=128, sur=128, sv=128, sw=512, se=512, sx=256 * (R + 1), sy=R * C, sh=256),
}
SCRATCH = {k: ("sbuf", [128, n], d) for d, b in _B.items() for k, n in b.items()}
SCRATCH.update({k: ("psum", [128, 2048 if k == "pd" else 512], "float32") for k in ("ps", "pp", "pe", "pg", "pd")})
WK = ("", "qur")
DMAS = ["dx", "du", "dn", "dwa", "dwb", "dws", "dv", "dz", "ds0", "ds1", "ds2", "ds3", "doc", "dot", "dy"]
SEMAPHORES = ["cv", "cs", "ct", "cg", "sent"] + ["%s%d" % (k, t) for k in ("arr", "lst") for t in range(R)] + DMAS

CUTS = (0, 64, 128, 224)
HALF = 128
PCUT = (0, 224)
HQ = "vvvv"
DQ = "vsv"
PICKS = (("s", 0, 64), ("v", 64, 128), ("v", 128, 176), ("s", 176, 224))
TQ, NQ, AQ = "ssss", "svsv", "svsv"
FIRST = """dn dx du pi c16 g_own r4 df g_slot ez0 pmi pq0 pq1 jw pf wt_end nt pm16 ul ramp sm sm4 k2 k1 k24 k14 nk1 nk kk nx16 g_prev
    qx j2 hs0 hs1 wt0 qu ez cb_end sur qur mS2 wt1 isc mS dwa dws sendq sends tp_zero at_pad ht_pad fb sg kt qe2
    mba mbb wt2 ca sc qe0 cb n1a n2a n0a n1b n2b lc mD2 n0b hi2 s3 hi1 la1 hi0 fn la2 mD0 ln1 ln2 la0 mN2 ln0
    hb hp dwb c2 mN0 qe1 sc1 pv16 eb qe3 mN1 we sendl fw xt_pad wf g_next N1 mN3 N2 zp m1 N3 wq ya kq sc4 b4
    A1 thr A3 q N0 A2 A0 t1 pn qa mW0 dv T0 jm mW2 y1 yo H0 mW1 mW3 mD1 H2 H1 mD3 l16 H3 T1 qh h0 T2 mP
    up TH0 TI0 TH2 TI2 down hv0 TH1 TI1 hv1 T3 hv2 TH3 TI3 hw0 hw1 hw2 lx0 lx1 lx2 X0 X1 X2 X3"""
LATER = """qx mS2 mS qz sendq sends mZ mZ2 sg sg2 fb fb2 fn mD2 mD0 mD3 mD1 T1 T0 T2 T3
    mba mbb ca hb cb n0a n1a n2a n0b n1b n2b c2 hi0 hi1 la0 hi2 la1 la2 ln0 ln1 lc ln2 sendl
    eb wf zp qv we mN1 mN0 mN3 mN2 N1 N0 N3 N2 m1 wq A1 thr A3 A0 A2 q qa t1 pn y1
    mW0 mW2 mW1 mW3 yo H0 H2 H1 l16 H3 qh mP h0 TH0 TI0 TH2 TI2 TH1 TI1 TH3 TI3
    up down hv0 hv1 hv2 hw0 hw1 hw2 lx0 lx1 lx2 X0 X1 X2 X3"""
LAST = "qx ots qz mY mY2 ys ys2 doc dzc dot ds0 ds1 ds2 ds3 dy dz"
FIRST = """wt_end ez0 hs1 pi pmi dn pq0 pq1 hs0 nx16 dx c16 ul jw g_own pm16 df du g_prev qx nt r4 qu pf k2 sendq k1 ez qur ramp sends
    wt0 k14 nk sur tp_zero mS2 sm qe1 mS dws k24 ht_pad cb_end fb kk sg mD1 wt1 qe0 nk1 sm4 kt mba wt2 mbb qe2 sc1 mN0 mN1 ca cb
    at_pad mN2 hp n1a dwa n2a n0a fn pv16 isc lc sc n1b T1 g_next n2b sc4 n0b hb hi1 la1 fw j2 hi2 hi0 la0 s3 c2 ln1 la2 b4 ln0
    jm ln2 sendl qe3 mN3 eb wf N1 we N3 dwb N0 mD3 xt_pad m1 zp N2 mD0 wq A1 A3 g_slot A0 A2 ya thr q qa mD2 T0 t1 mW0 pn mW2 y1
    mW1 T2 mW3 H0 kq H2 TI0 H1 H3 yo qh l16 h0 TH0 mP TI2 up TH3 down TH1 TI1 hv0 T3 TH2 hv1 dv hv2 TI3 hw0 hw1 lx0 hw2 X0 lx1
    lx2 X1 X2 X3"""
LAST = """qx doc qz mY ots ds0 mY2 ys dzc ds3 ds1 dot ys2 ds2 dy dz"""
LATER = """qx mS qz mS2 sends mZ mZ2 fb sendq sg fb2 mD2 mD1 sg2 fn mba mN0 mbb mN2 wf N0 ca hb cb n0a mN3 n1a n2a lc n0b n1b n2b mN1 c2
    hi0 la0 hi1 hi2 la2 la1 ln0 ln1 ln2 eb sendl mD0 N1 we zp N2 A0 N3 A2 m1 wq T1 A3 T2 A1 qv q mD3 qa mW0 mW2 t1 thr T3 y1 T0
    pn H0 H2 mW1 TH2 H1 mW3 H3 yo TI1 qh TI3 l16 TH1 mP down h0 TI0 up TH3 hv0 TH0 hv1 hv2 hw0 hw1 hw2 lx0 lx1 TI2 lx2 X1 X0 X3
    X2"""
FIRST = """zz dx df ez0 ez pi pq0 du c16 hs0 pmi pq1 qe2 wt_end qe3 jw nk1 g_own pf ul r4 nk qx k2 ramp mD3 k1 k24 k14 qu nt pm16 dn sur
    kk kt qur sends nx16 sm qe0 cb_end sendq mS2 sg wt0 hs1 wt2 mS at_pad wt1 mN2 fb qe1 sm4 mba mbb ca wf dws cb n1a s3 n0a fn
    n2a n1b T3 sc1 b4 n0b tp_zero ht_pad dwa n2b fw isc hb mN1 mN0 hi1 lc hi0 la0 hi2 j2 la2 ln1 la1 mN3 sc4 ln0 ln2 ya g_next sc
    c2 g_prev sendl kq eb N1 hp N2 jm mD0 mD1 N0 mD2 N3 A2 A0 pv16 A1 t1 zp T1 dwb A3 y1 we qa mW0 jo m1 g_slot wq xt_pad thr mW1
    q T2 H0 T0 mW2 TI0 mW3 H1 H2 H3 pn qh yo TH2 TH3 l16 TH0 TI3 mP down up dv h0 hv1 TH1 hv0 hv2 hw0 hw1 hw2 TI2 TI1 lx0 lx1 lx2
    X1 X0 X3 X2"""
LAST = """qx qz ds2 ramp mY ys ds3 mY2 doc ds0 ds1 ots dot ys2 dy"""
LATER = """qx mS2 qz mS fb mZ sends mZ2 sg fb2 qv sg2 mba mbb fn wf ca mD2 mD0 hb cb n0a n1a n2a n0b n1b n2b lc la0 hi0 hi1 sendq hi2
    mN2 la1 la2 ln0 ln1 ln2 mN1 c2 mN0 mD1 eb t1 N2 mN3 N0 sendl we y1 zp N1 N3 mD3 A1 A2 A3 m1 thr A0 T2 wq qa mW3 mW2 T0 q pn
    H3 H2 mW1 H1 mW0 H0 T1 T3 TI1 yo TH0 qh mP TI3 l16 TI0 down up TH2 h0 TH1 hv0 hv2 hw0 hv1 TI2 hw1 TH3 hw2 lx0 lx1 lx2 X0 X3
    X1 X2"""
FIRST = """ez0 pi zz pmi pq1 pq0 hs1 c16 df jw pm16 pf ez g_own nk1 ramp sm ul cb_end sm4 dx qe3 r4 qx k2 k1 du qe2 b4 nk qu sendq mD3 dn qe0 k14 ya wt_end nx16 qur sur mS2 k24 pr0 qe1 sends kk mS nt wt0 fb j2 sg pr1 isc mba mbb mD1 kq wt1 mN2 ca sc at_pad wt2 sc4 sc1 jm pr2 mN1 fn n0a kt cb n1a hs0 n2a n0b s3 g_next g_slot n1b T3 n2b lc la0 tp_zero hi0 mN0 hi2 la2 la1 ln0 ln1 mN3 ln2 N2 hb pr3 fw c2 wf hp N1 eb dws dwa mD2 dwb sendl N3 pv16 ht_pad N0 A1 A3 A2 mD0 A0 zp we t1 qa y1 mW0 wq m1 T0 jo thr T1 H0 mW1 H1 q xt_pad mW2 mW3 H2 H3 pn TI1 T2 TH2 TH0 qh TI0 yo mP l16 TH3 dv up down h0 hv0 hv1 TI2 TH1 hv2 hw0 hw1 TI3 hw2 lx0 X0 lx1 lx2 X1 X3 X2"""
LAST = """qx ramp qz doc mY ots mY2 ys ys2 dy dot ds0 ds1 ds2 ds3"""
LATER = """qx qz mS2 sg sendq mS mZ mZ2 sg2 fb fb2 mba mbb ca wf sends cb n0a mD3 n1a mD1 T3 mD0 mD2 n2a fn n0b n1b mN2 T0 mN0 T2 n2b lc T1 la0 hi0 hi2 la2 la1 ln1 ln0 ln2 hb sendl c2 N2 t1 mN1 mN3 eb N3 N1 qv A3 A1 we N0 thr zp A2 y1 A0 qa m1 mW3 wq mW2 mW1 q mW0 H3 H2 H1 H0 pn TI1 qh TI0 TI2 mP yo l16 up TH0 down TH2 h0 hv0 hv2 hw0 hv1 hw1 TI3 hw2 lx0 lx1 TH1 TH3 lx2 X0 X1 X3 X2"""
FIRST = """zz dx df ez0 ez pi pq0 du c16 hs0 pmi pq1 qe2 wt_end qe3 jw nk1 g_own pf ul r4 nk qx k2 ramp mD3 k1 k24 k14 qu nt pm16 dn dwa dws sur
    kk kt qur dwb sends nx16 sm qe0 cb_end sendq mS2 sg wt0 hs1 wt2 mS at_pad wt1 mN2 fb qe1 sm4 mba mbb ca wf cb n1a s3 n0a fn
    n2a n1b T3 sc1 b4 n0b tp_zero ht_pad n2b fw isc hb mN1 mN0 hi1 lc hi0 la0 hi2 j2 la2 ln1 la1 mN3 sc4 ln0 ln2 ya g_next sc
    c2 pr0 sendl kq eb N1 hp N2 jm mD0 mD1 N0 mD2 N3 A2 A0 pv16 A1 t1 zp T1 A3 y1 we qa mW0 jo m1 g_slot wq xt_pad thr mW1
    q T2 H0 T0 mW2 TI0 mW3 H1 H2 H3 pn qh yo TH2 TH3 l16 TH0 TI3 mP down up dv h0 hv1 TH1 hv0 hv2 hw0 hw1 hw2 TI2 TI1 lx0 lx1 lx2
    X1 X0 X3 X2"""
LAST = "qx qz doc ds0 ds1 ds2 ds3 ramp mY ys mY2 ys2 dy ots dot"
LATER = """qx qz mS2 qv mS sg mZ fb mZ2 fb2 mba sg2 mbb ca sendq wf sends cb n0a n1a n2a mD1 n0b mN2 mN0 fn n1b mN1 n2b lc hi0 la0 mN3 hi1 hi2 la2 ln0 mD2 la1 ln1 ln2 N2 hb t1 sendl c2 eb mD3 N0 zp N1 N3 A2 we y1 A1 A3 A0 T3 wq mD0 T1 thr m1 qa q mW3 mW2 pn H3 mW1 H2 T0 mW0 T2 TH3 H1 TI1 H0 TH0 yo qh TI0 mP l16 h0 up TH2 down hv0 hv2 hw0 hv1 TI2 TH1 TI3 hw1 hw2 lx0 X0 lx1 lx2 X3 X1 X2"""


def _emit(g, T, ops, sent):
    eng = {"v": g.vector, "s": g.scalar, "t": g.tensor, "g": g, "y": g.sync}
    own = {"v": "cv", "s": "cs", "t": "ct", "g": "cg"}
    count, waited = {}, {}
    known = {q: {} for q in eng}
    writer, readers, mark = {}, {}, []
    for i, (q, fn, reads, writes, kind) in enumerate(ops):
        reads, writes = reads.split(), writes.split()
        deps = set()
        for k in reads:
            if k in writer:
                deps.add(writer[k])
            if k.startswith("p:"):
                deps.update(j for j in readers.get(k, []) if ops[j][0] != q)
        for k in writes:
            if k in writer:
                deps.add(writer[k])
            deps.update(readers.get(k, []))
        for k in reads:
            readers.setdefault(k, []).append(i)
        for k in writes:
            writer[k] = i
            readers[k] = []
        if q is None:
            mark.append((kind[0], kind[1], {}))
            count[kind[0]] = kind[1]
            continue
        for j in sorted(deps, reverse=True):
            sem, n, seen = mark[j]
            if sem is None or known[q].get(sem, 0) >= n:
                continue
            eng[q].wait_ge(T.sem[sem], n)
            known[q][sem] = n
            waited[sem] = max(waited.get(sem, 0), n)
            for s, m in seen.items():
                known[q][s] = max(known[q].get(s, 0), m)
        ins = fn()
        if kind == "remote":
            mark.append((None, 0, {}))
            continue
        sem, step = (own[q], 1) if kind is None else (kind, 16)
        count[sem] = count.get(sem, 0) + step
        ins.then_inc(T.sem[sem], step)
        mark.append((sem, count[sem], dict(known[q])))
    count["sent"] = sent
    for sem in SEMAPHORES:
        if count.get(sem, 0) > waited.get(sem, 0):
            g.wait_ge(T.sem[sem], count[sem])


def rank_program(g, core, T, topo):
    rank = T.rank_of(core)
    if rank is None:
        return
    nxt = T.cores[(rank + 1) % len(T.cores)]
    prv = T.cores[rank - 1]
    rid, pid = topo.addr(nxt, core)
    mask = topo.mask(core, nxt)
    ne_out, ne_in = len(topo.engines(core, nxt)), len(topo.engines(prv, core))
    V, S, PE = g.vector, g.scalar, g.tensor
    ops, steps = [], {}

    def op(q, fn, r, w, kind=None, name=None):
        steps[name or w.split()[0]] = (q, fn, r, w, kind)

    def issue(order):
        names = [n for n in order if n in steps]
        assert len(names) == len(steps), sorted(set(steps) - set(names))
        ops.extend(steps.pop(n) for n in names)

    def ts(out, in0, a, b, o0, o1, r, w):
        if o1 is None:
            op("v", lambda: V.tensor_scalar(out, in0, a, None, o0), r, w)
        else:
            op("v", lambda: V.tensor_scalar(out, in0, a, b, o0, o1), r, w)

    def tt(out, in0, in1, o, r, w):
        op("v", lambda: V.tensor_tensor(out, in0, in1, o), r, w)

    def act(out, in_, func, r, w, **k):
        op("s", lambda: S.activation(out, in_, func, **k), r, w)

    def cp(q, out, in_, r, w):
        if q == "v":
            op("v", lambda: V.tensor_copy(out, in_), r, w)
        else:
            act(out, in_, Act.Copy, r, w)

    def scan(out, d0, d1, init, o0, o1, r, w):
        op("v", lambda: V.tensor_tensor_scan(out, d0, d1, init, o0, o1), r, w)

    def wrap(out, in_, o, r, w):
        scan(out, T.kt[:], in_, 0.0, Op.mult, o, r + " kt", w)

    def quant(q, s, in_, r, w, name=None):
        op("v", lambda: V.quantize_mx(q, s, in_), r, w, None, name)

    def mm(out, a, sa, b, sb, r, w, name):
        op("t", lambda: PE.matmul_mx(out, a, sa, b, sb, True, True), r, w, None, name)

    def fill(ap, val, w, name=None):
        op("v", lambda: V.memset(ap, val), "", w, None, name)

    def iota(out, pattern, base, mult, w, small=True):
        if small:
            op("g", lambda: g.iota(out, pattern, base, mult, allow_small_or_imprecise_dtypes=True), "", w)
        else:
            op("g", lambda: g.iota(out, pattern, base, mult), "", w)

    def dma(q, out, in_, r, w, sem):
        e = g.sync if q == "y" else S
        op(q, lambda: e.dma_start(out, in_), r, w, sem, sem)

    def send(out, in_, sem, r, name):
        op("g", lambda: g.remote_dma(out, in_, T.sem[sem], T.sem.sent, pid, rid, mask), r, "", "remote", name)

    def unpack(banks, q, s, key, name):
        for b, (bank, pk) in enumerate(banks):
            mm(bank, T.qe[:, 128 * b:128 * b + 128], T.se[:, 128 * b:128 * b + 128], q, s, "qe%d %s" % (b, key), pk, name + str(b))

    def scores():
        PE.matmul_mx(T.pp[:, 0:128], T.qur[:], T.sur[:], T.qh[:, 0:128], T.sh[:, 0:128], True, False)
        return PE.matmul_mx(T.pp[:, 0:128], T.qur[:], T.sur[:], T.qh[:, K:K + 128], T.sh[:, K:K + 128], False, True)

    def pieces(key, c, d):
        return " ".join(key + str(i) for i in range(len(CUTS) - 1) if CUTS[i] < d and c < CUTS[i + 1])

    def picked(c, d):
        return " ".join("X%d" % i for i, p in enumerate(PICKS) if p[1] < d and c < p[2])

    dma("y", T.nxi[:, 0:14], T.nx[:], "", "nxi", "dn")
    dma("y", T.ut[:], T.u[:], "", "ut", "du")
    dma("y", T.x0[:], T.x[:], "", "x0", "dx")
    dma("y", T.qw[:, 0:256].bitcast(dt.uint8), T.wc[:, 0:1024], WK[0], "qw0 qw1", "dwa")
    dma("y", T.sw[:], T.ws[:], WK[0], "sw", "dws")
    dma("y", T.qw[:, 256:512].bitcast(dt.uint8), T.wc[:, 1024:2048], WK[1], "qw2 qw3", "dwb")
    dma("y", T.vt[:], T.v[:], "qa", "vt", "dv")

    col = lambda i: T.sc[:, i:i + 1]
    sc, isc, s3, sc1, sc4, b4 = [col(i) for i in range(6)]
    place = T.gw[:, 0:C]
    iota(T.df[:], [[1, 128]], 0, -1, "df")
    iota(T.pi[:], [[0, 14]], 0, 1, "pi", False)
    iota(T.c16[:], [[16, 14]], 0, 0, "c16", False)
    iota(place, [[1, C]], -int(MID), 0, "g_own")
    iota(T.r4[:], [[2, 2], [0, 2], [1, 8]], -2, 0, "r4")
    iota(T.gw[:, SLOT:GW:4], [[2, K], [-1, 2]], C + 1 - int(MID), 0, "g_slot")
    for ap, n, key in ((T.tp[:, 240:1024:256], 4, "tp_zero"), (T.at[:, 384:512], 128, "at_pad"),
                       (T.xt[:, 896:1024], 128, "xt_pad"), (T.ht[:, 384:512], 128, "ht_pad"), (T.fw[:, 0:SLOT], SLOT, "fw")):
        iota(ap, [[0, n]], 0, 0, key)
    fill(T.ez[:], 0.0, "ez", "ez0")
    fill(T.zz[:], 0.0, "zz")
    for ap, n, val, key in ((T.cb[:, C:C + 1], 1, 256.0, "cb_end"), (T.wt[:, C:C + 1], 1, 2.0 - 513 * 240 / UNIT, "wt_end"),
                            (T.hs[:, 0:K], K, -HS, "hs0"), (T.hs[:, K:2 * K], K, HS, "hs1"), (T.ya[:, 0:28:2], 14, BIG * BIG, "ya")):
        act(ap, T.zz[:, 0:n], Act.Identity, "zz", key, bias=val)
    ts(T.ez[:, 3:515:4], T.df[:], 0.0, None, Op.is_equal, None, "df", "ez")
    for b in range(4):
        quant(T.qe[:, 128 * b:128 * b + 128], T.se[:, 128 * b:128 * b + 128], T.ez[:, 3 - b:515 - b], "ez", "qe%d" % b)
    ts(T.pmi[:], T.pi[:], 15, None, Op.bitwise_and, None, "pi", "pmi")
    ts(T.pq[:, 0:1], T.pi[:, 0:1], 1, 6, Op.arith_shift_right, Op.bitwise_and, "pi", "pq0")
    ts(T.pq[:, 1:2], T.pi[:, 0:1], 3, None, Op.bitwise_and, None, "pi", "pq1")
    cp("v", T.pf[:], T.pq[:], "pq0 pq1", "pf")
    tt(T.jw[:], T.c16[:], T.pmi[:], Op.add, "c16 pmi", "jw")
    cp("v", T.ul[:], T.c16[:, 0:8], "c16", "ul")
    cp("v", T.pm16[:], T.pmi[:], "pmi", "pm16")
    ts(T.k1[:, 0:16], T.gw[:, 63:79], T.jw[:, 0:1], BIG, Op.is_equal, Op.mult, "g_own jw", "k1")
    ts(T.k2[:, 0:16], T.gw[:, 64:80], T.jw[:, 0:1], None, Op.not_equal, None, "g_own jw", "k2")
    ts(T.k1[:, 16:32], T.r4[:, 0:16], T.pf[:, 0:1], BIG, Op.is_equal, Op.mult, "r4 pf", "k14")
    ts(T.k2[:, 16:32], T.r4[:, 16:32], T.pf[:, 0:1], None, Op.not_equal, None, "r4 pf", "k24")
    tt(T.kk[:], T.k1[:], T.k2[:], Op.max, "k1 k2 k14 k24", "kk")
    cp("s", T.kt[:], T.kk[:, 0:16].indirect(T.pm16[:]), "kk pm16", "kt")
    cp("s", T.kq[:], T.kk[:, 16:32].indirect(T.pm16[:]), "kk pm16", "kq")
    ts(col(6), T.jw[:, 0:1], 15.0, BIG - 1.0, Op.not_equal, Op.mult, "jw", "sm")
    ts(col(7), T.pf[:, 0:1], 6.0, BIG - 1.0, Op.not_equal, Op.mult, "pf", "sm4")
    act(sc, col(6), Act.Identity, "sm", "sc", bias=8.0, scale=-8.0 / BIG)
    act(isc, col(6), Act.Identity, "sm", "isc", bias=0.5, scale=0.5)
    act(s3, col(6), Act.Identity, "sm", "s3", bias=-2.0, scale=-2.0)
    act(sc1, col(6), Act.Identity, "sm", "sc1", bias=1.0, scale=-1.0 / BIG)
    act(sc4, col(7), Act.Identity, "sm4", "sc4", bias=4.0, scale=-4.0 / BIG)
    act(b4, T.pf[:, 1:2], Act.Identity, "pf", "b4", bias=4 * MID + 0.25)
    act(T.nk[:, 0:1], T.jw[:, 0:1], Act.Copy, "jw", "nk", scale=-2.0)
    act(T.nk[:, 1:2], T.jw[:, 0:1], Act.Identity, "jw", "nk1", scale=2.0, bias=2.0 * E0)
    act(T.j2[:], T.jw[:], Act.Identity, "jw", "j2", bias=(NEXT - 2 * C) / 4, scale=0.25)
    act(T.jm[:], T.j2[:], Act.Copy, "j2 isc", "jm", scale=isc)
    act(T.yb[:, 0:28:2], T.jm[:], Act.Identity, "jm s3", "jo", bias=s3)
    cp("v", T.nx16[:], T.nxi[:, 0:14], "nxi", "nx16")
    cp("s", T.gw[:, NEXT:PREV], place.indirect(T.nx16[:]), "g_own nx16", "g_next")
    for i, (c, d) in enumerate(zip(PCUT, PCUT[1:])):
        op("v", lambda c=c, d=d: V.tensor_copy(T.gw[:, PREV:SLOT].indirect(T.nx16[:, c // 16:d // 16]), T.gw[:, c:d]),
           "g_own nx16", "g_prev", None, "pr%d" % i)
    wrap(T.hp[:], T.gw[:, PREV:SLOT], Op.add, "g_prev", "hp")
    ts(T.pv16[:], T.hp[:, 15:C:16], sc1, MID + 0.25, Op.mult, Op.add, "hp sc1", "pv16")
    act(T.ramp[:], place, Act.Identity, "g_own", "ramp", bias=2.0 - 512 * (16 + MID) / UNIT, scale=-512 / UNIT)
    act(T.nt[:], place, Act.Identity, "g_own", "nt", bias=-(16 + MID) / UNIT, scale=-1.0 / UNIT)
    tt(T.wt[:, 0:C], T.nt[:].indirect(T.nx16[:]), T.ramp[:], Op.add, "nt nx16 ramp", "wt0")
    for r in (1, 2):
        act(T.wt[:, WL * r:WL * r + C + 1], T.wt[:, 0:C + 1], Act.Identity, "wt0 wt_end", "wt%d" % r, bias=32.0 * r)
    quant(T.qu[:], T.su[:], T.ut[:], "ut", "qu")
    cp("v", T.qur[:].bitcast(dt.uint32), T.qu[:].bitcast(dt.uint32).indirect(T.ul[:]), "qu ul", "qur")
    cp("s", T.sur[:], T.su[:].indirect(T.ul[:]), "qu ul", "sur")

    def halves(t):
        a, b = [(T.qx[:, 256 * t + c:256 * t + c + 128], T.sx[:, 256 * t + c:256 * t + c + 128]) for c in (0, 128)]
        quant(a[0], a[1], T.xt[:, 0:512], picked(0, 128), "qx%d" % t, "qx")
        quant(b[0], b[1], T.xt[:, 512:1024], picked(128, C) + " xt_pad", "qz%d" % t, "qz")
        return a, b

    def signs(q, key, c, n, banks, names):
        for (bank, pk), name in zip(banks, names[:2]):
            mm(bank[:, 0:max(n, 128)], T.qur[:], T.sur[:], q[0], q[1], "qur sur " + key, pk, name)
        ts(T.fb[:, c:c + n], banks[0][0][:, 0:n], 0.0, 1.0, Op.is_gt, Op.add, banks[0][1], names[2])
        act(T.sg[:, c:c + n], banks[1][0][:, 0:n], Act.Sign, banks[1][1], names[3])

    qa, sa = T.qh[:, 128:256], T.sh[:, 128:256]
    for t in range(R):
        qx, sx, qk = T.qx[:, 256 * t:256 * t + C], T.sx[:, 256 * t:256 * t + C], "qx%d qz%d" % (t, t)
        qy, sy = T.qy[:, C * t:C * t + C], T.sy[:, C * t:C * t + C]
        lo, arr, lst = 8 * t, "arr%d" % t, "lst%d" % t
        ops.append((None, None, "", arr, (arr, 2 * ne_in)))
        ops.append((None, None, "", lst, (lst, ne_in)))
        if t == 1:
            quant(T.qv[:], T.sv[:], T.vt[:], "vt", "qv")
        front, back = ((T.ps, "p:s"), (T.pp, "p:p")), ((T.pe, "p:e"), (T.pg, "p:g"))
        if t:
            a, b = halves(t)
            signs(a, "qx%d" % t, 0, 128, front, ("mS", "mS2", "fb", "sg"))
            signs(b, "qz%d" % t, 128, C - 128, back, ("mZ", "mZ2", "fb2", "sg2"))
        else:
            quant(qx, sx, T.x0[:], "x0", qk, "qx")
            signs((qx, sx), qk, 0, C, front, ("mS", "mS2", "fb fb2", "sg sg2"))
        send(qy.bitcast(dt.uint8), qx.bitcast(dt.uint8), arr, qk, "sendq")
        send(sy, sx, arr, qk, "sends")
        own = [(bank[:, 0:C], pk) for bank, pk in front + back]
        unpack(own, qx, sx, qk, "mD")
        for b, (bank, pk) in enumerate(own):
            cp(TQ[b], T.tw[:, b:4 * C:4], bank, pk, "T%d" % b)
        for h, c, d in (("a", 0, HALF), ("b", HALF, C)):
            nx, cnt = T.nx16[:, c // 16:d // 16], T.cb if c else T.ca
            tt(T.mb[:, c:d], T.fb[:].indirect(nx), T.sg[:, c:d], Op.is_le, "fb fb2 nx16 sg" + (" sg2" if c else ""), "mb" + h)
            scan(cnt[:, 0:d], T.mb[:, 0:d], T.mb[:, 0:d], T.nk[:, 0:1], Op.add, Op.add, "mba mb%s nk" % h, "c" + h)
            for r in range(3):
                w = WL * r
                i, j = (c, d + 1) if c else (16 * r, d)
                scan(T.cn[:, w + i:w + j], T.wt[:, w + i:w + j], cnt[:, i:j], T.cn[:, w + c - 1:w + c] if c else -100.0,
                     Op.max, Op.min, "wt%d wt_end cb_end c%s %s" % (r, h, "n%da" % r if c else ""), "n%d%s" % (r, h))
        ts(T.lo[:, lo:lo + 2], T.cb[:, C - 2:C], T.nk[:, 1:2], None, Op.add, None, "cb nk1", "lc")
        for r in range(3):
            last = T.cn[:, WL * r + C:WL * r + C + 1]
            ts(T.hi[:, r:r + 1], last, ROUND, ROUND, Op.add, Op.subtract, "n%db" % r, "hi%d" % r)
            ts(T.lo[:, lo + 2 + r:lo + 3 + r], last, 32.0 * r + 2.0, -UNIT / 512, Op.subtract, Op.mult, "n%db" % r, "la%d" % r)
            ts(T.lo[:, lo + 5 + r:lo + 6 + r], last, T.hi[:, r:r + 1], -UNIT, Op.subtract, Op.mult, "n%db hi%d" % (r, r), "ln%d" % r)
        send(T.li[:, lo:lo + 8], T.lo[:, lo:lo + 8], lst, "lc la0 la1 la2 ln0 ln1 ln2", "sendl")

        q = T.yb[:, 1:28:2]
        cp("s", T.fn[:], T.fb[:].indirect(T.nx16[:]), "fb fb2 nx16", "fn")
        scan(T.hb[:], T.fn[:], T.fb[:], 0.0, Op.max, Op.subtract, "fn fb fb2", "hb")
        scan(T.c2[:], T.hb[:], T.mb[:], E0 - 0.5, Op.add, Op.add, "hb mba mbb", "c2")
        scan(T.eb[:], T.c2[:], T.hb[:], 0.0, Op.max, Op.mult, "hb c2", "eb")
        act(T.zp[:], T.eb[:].indirect(T.pv16[:]), Act.Identity, "eb pv16", "zp", bias=-0.5)
        wrap(T.wo[:, 0:C], T.fb[:], Op.max, "fb fb2", "wf")
        wrap(T.wo[:, C:2 * C], T.eb[:], Op.max, "eb", "we")
        wrap(T.wo[:, 2 * C:3 * C], T.zp[:], Op.max, "zp", "wq")
        ts(T.t1[:], T.wo[:, 15:C:16], C / 8, None, Op.mult, None, "wf", "t1")
        tt(T.y1[:], T.t1[:], T.jm[:], Op.add, "t1 jm", "y1")
        tt(T.m1[:], T.y1[:], T.wo[:, C + 15:2 * C:16], Op.max, "y1 we", "m1")
        tt(q, T.m1[:], T.wo[:, 2 * C + 15:3 * C:16], Op.max, "m1 wq", "q")
        ts(T.thr[:], T.li[:, lo + 1:lo + 2], 2.0 * (E0 + K), isc, Op.min, Op.mult, lst + " isc", "thr")
        ts(T.ya[:, 1:28:2], q, T.thr[:], BIG * BIG, Op.is_lt, Op.mult, "q thr", "pn")
        scan(T.yo[:], T.ya[:], T.yb[:], 0.0, Op.add, Op.min, "ya pn q jo", "yo")
        ts(T.l16[:], T.yo[:, 1:28:2], sc, C + 0.25, Op.mult, Op.add, "yo sc", "l16")
        cp("s", T.hd[:, 0:2 * C:2], T.gw[:].indirect(T.l16[:]), "l16 g_own g_slot g_next g_prev", "h0")

        unpack([(T.pd[:, 512 * b:512 * b + C], "p:d%d" % b) for b in range(4)], qy, sy, arr, "mN")
        for b in range(4):
            p = 512 * b
            cp(NQ[b], T.tp[:, 256 * b + 16:256 * b + 240], T.pd[:, p:p + C], "p:d%d" % b, "N%d" % b)
            cp(AQ[b], T.at[:, b:384:4], T.tp[:, 256 * b:256 * b + 256].indirect(T.li[:, lo + 2:lo + 8]),
               "%s N%d tp_zero" % (lst, b), "A%d" % b)
            mm(T.pd[:, p:p + 128], T.qw[:, 128 * b:128 * b + 128], T.sw[:, 128 * b:128 * b + 128], qa, sa,
               "qw%d sw qa" % b, "p:d%d" % b, "mW%d" % b)
            if HQ[b] == "v":
                tt(T.ht[:, b:8 * K:4], T.pd[:, p:p + 2 * K], T.hs[:], Op.mult, "p:d%d hs0 hs1" % b, "H%d G%d" % (b, b))
            else:
                act(T.ht[:, b:4 * K:4], T.pd[:, p:p + K], Act.Copy, "p:d%d" % b, "H%d" % b, scale=-HS)
                act(T.ht[:, 4 * K + b:8 * K:4], T.pd[:, p + K:p + 2 * K], Act.Copy, "p:d%d" % b, "G%d" % b, scale=HS)
            for s, name in enumerate(("TH", "TI")):
                act(T.tw[:, 4 * C + 4 * s + b:4 * C + 8 * K:8], T.pd[:, p + K * s:p + K * s + K], Act.Copy, "p:d%d" % b,
                    name + str(b), scale=HS)
        quant(qa, sa, T.at[:], "at_pad A0 A1 A2 A3", "qa")
        quant(T.qh[:, 0:128], T.sh[:, 0:128], T.ht[:], "ht_pad H0 H1 H2 H3 G0 G1 G2 G3", "qh")
        op("t", scores, "qur sur qh qa", "p:p", None, "mP")
        ts(T.fw[:, SLOT + 4:GW:8], T.pp[:, 0:K], 0.0, 1.0, Op.is_gt, Op.mult, "p:p", "up")
        ts(T.fw[:, SLOT:GW:8], T.pp[:, 0:K], 0.0, -1.0, Op.is_gt, Op.mult, "p:p", "down")
        for i, (c, d) in enumerate(zip(CUTS, CUTS[1:])):
            cp(DQ[i], T.hd[:, 2 * c + 1:2 * d:2], T.fw[:].indirect(T.l16[:, c // 16:d // 16]), "up down fw l16", "hv%d" % i)
            scan(T.hw[:, 2 * c:2 * d], T.kq[:, 0:2 * (d - c)], T.hd[:, 2 * c:2 * d], 0.0, Op.mult, Op.add,
                 "hv%d h0 kq" % i, "hw%d" % i)
            ts(T.lx[:, c // 4:d // 4], T.hw[:, 2 * c + 7:2 * d:8], sc4, b4, Op.mult, Op.add, "hw%d sc4 b4" % i, "lx%d" % i)
        for i, (e, c, d) in enumerate(PICKS):
            cp(e, T.xt[:, 4 * c:4 * d], T.tw[:].indirect(T.lx[:, c // 4:d // 4]),
               pieces("lx", c, d) + " T0 T1 T2 T3 TH0 TH1 TH2 TH3 TI0 TI1 TI2 TI3", "X%d" % i)
        issue((LATER if t else FIRST).split())

    lo = 256 * R
    tt(T.ramp[:], T.hd[:, 0:2 * C:2], T.hd[:, 1:2 * C:2], Op.add, pieces("hv", 0, C) + " h0", "ramp")
    act(T.ots[:], T.ramp[:], Act.Identity, "ramp", "ots", bias=MID)
    a, b = halves(R)
    mm(T.ps[:, 0:128], T.qv[:], T.sv[:], a[0], a[1], "qv qx3", "p:s", "mY")
    mm(T.pe[:, 0:128], T.qv[:], T.sv[:], b[0], b[1], "qv qz3", "p:e", "mY2")
    cp("v", T.ys[:, 0:128], T.ps[:, 0:128], "p:s", "ys")
    cp("v", T.ys[:, 128:C], T.pe[:, 0:C - 128], "p:e", "ys2")
    dma("y", T.oc[:], T.qx[:, lo:lo + C].bitcast(dt.uint8), "qx3 qz3", "", "doc")
    dma("s", T.ot[:], T.ots[0:128:16, :], "ots", "", "dot")
    for k in range(4):
        dma("s", T.osc[4 * k:4 * k + 4, :], T.sx[32 * k:32 * k + 4, lo:lo + C], "qx3 qz3", "", "ds%d" % k)
    dma("y", T.y[:], T.ys[:], "ys ys2", "", "dy")
    issue(LAST.split())
    _emit(g, T, ops, 3 * R * ne_out)
